import numpy as np, ml_dtypes
CORES = [78,86,94,102,110,118]
N = 6
BF = ml_dtypes.bfloat16
def gentries(a):
    return np.ascontiguousarray(a.reshape(8, 16, -1).transpose(0, 2, 1)).reshape(8, -1)
def gtable(e):
    e = np.asarray(e); return np.ascontiguousarray(e.reshape(8, -1, 16).transpose(0, 2, 1)).reshape(128, -1).astype(np.int32)
V, A, K, DB, DP, EP = 3072, 128, 2, 5, 32, 2
RI, GI, G8 = np.arange(N)[:, None, None], np.arange(8)[None, :, None], np.arange(8)[:, None]
def pick(a, i):
    return a[RI, GI, i]
def tall(x):
    return np.ascontiguousarray(x.astype(np.float32).reshape(N, 8, 16, V).transpose(0, 1, 3, 2)).astype(np.int32)
def depths(par):
    j = np.reshape(par, (-1, V)).astype(np.int64); t = np.zeros(j.shape, np.int64) + np.arange(V); n = np.zeros(j.shape, np.int64)
    for _ in range(DP):
        n += t >= A; t = np.take_along_axis(j, t, 1)
    return n.reshape(np.shape(par))
def forest(rng, m, power):
    n = V - A; lev = np.minimum(1 + np.floor(m * rng.random(n) ** power).astype(np.int64), m); lev[rng.permutation(n)[:m]] = np.arange(1, m + 1)
    p = np.arange(V); o = A + np.argsort(lev, kind="stable"); cnt = np.bincount(lev, minlength=m + 1); before = np.arange(A); a = 0
    for l in range(1, m + 1):
        now = o[a:a + cnt[l]]; p[now] = before[rng.integers(0, before.size, now.size)]; before = now; a += cnt[l]
    return p
def parts(rng, deep, power):
    hf = 1 - 2 * rng.integers(0, 2, (N, 128, V)); bt = rng.integers(0, 256, (N, 128, V)); dr = rng.integers(0, 256, (N, 128, V))
    par = np.stack([np.stack([forest(rng, int(deep[r, g]), float(power[r, g])) for g in range(8)]) for r in range(N)])
    return hf, bt, dr, par, rng.integers(0, V, (N, 8, K, V)), rng.integers(0, V, (N, 8, A))
def pack(hf, bt, dr, par, nb, up):
    return {"hf": hf.astype(np.float32).astype(BF), "bt": bt.astype(np.float32).astype(BF), "dr": dr.astype(np.float32).astype(BF), "par": par.astype(np.int32),
            "nb": np.stack([gtable(a.reshape(8, -1)) for a in nb]), "up": np.stack([gtable(a) for a in up])}
def setup_inputs(rng):
    deep = rng.choice(np.array([DP - 1, DP // 2 + 1, DP // 2, DP // 4]), (N, 8)); deep[:, rng.integers(0, 8)] = DP - 1; deep[0, 0] = DP - 1
    return pack(*parts(rng, deep, rng.choice(np.array([0.5, 1.0, 1.5]), (N, 8))))
def setup_inputs_deep(rng):
    hf, bt, dr, par, nb, up = parts(rng, np.full((N, 8), DP - 1), rng.choice(np.array([0.1, 0.25]), (N, 8)))
    o = np.argsort(-depths(par), axis=-1, kind="stable")[:, :, :A]
    for r in range(1, N): up[r] = rng.permuted(o[r - 1], axis=-1)
    hf[:, 16:32] = 1; hf[0, 16:24, :A] = -1; bt[:, 16:32] = 255; dr[:, 16:32] = 0; nb[:, 1] = np.arange(V)
    return pack(hf, bt, dr, par, nb, up)
def setup_inputs_ties(rng):
    hf, bt, dr, par, nb, up = parts(rng, rng.choice(np.array([DP - 1, DP // 2, 5]), (N, 8)), np.full((N, 8), 1.0))
    bt = (bt >> 6) * 64; dr = (dr >> 6) * 64; h4, b4, d4 = hf.reshape(N, 8, 16, V), bt.reshape(N, 8, 16, V), dr.reshape(N, 8, 16, V)
    h4[:, ::2] = h4[:, ::2, :1]; b4[:, ::2] = (b4[:, ::2, :1] >> 7) * 128; d4[:, ::2] = (d4[:, ::2, :1] >> 7) * 128
    nb[:, :, 1:] = np.where(rng.random((N, 8, K - 1, V)) < 0.2, nb[:, :, :1], nb[:, :, 1:]); nb = np.where(rng.random(nb.shape) < 0.1, np.arange(V), nb)
    return pack(hf, bt, dr, par, nb, up)
def setup_inputs_flat(rng):
    deep = np.full((N, 8), DP // 2); deep[:, 0] = 1; deep[:, 1] = 2; deep[:, 2] = DP - 1
    hf, bt, dr, par, nb, up = parts(rng, deep, np.full((N, 8), 1.0)); dep = depths(par); v = np.arange(V); hf[:, 64:80] = 1
    for r in range(N):
        par[r, 1] = np.where(dep[r, 1] == 2, np.flatnonzero(dep[r, 1] == 1)[0], par[r, 1])
        ch = np.arange(V); ch[par[r, 7, A:]] = np.arange(A, V); nb[r, 7, 0] = ch
        c = np.where(v < A, v, 2 * rng.integers(0, A // 2, V) + dep[r, 4] % 2); c = np.where((v >= A) & (c == par[r, 4]), (c + 2) % A, c)
        w = bt[r, 64:80, :A][:, c]; bt[r, 64:80, A:] = (w - w[:, par[r, 4]])[:, A:] & 255; nb[r, 4, r % K] = c
    nb[:, 2] = np.arange(V); hf[:, 48:64] = -1; bt[:, 48:64] = 255; dr[:, 48:64] = 255; up[:, 4] = V - 1; up[:, 5] = rng.integers(0, A, (N, A))
    up[:, 6] = rng.choice(np.array([0, V - 1]), (N, A)); nb[:, 6] = rng.choice(np.array([0, A - 1, A, V - 1]), (N, K, V))
    return pack(hf, bt, dr, par, nb, up)
def setup_inputs_spread(rng):
    hf, bt, dr, par, nb, up = parts(rng, rng.integers(1, DP, (N, 8)), rng.choice(np.array([0.2, 1.0, 4.0]), (N, 8)))
    share = rng.choice(np.array([0.02, 0.3, 0.5, 0.98]), (N, 8, 1, 1)); hf = np.where(rng.random((N, 8, 16, V)) < share, -1, 1).reshape(N, 128, V)
    k = lambda: rng.integers(0, 9, (N, 1, V)); bt = (bt >> k()) * (rng.random((N, 1, V)) > 0.0625); dr = (dr >> k()) * (rng.random((N, 1, V)) > 0.0625)
    nb = np.minimum((V * rng.random(nb.shape) ** 3).astype(np.int64), V - 1); up = np.minimum((V * rng.random(up.shape) ** 3).astype(np.int64), V - 1)
    return pack(hf, bt, dr, par, nb, up)
def check_inputs(d):
    bad = []
    if not np.all(np.abs(d["hf"].astype(np.float32)) == 1): bad.append("hf is 1 or -1")
    for k in ("bt", "dr"):
        x = d[k].astype(np.float32)
        if not np.all((x >= 0) & (x <= 255) & (x == np.floor(x))): bad.append("range of " + k)
    for k in ("par", "nb", "up"):
        if np.min(d[k]) < 0 or np.max(d[k]) > V - 1: bad.append("range of " + k)
    if "range of par" not in bad:
        if np.any(d["par"][:, :, :A] != np.arange(A)): bad.append("an anchor is its own parent")
        if np.max(depths(d["par"])) >= DP: bad.append("depth")
    return bad
def reference(hf, bt, dr, par, nb, up):
    h, b, d = tall(hf), tall(bt), tall(dr); g = np.where(d >= 128, -1, 1).astype(np.int32); move = np.arange(V) >= A
    p = par.astype(np.int64); nl = np.stack([gentries(a) for a in nb]).astype(np.int64).reshape(N, 8, K, V); ul = np.stack([gentries(a) for a in up]).astype(np.int64)
    for e in range(EP):
        Hm = h.copy(); Zm = b.copy(); Hm[:, :, :A] = 1; Zm[:, :, :A] = 0
        j = p; dep = np.broadcast_to(move, p.shape).astype(np.int64)
        for _ in range(DB):
            hp = pick(Hm, j); Zm = hp * Zm + pick(Zm, j); Hm = hp * Hm; dep = dep + pick(dep, j); j = pick(j, j)
        H = np.empty_like(Hm); Z = np.empty_like(Zm)
        for r in range(N):
            ah, az = h[r, :, :A], b[r, :, :A]
            if r > 0:
                uh = H[r - 1][G8, ul[r]]; az = uh * az + Z[r - 1][G8, ul[r]]; ah = uh * ah
            ch = ah[G8, j[r]]; H[r] = ch * Hm[r]; Z[r] = (ch * Zm[r] + az[G8, j[r]]) & 255
        best = np.add.reduce(np.abs(Z - pick(Z, p)), axis=3); new = p
        for k in range(K):
            c = pick(p, nl[:, :, k]); s = np.add.reduce(np.abs(Z - pick(Z, c)), axis=3)
            ok = (pick(dep, c) < dep) & (s < best)
            new = np.where(ok, c, new); best = np.where(ok, s, best)
        p = new
        if e < EP - 1:
            hp = pick(H, p); zb = (hp * (Z - pick(Z, p)) + d) & 255; m = move[:, None]
            h = np.where(m, g * hp * H, h); b = np.where(m, zb, b)
    return {"yx": np.ascontiguousarray(Z.transpose(0, 1, 3, 2)).reshape(N, 128, V).astype(np.float32).astype(BF), "yp": p.astype(np.float32)}

@@ -1,0 +1,595 @@
+from concourse.bass import DstId, RemoteDMATransfer
+from concourse.mybir import AluOpType as ALU, ActivationFunctionType as AF
+
+V, A, NR, EP = 3072, 128, 6, 2
+NW = V // 16
+KK = 8192.0
+MID = 49152.0
+PEN = 2.0 ** 45
+
+BF, F32, I32, U16 = "bfloat16", "float32", "int32", "uint16"
+SCRATCH = {}
+for _d, _w, _names in (
+        (BF, V, "h0 b0 d0 gs va vb pw j2 j4 j8 j16 j32 n0 n1 da db dc xp yy hs xw vd xd"), (F32, V, "za zb zd"),
+        (U16, NW, "l1 l2 l4 l8 l16 l32 lc0 lc1"), (F32, NW, "pv e0 e1 w1 mm cc blk"), (BF, NW, "hi lo pen0 pen1 q0 q1 dv"),
+        (I32, NW, "pari"), (I32, 2 * NW, "nbi"), (U16, 2 * NW, "ln"), (F32, 2 * NW, "t1 t2"), (U16, 24, "f1 f3"), (U16, 12, "f2 f4"),
+        (I32, 16, "ci s2"), (F32, 16, "cf s3"), (F32, 80, "iw"), (F32, 48, "s1"), (BF, 144, "msel mdep msum mneg"),
+        (BF, 128, "idp idn idk idb c64 hu qq xa"), (F32, 128, "idf kh zanc"), (F32, 1024, "zg"), (BF, 512, "ones"),
+        (I32, 8, "upi upn"), (BF, 256, "an ann sj sk"), (U16, 32, "lh"), (F32, 256, "z0 z1 z2 ee"), (I32, 128, "zi zj yi yj"),
+        (BF, EP * 256, "msg"), (U16, EP * 16, "ptr"), (BF, EP * 5 * 256, "lmsg"), (U16, EP * 5 * 16, "lptr"),
+        (F32, 5 * 256, "uu"), (F32, 5 * 128, "zz")):
+    for _n in _names.split():
+        SCRATCH[_n] = ("sbuf", [128, _w], _d)
+SCRATCH.update({"pb": ("psum", [128, V], F32), "ex0": ("psum", [128, 512], F32), "ex1": ("psum", [128, 512], F32)})
+NDMA = 120
+SEMAPHORES = (["qv", "qa", "qt", "qg", "sent", "aup", "aan"] + ["dma%d" % i for i in range(NDMA)]
+              + ["am%d_%d" % (e, r) for e in range(EP) for r in range(5)] + ["ap%d_%d" % (e, r) for e in range(EP) for r in range(5)])
+
+C3 = [(0, 1024), (1024, 2048), (2048, 3072)]
+C3N = [(A, 1024), (1024, 2048), (2048, 3072)]
+C6 = [(512 * i, 512 * i + 512) for i in range(6)]
+C6N = [(A, 512)] + C6[1:]
+OPT = {
+    "share": [(2304, 2560), (2560, 3072)],
+    "zch": [(A, 704), (704, 1280), (1280, 1792), (1792, 2304)],
+    "x_act": (0, 1, 2),
+    "c_act": (0, 1),
+    "hdup": "aaaggg", "vdup": "ssgssg", "zdup": "ggsgs", "xdup": "ssssss",
+    "cyc": 1.04e-3, "gc": 1.56, "pe": 0.55e-3, "bw": 2.0e5, "hop": 0.1, "fix": 0.07, "dl": 2.0,
+    "arrive": 11.0, "urgent": 14.0, "slack": 0.25, "small": 0.35,
+}
+
+
+def R(name, c0=None, c1=None, step=1, rows=None, lane=None):
+    if c0 is None:
+        c0, c1 = 0, SCRATCH[name][1][1]
+    return {"n": name, "c0": c0, "c1": c1, "st": step, "rows": rows, "lane": lane}
+
+
+def G(win, off):
+    return {"win": win, "off": off}
+
+
+def ap(T, r):
+    if "win" in r:
+        return ap(T, r["win"]).indirect(ap(T, r["off"]))
+    rows = slice(None) if r["rows"] is None else r["rows"]
+    if r["st"] == 1:
+        return T[r["n"]][rows, r["c0"]:r["c1"]]
+    return T[r["n"]][rows, r["c0"]:r["c1"]:r["st"]]
+
+
+def regs(rs):
+    out = []
+    for r in rs:
+        if isinstance(r, dict):
+            out += [r["win"], r["off"]] if "win" in r else [r]
+    return out
+
+
+def width(r):
+    return len(range(r["c0"], r["c1"], r["st"]))
+
+
+def two(*rs):
+    return all(SCRATCH[r["n"]][2] in (BF, U16) for r in rs)
+
+
+def psum(r):
+    return SCRATCH[r["n"]][0] == "psum"
+
+
+def build(rank, T, topo):
+    ops = []
+    state = {"dma": 0, "ex": 0, "pb": 0}
+    CYC, GC, PEC, BW = OPT["cyc"], OPT["gc"], OPT["pe"], OPT["bw"]
+    ID, ABS, SIGN = AF.Identity, AF.Abs, AF.Sign
+    ADD, SUB, MUL = ALU.add, ALU.subtract, ALU.mult
+
+    def val(x):
+        return ap(T, x) if isinstance(x, dict) else x
+
+    def add(eng, fn, rd, wr, dur, **kw):
+        o = {"eng": eng, "fn": fn, "rd": regs(rd), "wr": regs(wr), "dur": dur, "lat": 0.0, "kind": "c", "after": [], "bonus": 0.0, "id": len(ops)}
+        o.update(kw)
+        ops.append(o)
+        return o
+
+    def vdur(n, c):
+        return OPT["fix"] + max(n * c, 64) * CYC
+
+    def tt(out, a, b, op):
+        c = GC if "win" in a else (1 if psum(a) or psum(b) else 2)
+        return add("v", lambda e: e.tensor_tensor(ap(T, out), ap(T, a), ap(T, b), op), [a, b], [out], vdur(width(out), c))
+
+    def ts(out, a, s1, op0, s2=None, op1=None):
+        c = 0.5 if two(out, a) else 1
+        if op1 is None:
+            fn = lambda e: e.tensor_scalar(ap(T, out), ap(T, a), val(s1), None, op0)
+        else:
+            fn = lambda e: e.tensor_scalar(ap(T, out), ap(T, a), val(s1), val(s2), op0, op1)
+        return add("v", fn, [a, s1, s2], [out], vdur(width(out), c))
+
+    def cp(out, a):
+        c = GC if "win" in a else (0.5 if two(out, a) else 1)
+        return add("v", lambda e: e.tensor_copy(ap(T, out), ap(T, a)), [a], [out], vdur(width(out), c))
+
+    def tr(out, a):
+        return add("v", lambda e: e.transpose(ap(T, out), ap(T, a)), [a], [out], vdur(width(out), 1))
+
+    def act(out, a, func, bias=0.0, scale=1.0):
+        c = GC if "win" in a else 1
+        return add("a", lambda e: e.activation(ap(T, out), ap(T, a), func, bias=bias, scale=scale), [a], [out], 0.02 + vdur(width(out), c))
+
+    def mm(out, terms, start=True, stop=True):
+        def fn(e):
+            for k, (l, r) in enumerate(terms):
+                ins = e.matmul(ap(T, out), ap(T, l), ap(T, r), start and k == 0, stop and k == len(terms) - 1)
+            return ins
+        return add("t", fn, [x for t in terms for x in t], [out], 0.05 + sum(1 if two(l) else 4 for l, r in terms) * max(64, width(out)) * PEC)
+
+    def diag(mat, src, m0, m1):
+        return [(R(mat, 15 - i, 143 - i), R(src, 16 * m0 + i, 16 * m1, 16)) for i in range(16)]
+
+    def exb():
+        state["ex"] ^= 1
+        return "ex%d" % state["ex"]
+
+    def spare(m0, m1):
+        state["pb"] = (state["pb"] + 1) % 4
+        return R("pb", 512 * state["pb"] + m0, 512 * state["pb"] + m1)
+
+    def iota(out, pattern, base, mult):
+        if SCRATCH[out["n"]][2] != I32:
+            fn = lambda e: e.iota(ap(T, out), pattern, base, mult, allow_small_or_imprecise_dtypes=True)
+        else:
+            fn = lambda e: e.iota(ap(T, out), pattern, base, mult)
+        return add("g", fn, [], [out], 0.15 + 2 * width(out) * CYC)
+
+    def whole(out, x):
+        return iota(out, [[0, width(out)]], x, 0)
+
+    def pick(out, a, step, op, other, mult):
+        n = width(out)
+        return add("g", lambda e: e.affine_select(ap(T, out), ap(T, a), [[step, n]], op, other, 0, mult), [a], [out], 0.2 + 2 * n * CYC)
+
+    def mark_anchors(name, x):
+        return pick(R(name, 0, A), R("ones", 0, A), 0, ALU.not_equal, x, 0)
+
+    def dma(q, out, in_, nbytes, after=(), bonus=0.0):
+        rd = [in_] if isinstance(in_, dict) else []
+        wr = [out] if isinstance(out, dict) else []
+        k = state["dma"]
+        state["dma"] += 1
+        return add(q, lambda e: e.dma_start(val(out), val(in_)), rd, wr, 0.1, kind="d", lat=OPT["dl"] + nbytes / BW, xfer=nbytes / BW, bonus=bonus,
+                   sem="dma%d" % k, after=list(after))
+
+    def dup(how, out, a):
+        if how == "s":
+            return dma("s", out, a, 128 * width(a) * (2 if two(a) else 4))
+        if how == "a":
+            return act(out, a, ID)
+        if how == "v":
+            return cp(out, a)
+        return pick(out, a, 0, ALU.is_ge, 0.0, 0)
+
+    me = T.cores[rank]
+
+    def send(tos, out, in_, sem, tail):
+        dsts = [T.cores[to] for to in tos]
+        mask = topo.mask(me, dsts[0])
+        ids = [DstId(rid=topo.addr(d)[0], pnc=topo.addr(d)[1]) for d in dsts]
+        fn = lambda e: e.remote_dma_fused([RemoteDMATransfer(dst_ids=ids, dma_engine_mask=mask, remote_sem=T.sem[sem], srcs=[ap(T, in_)],
+                                                             dsts=[ap(T, out) for d in dsts])], local_sem=T.sem["sent"])
+        return add("g", fn, [in_], [], 0.3, kind="s", tail=tail, n=len(topo.engines(me, dsts[0])))
+
+    def arrive(frm, buf, sem, after, lat):
+        return add("x", None, [], [buf], 0.0, kind="r", lat=lat, sem=sem, n=len(topo.engines(T.cores[frm], me)), after=list(after))
+
+    sends, gets = rank < NR - 1, rank > 0
+    later = range(NR - 1, rank, -1)
+
+    dma("s", R("pari"), T.par[:], 98304, bonus=300.0)
+    dma("a", R("h0", A, 1536), T.hf[:, A:1536], 380000, bonus=80.0)
+    dma("s", R("h0", 1536, V), T.hf[:, 1536:V], 380000, bonus=80.0)
+    dma("s", R("an", 0, A), T.hf[:, 0:A], 32768)
+    dma("s", R("an", A, 2 * A), T.bt[:, 0:A], 32768)
+    if gets:
+        dma("s", R("upi"), T.up[:], 4096)
+
+    iota(R("ci", 0, 1), [[0, 1]], 0, 1)
+    iota(R("iw", 0, 24), [[16, 12], [0, 2]], 0, 0)
+    iota(R("iw", 24, 36), [[16, 12]], 0, 0)
+    iota(R("iw", 36, 44), [[1, 8]], 0, 0)
+    iota(R("iw", 44, 68), [[1, 12], [0, 2]], 0, 0)
+    iota(R("iw", 68, 80), [[32, 12]], 0, 0)
+    add("v", lambda e: e.memset(ap(T, R("pw")), 0.0), [], [R("pw")], vdur(V, 0.5))
+    for k, x in ((1, 15), (2, 16), (3, 31)):
+        ts(R("ci", k, k + 1), R("ci", 0, 1), x, ALU.bitwise_and)
+    ts(R("ci", 4, 5), R("ci", 0, 1), 4, ALU.arith_shift_right)
+    cp(R("cf", 1, 5), R("ci", 1, 5))
+    age, odd, m32, grp = R("cf", 1, 2), R("cf", 2, 3), R("cf", 3, 4), R("cf", 4, 5)
+    ts(R("f1"), R("iw", 0, 24), age, ADD)
+    ts(R("s1", 0, 12), R("iw", 24, 36), age, ADD)
+    ts(R("s3", 0, 12), R("s1", 0, 12), -5.5, ADD, 1.0 / 12.0, MUL)
+    cp(R("s2", 0, 12), R("s3", 0, 12))
+    ts(R("s1", 12, 24), R("s2", 0, 12), -383.0, MUL, odd, ADD)
+    ts(R("s1", 24, 36), R("s1", 0, 12), 32.0, MUL)
+    tt(R("s1", 36, 48), R("s1", 12, 24), R("s1", 24, 36), ADD)
+    cp(R("f2"), R("s1", 36, 48))
+    ts(R("cf", 5, 6), age, 12.0, MUL)
+    ts(R("cf", 6, 7), age, 1.0, ALU.is_le)
+    ts(R("cf", 7, 8), age, 2.0, ALU.is_equal)
+    ts(R("f3"), R("iw", 44, 68), R("cf", 5, 6), ADD)
+    ts(R("f4"), R("iw", 68, 80), m32, ADD)
+    for name, w in (("msel", R("cf", 6, 7)), ("mdep", R("cf", 7, 8)), ("msum", 1.0)):
+        whole(R(name), 0)
+        ts(R(name, 15, 143, 16), R("iw", 36, 44), grp, ALU.is_equal, w, MUL)
+    act(R("mneg"), R("msum"), ID, scale=-1.0)
+    whole(R("ones", 0, A), 1)
+    mark_anchors("h0", 0.5)
+    pick(R("idp"), R("ones", 0, A), -1, ALU.is_equal, 0.0, 1)
+    for name, w in (("idn", -1.0), ("idk", KK), ("idb", 512.0), ("idf", 1.0)):
+        act(R(name), R("idp"), ID, scale=w)
+    whole(R("ones", A, 512), 1)
+    whole(R("c64"), -int(KK) // 128)
+    mark_anchors("gs", 0.5)
+    whole(R("za", 0, A), 0)
+    if sends:
+        whole(R("z0", A, 2 * A), 0)
+
+    def rows_from(blk, how):
+        dup(how, R("hi"), blk)
+        tt(R("lo"), blk, R("hi"), SUB)
+        dma("s", R("pw", rows=slice(0, 128, 16), lane=0), R("hi"), 49152)
+        dma("s", R("pw", rows=slice(1, 128, 16), lane=1), R("lo"), 49152)
+
+    for j, c in enumerate(C6N):
+        dup(OPT["hdup"][j], R("vd", *c), R("h0", *c))
+    rows_from(R("pari"), "v")
+    cp(R("t1"), G(R("pari"), R("f1")))
+    tr(R("t2"), R("t1"))
+    cp(R("l1"), G(R("t2"), R("f2")))
+    cp(R("pv"), G(R("t2"), R("f2")))
+
+    if gets:
+        send([rank - 1], R("upn"), R("upi"), "aup", None)
+        send([rank - 1], R("ann"), R("an"), "aan", None)
+    if sends:
+        arrive(rank + 1, R("upn"), "aup", [], 16.0)
+        arrive(rank + 1, R("ann"), "aan", [], 17.0)
+        cp(R("lh", 0, 8), R("upn"))
+
+    def off(name, c, base=0):
+        return R(name, base + c[0] // 16, base + c[1] // 16)
+
+    def compose(hwin, zwin, p16, e256, k, zout):
+        tt(R("uu", 256 * k, 256 * k + 256), G(hwin, p16), e256, MUL)
+        tt(zout, G(zwin, R(p16["n"], p16["c0"], p16["c0"] + 8)), R("uu", 256 * k + A, 256 * k + 256), ADD)
+        return R("uu", 256 * k, 256 * k + A)
+
+    lists = ["l1", "l2", "l4", "l8", "l16", "l32"]
+    wins = ["pw", "j2", "j4", "j8", "j16"]
+    own = OPT["zch"]
+    edge = own[-1][1]
+    for e in range(EP):
+        first = e == 0
+        whole(R("zb", 0, A), 0)
+        tail = {}
+        if not first:
+            for c in C3N:
+                act(R("xp", *c), G(R("xw"), off("l1", c)), ID)
+                tt(R("yy", *c), G(R("hs"), off("l1", c)), R("d0", *c), MUL)
+            for c in C6N:
+                mm(R("pb", *c), [(R("idp"), R("yy", *c)), (R("idp"), R("xw", *c)), (R("idn"), R("xp", *c)), (R("idb"), R("gs", *c))])
+            for c in C3N:
+                act(R("pb", *c), R("pb", *c), ABS)
+                act(R("pb", *c), R("pb", *c), ID, bias=-512.0)
+        vw = "h0" if first else "gs"
+        for r in range(5):
+            if first:
+                cp(R(lists[r + 1], 0, 8), R("pv", 0, 8))
+            if r < 4:
+                if first:
+                    dup("g", R(wins[r + 1], 0, A), R("pw", 0, A))
+                for c in C3N:
+                    act(R(wins[r + 1], *c), G(R(wins[r]), off(lists[r], c)), ID)
+                    x = off(exb(), c)
+                    mm(x, diag("msel", wins[r + 1], x["c0"], x["c1"]))
+                    cp(off(lists[r + 1], c), x)
+            vn = "va" if r % 2 == 0 else "vb"
+            mark_anchors(vn, 0.5 ** (2 ** (r + 1)))
+            for j, c in enumerate(C6N):
+                o = tt(R(vn, *c), G(R(vw), off(lists[r], c)), R("vd", *c), MUL)
+                if first and r == 0:
+                    dma("s", R("b0", *c), T.bt[:, c[0]:c[1]], 131072, after=[o])
+                if first and r == 1 and j in (0, 3):
+                    k = j // 3
+                    dma("s", R("nbi", NW * k, NW * k + NW), T.nb[:, NW * k:NW * k + NW], 98304, after=[o])
+                    cp(R("ln", NW * k, NW * k + NW), R("nbi", NW * k, NW * k + NW))
+                if first and r == 2:
+                    dma("s", R("d0", *c), T.dr[:, c[0]:c[1]], 131072, after=[o])
+                if r < 4:
+                    dup(OPT["vdup"][j], R("vd", *c), R(vn, *c))
+            vw = vn
+        if first:
+            for c in C6N:
+                mm(R("pb", *c), [(R("idp"), R("b0", *c)), (R("idk"), R("h0", *c)), (R("c64"), R("ones", 0, c[1] - c[0]))])
+            for c in C3N:
+                act(R("pb", *c), R("pb", *c), ABS)
+        for j, c in enumerate(C6N):
+            act(R("yy", *c), R("va", *c), SIGN)
+            tt(R("za", *c), R("yy", *c), R("pb", *c), MUL)
+            if c[0] < edge:
+                dup(OPT["zdup"][j], R("zd", c[0], min(c[1], edge)), R("za", c[0], min(c[1], edge)))
+        dma("s", R("pw", rows=slice(2, 128, 16), lane=2), R("va", rows=slice(2, 128, 16)), 49152)
+        mh, mz, mp = R("msg", 256 * e, 256 * e + A), R("msg", 256 * e + A, 256 * e + 256), R("ptr", 16 * e, 16 * e + 16)
+        if sends:
+            act(R("sj", 0, A), G(R("j8"), R("lh", 0, 8)), ID)
+            act(R("sj", A, 2 * A), G(R("j16"), R("lh", 0, 8)), ID)
+            x = exb()
+            mm(R(x, 0, 16), diag("msel", "sj", 0, 16))
+            cp(R("lh", 8, 24), R(x, 0, 16))
+            act(R("sk", 0, A), G(R("j8"), R("lh", 16, 24)), ID)
+            act(R("sk", A, 2 * A), G(R("j16"), R("lh", 16, 24)), ID)
+            x = exb()
+            mm(R(x, 0, 16), diag("msel", "sk", 0, 16))
+            cp(R("lh", 24, 32), R(x, 0, 8))
+            cp(R("ptr", 16 * e, 16 * e + 8), R(x, 8, 16))
+            cp(R("ptr", 16 * e + 8, 16 * e + 16), R(x, 8, 16))
+            act(R("hu"), G(R("va"), R("lh", 0, 8)), SIGN)
+            hdst = R("ee", 0, A) if rank == 0 else mh
+            if first:
+                tt(hdst, R("hu"), R("ann", 0, A), MUL)
+                tt(R("z0", 0, A), R("hu"), R("ann", A, 2 * A), MUL)
+            else:
+                act(hdst, R("hu"), ID)
+                tt(R("z0", 0, A), R("hu"), R("qq"), MUL)
+            if rank > 0:
+                send(later, R("lptr", 16 * (5 * e + rank), 16 * (5 * e + rank) + 16), mp, "ap%d_%d" % (e, rank), tail)
+        for c in C3N:
+            m0, m1 = c[0] // 16, c[1] // 16
+            act(R("j32", *c), G(R("j16"), off("l16", c)), ID)
+            x = spare(m0, m1)
+            mm(x, diag("msel", "j32", m0, m1))
+            cp(off("l32", c), x)
+        for c in C3N:
+            m0, m1 = c[0] // 16, c[1] // 16
+            x = spare(m0, m1)
+            mm(x, diag("mdep", "va", m0, m1))
+            act(off("dv", c), x, ABS)
+        for k in range(2):
+            nk, qk = "n%d" % k, "q%d" % k
+            for c in C3N:
+                m0, m1 = c[0] // 16, c[1] // 16
+                act(R(nk, *c), G(R("pw"), off("ln", c, NW * k)), ID)
+                x = spare(m0, m1)
+                mm(x, diag("msel", nk, m0, m1))
+                cp(off("lc%d" % k, c), x)
+                tt(off("e%d" % k, c), x, off("pv", c), SUB)
+                x = spare(m0, m1)
+                mm(x, diag("mdep", nk, m0, m1))
+                act(off(qk, c), x, ABS)
+            x = spare(8, NW)
+            mm(x, [(R("idp"), R(qk, 8, NW)), (R("idn"), R("dv", 8, NW))])
+            act(R("pen%d" % k, 8, NW), x, AF.Relu, scale=PEN)
+        if first:
+            for c in C3N:
+                act(R("gs", *c), R("d0", *c), SIGN, bias=127.5, scale=-1.0)
+                dup("s", R("vd", *c), R("gs", *c))
+        zw = "za"
+        mark = None
+        base = (R("an", 0, A), R("an", A, 2 * A)) if first else (R("ones", 0, A), R("xa"))
+        for r in range(5):
+            zn = "zb" if r % 2 == 0 else "za"
+            for j, c in enumerate(OPT["share"]):
+                zg = R("zg", 512 * j, 512 * j + c[1] - c[0])
+                act(zg, G(R(zw), off(lists[r], c)), ID)
+                mm(R("pb", *c), [(R("idf"), R(zw, *c))], True, False)
+                mm(R("pb", *c), [(R("idf"), zg)], False, True)
+                act(R(zn, *c), R("pb", *c), ID)
+            for j, c in enumerate(own):
+                o = tt(R(zn, *c), G(R(zw), off(lists[r], c)), R("zd", *c), ADD)
+                if r < 4:
+                    dup(OPT["zdup"][j], R("zd", *c), R(zn, *c))
+            zw = zn
+            if r == 2:
+                mark = o
+                if sends:
+                    tt(R("z1"), G(R(zw), R("lh", 0, 16)), R("z0"), ADD)
+                    tt(R("z2"), G(R(zw), R("lh", 16, 32)), R("z1"), ADD)
+                    if rank == 0:
+                        tt(R("ee", A, 2 * A), R("z2", 0, A), R("z2", A, 2 * A), ADD)
+                        act(mh, compose(base[0], base[1], mp, R("ee"), 0, R("yi")), ID)
+                    else:
+                        tt(R("yi"), R("z2", 0, A), R("z2", A, 2 * A), ADD)
+                    ts(R("yj"), R("yi"), 255, ALU.bitwise_and)
+                    cp(mz, R("yj"))
+                    s = 256 * (5 * e + rank)
+                    send(later, R("lmsg", s, s + 256), R("msg", 256 * e, 256 * e + 256), "am%d_%d" % (e, rank), tail)
+        hw, zt = base
+        if gets:
+            for f in range(rank):
+                s = 5 * e + f
+                arrive(f, R("lmsg", 256 * s, 256 * s + 256), "am%d_%d" % (e, f), [mark], OPT["arrive"])
+                if f > 0:
+                    arrive(f, R("lptr", 16 * s, 16 * s + 16), "ap%d_%d" % (e, f), [mark], 1.0)
+            s = 256 * 5 * e
+            hw, zt = R("lmsg", s, s + A), R("lmsg", s + A, s + 256)
+            for f in range(1, rank):
+                s = 5 * e + f
+                zo = R("zi") if f == rank - 1 else R("zz", A * f, A * f + A)
+                hw = compose(hw, zt, R("lptr", 16 * s, 16 * s + 16), R("lmsg", 256 * s, 256 * s + 256), f, zo)
+                zt = zo
+            if rank > 1:
+                ts(R("zj"), R("zi"), 255, ALU.bitwise_and)
+                zt = R("zj")
+        if first:
+            act(R("kh"), hw, ID, bias=MID, scale=KK)
+            tail["op"] = tt(R("zanc"), zt, R("kh"), ADD)
+        else:
+            tail["op"] = ts(R("zanc"), zt, MID, ADD)
+        for j, c in enumerate(C6):
+            tt(R("za", *c), G(hw, off("l32", c)), R("zb", *c), MUL)
+            tt(R("zb", *c), G(R("zanc"), off("l32", c)), R("za", *c), ADD)
+            act(R("yy", *c), R("zb", *c), ID, bias=-127.5)
+            if j in OPT["x_act"]:
+                mm(R("pb", *c), [(R("idf"), R("zb", *c))], True, False)
+                mm(R("pb", *c), [(R("idn"), R("yy", *c))], False, True)
+                act(R("xw", *c), R("pb", *c), ID)
+            else:
+                mm(R("pb", *c), [(R("idp"), R("yy", *c))])
+                tt(R("xw", *c), R("zb", *c), R("pb", *c), SUB)
+            dup(OPT["xdup"][j], R("xd", max(c[0], A), c[1]), R("xw", max(c[0], A), c[1]))
+        if first:
+            for c in C3:
+                act(R("hs", *c), R("zb", *c), SIGN, bias=-MID)
+            if rank == 0:
+                act(R("xa"), R("xw", 0, A), ID)
+            if sends:
+                tt(R("qq"), G(R("hs"), R("lh", 0, 8)), R("ann", A, 2 * A), MUL)
+        else:
+            for c in C3:
+                dma("s", T.yx[:, c[0]:c[1]], R("xw", *c), 262144)
+        for j, c in enumerate(C3N):
+            if j in OPT["c_act"]:
+                act(R("dc", *c), G(R("xw"), off("lc1", c)), ID)
+                for b in C6N[2 * j:2 * j + 2]:
+                    mm(R("pb", *b), [(R("idp"), R("dc", *b)), (R("idn"), R("xw", *b))])
+        for name, l in (("da", "l1"), ("db", "lc0"), ("dc", "lc1")):
+            for j, c in enumerate(C3N):
+                if name == "dc" and j in OPT["c_act"]:
+                    act(R("dc", *c), R("pb", *c), ABS)
+                else:
+                    tt(R(name, *c), G(R("xw"), off(l, c)), R("xd", *c), SUB)
+                    act(R(name, *c), R(name, *c), ABS)
+        for k, name in enumerate(("db", "dc")):
+            for c in C3N:
+                x = off("ex%d" % k, c)
+                mm(x, [(R("idp"), off("pen%d" % k, c))] + diag("mneg", "da", x["c0"], x["c1"]), True, False)
+                mm(x, diag("msum", name, x["c0"], x["c1"]), False, True)
+        n = (8, NW)
+        ta, tb = R("pb", 2568, 2752), R("pb", 2824, 3008)
+        ts(ta, R("ex0", *n), 0.0, ALU.is_lt)
+        ts(R("mm", *n), R("ex0", *n), 0.0, ALU.min)
+        tt(tb, ta, R("e0", *n), MUL)
+        tt(R("cc", *n), R("pv", *n), tb, ADD)
+        tt(ta, R("e1", *n), tb, SUB)
+        tt(R("w1", *n), R("ex1", *n), R("mm", *n), ALU.is_lt)
+        tt(tb, ta, R("w1", *n), MUL)
+        tt(R("pv", *n), R("cc", *n), tb, ADD)
+        if first:
+            cp(R("l1", *n), R("pv", *n))
+        act(R("t1"), G(R("pv"), R("f3")), ID)
+        tr(R("t2"), R("t1"))
+        act(R("blk"), G(R("t2"), R("f4")), ID)
+        if first:
+            rows_from(R("blk"), "a")
+        else:
+            dma("s", T.yp[:], R("blk"), 98304)
+    return ops
+
+
+def clash(a, b):
+    if a["lane"] is not None and b["lane"] is not None and a["lane"] != b["lane"]:
+        return False
+    if psum(a):
+        return a["c0"] // 512 <= (b["c1"] - 1) // 512 and b["c0"] // 512 <= (a["c1"] - 1) // 512
+    return a["c0"] < b["c1"] and b["c0"] < a["c1"]
+
+
+def schedule(ops):
+    seen = {}
+    for o in ops:
+        pre = set(p["id"] for p in o["after"])
+        acc = [(r, False) for r in o["rd"]] + [(r, True) for r in o["wr"]]
+        for r, w in acc:
+            for r2, w2, o2 in seen.get(r["n"], []):
+                if (w or w2 or (psum(r) and o2["eng"] != o["eng"])) and clash(r, r2):
+                    pre.add(o2["id"])
+        pre.discard(o["id"])
+        o["pre"] = pre
+        for r, w in acc:
+            seen.setdefault(r["n"], []).append((r, w, o))
+    hop = OPT["hop"]
+    nxt = [[] for _ in ops]
+    for o in ops:
+        for p in o["pre"]:
+            nxt[p].append(o["id"])
+    for o in reversed(ops):
+        tail = 0.0
+        if o["kind"] == "s":
+            tail = 250.0 if o["tail"] is None else OPT["urgent"] + o["tail"]["op"]["prio"]
+        o["prio"] = o["bonus"] + o["dur"] + o["lat"] + max([tail] + [hop + ops[k]["prio"] for k in nxt[o["id"]]])
+    left = [len(o["pre"]) for o in ops]
+    ready = [o["id"] for o in ops if not o["pre"]]
+    free = {}
+    order = []
+    while ready:
+        for k in ready:
+            o = ops[k]
+            o["est"] = max([free.get(o["eng"], 0.0)] + [ops[p]["end"] + hop for p in o["pre"]])
+        t0 = min(ops[k]["est"] for k in ready)
+        eng = [ops[k]["eng"] for k in ready if ops[k]["est"] == t0][0]
+        cand = [ops[k] for k in ready if ops[k]["eng"] == eng and ops[k]["est"] <= t0 + OPT["slack"]]
+        best = max(cand, key=lambda o: (t0 > 8.0 and o["dur"] < OPT["small"], o["prio"], -o["id"]))
+        if eng != "x":
+            free[eng] = best["est"] + best["dur"]
+        best["end"] = best["est"] + best["dur"] + best["lat"]
+        if best["kind"] == "d":
+            best["end"] = max(best["end"], free.get("dma", 0.0) + best["xfer"])
+            free["dma"] = best["end"]
+        order.append(best)
+        ready.remove(best["id"])
+        for k in nxt[best["id"]]:
+            left[k] -= 1
+            if left[k] == 0:
+                ready.append(k)
+    return order
+
+
+def rank_program(g, core, T, topo):
+    rank = T.rank_of(core)
+    if rank is None:
+        return
+    ops = build(rank, T, topo)
+    order = schedule(ops)
+    queue = {"v": g.vector, "a": g.scalar, "t": g.tensor, "g": g, "s": g.sync}
+    count = {"v": 0, "a": 0, "t": 0, "g": 0}
+    total = {}
+    for o in order:
+        if o["kind"] == "c":
+            count[o["eng"]] += 1
+            o["sig"] = ("q" + o["eng"], count[o["eng"]])
+        elif o["kind"] == "d":
+            o["sig"] = (o["sem"], 16)
+        elif o["kind"] == "r":
+            o["sig"] = (o["sem"], o["n"])
+        else:
+            total["sent"] = total.get("sent", 0) + o["n"]
+            continue
+        total[o["sig"][0]] = o["sig"][1]
+    waited = {}
+    for o in order:
+        if o["kind"] == "r":
+            continue
+        q = queue[o["eng"]]
+        need = {}
+        for p in o["pre"]:
+            p = ops[p]
+            if p["eng"] == "t" and o["eng"] == "t":
+                continue
+            s, n = p["sig"]
+            need[s] = max(need.get(s, 0), n)
+        for s in sorted(need):
+            if waited.get((o["eng"], s), 0) < need[s]:
+                q.wait_ge(T.sem[s], need[s])
+                waited[(o["eng"], s)] = need[s]
+        ins = o["fn"](q)
+        if o["kind"] == "c":
+            ins.then_inc(T.sem[o["sig"][0]], 1)
+        elif o["kind"] == "d":
+            ins.then_inc(T.sem[o["sem"]], 16)
+    for s in sorted(total):
+        if not any(waited.get((q, s), 0) >= total[s] for q in "vatgs"):
+            g.wait_ge(T.sem[s], total[s])

@@ -3,47 +3,56 @@ from concourse.mybir import AluOpType as ALU, ActivationFunctionType as AF
 
 V, A, NR, EP = 3072, 128, 6, 2
 NW = V // 16
-KK = 8192.0
-MID = 49152.0
-PEN = 2.0 ** 45
+KK = 16384.0
+LL = 65536
+PEN = 4096.0
+MS = A + 16
 
 BF, F32, I32, U16 = "bfloat16", "float32", "int32", "uint16"
 SCRATCH = {}
 for _d, _w, _names in (
-        (BF, V, "h0 b0 d0 gs va vb pw j2 j4 j8 j16 j32 n0 n1 da db dc xp yy hs xw vd xd"), (F32, V, "za zb zd"),
-        (U16, NW, "l1 l2 l4 l8 l16 l32 lc0 lc1"), (F32, NW, "pv e0 e1 w1 mm cc blk"), (BF, NW, "hi lo pen0 pen1 q0 q1 dv"),
-        (I32, NW, "pari"), (I32, 2 * NW, "nbi"), (U16, 2 * NW, "ln"), (F32, 2 * NW, "t1 t2"), (U16, 24, "f1 f3"), (U16, 12, "f2 f4"),
-        (I32, 16, "ci s2"), (F32, 16, "cf s3"), (F32, 80, "iw"), (F32, 48, "s1"), (BF, 144, "msel mdep msum mneg"),
-        (BF, 128, "idp idn idk idb c64 hu qq xa"), (F32, 128, "idf kh zanc"), (F32, 1024, "zg"), (BF, 512, "ones"),
-        (I32, 8, "upi upn"), (BF, 256, "an ann sj sk"), (U16, 32, "lh"), (F32, 256, "z0 z1 z2 ee"), (I32, 128, "zi zj yi yj"),
-        (BF, EP * 256, "msg"), (U16, EP * 16, "ptr"), (BF, EP * 5 * 256, "lmsg"), (U16, EP * 5 * 16, "lptr"),
-        (F32, 5 * 256, "uu"), (F32, 5 * 128, "zz")):
+        (BF, V, "h0 b0 d0 gs va vb vd pw j2 j4 j8 j16 j32 n0 n1 da db dc xd hs hm"), (F32, V, "za zb zd"), (I32, V, "ui xi"),
+        (U16, NW, "l1 l2 l4 l8 l16 l32 lc0 lc1"), (F32, NW, "pv e0 e1 w1c mn cc blk dp"), (BF, NW, "hi lo pen0 pen1 q0 q1 dv"),
+        (I32, NW, "pari"), (I32, 2 * NW, "nbi"), (U16, 2 * NW, "ln"), (F32, 2 * NW, "t1 t2"), (U16, 24, "f3"), (U16, 12, "f4"),
+        (I32, 16, "ci"), (F32, 16, "cf"), (F32, 80, "iw"), (BF, 144, "msel mdep msum mneg mtwo"),
+        (BF, A, "idp idn idk idb idl ones hu qq ez cu au"), (F32, A, "idf ze y0"), (F32, 1024, "zg"), (F32, 512, "zq"),
+        (I32, 8, "upi upn"), (BF, 256, "an ann sj sk"), (U16, 32, "lh"), (U16, 16, "pu"), (I32, A, "yi"),
+        (BF, EP * MS, "msg"), (BF, EP * A, "mz"), (BF, EP * 5 * MS, "lsg"), (BF, EP * 5 * A, "lz"), (U16, 5 * 8, "lp"),
+        (F32, 5 * A, "uu zz")):
     for _n in _names.split():
         SCRATCH[_n] = ("sbuf", [128, _w], _d)
 SCRATCH.update({"pb": ("psum", [128, V], F32), "ex0": ("psum", [128, 512], F32), "ex1": ("psum", [128, 512], F32)})
+SHARED = {"qd": "n0", "xp": "n1"}
 NDMA = 120
 SEMAPHORES = (["qv", "qa", "qt", "qg", "sent", "aup", "aan"] + ["dma%d" % i for i in range(NDMA)]
-              + ["am%d_%d" % (e, r) for e in range(EP) for r in range(5)] + ["ap%d_%d" % (e, r) for e in range(EP) for r in range(5)])
+              + ["am%d_%d" % (e, r) for e in range(EP) for r in range(5)] + ["as%d_%d" % (e, r) for e in range(EP) for r in range(5)])
 
 C3 = [(0, 1024), (1024, 2048), (2048, 3072)]
 C3N = [(A, 1024), (1024, 2048), (2048, 3072)]
 C6 = [(512 * i, 512 * i + 512) for i in range(6)]
 C6N = [(A, 512)] + C6[1:]
 OPT = {
-    "share": [(2304, 2560), (2560, 3072)],
-    "zch": [(A, 704), (704, 1280), (1280, 1792), (1792, 2304)],
-    "x_act": (0, 1, 2),
-    "c_act": (0, 1),
-    "hdup": "aaaggg", "vdup": "ssgssg", "zdup": "ggsgs", "xdup": "ssssss",
-    "cyc": 1.04e-3, "gc": 1.56, "pe": 0.55e-3, "bw": 2.0e5, "hop": 0.1, "fix": 0.07, "dl": 2.0,
-    "arrive": 11.0, "urgent": 14.0, "slack": 0.25, "small": 0.35,
+    "sch": [(A, 864), (864, 1600), (1600, 2336), (2336, 3072)], "hdup": "aaga", "vdup": "ssgs", "gdup": "s",
+    "share": [(2560, 3072)],
+    "zch": [(A, 768), (768, 1408), (1408, 1984), (1984, 2560)], "zdup": ("sgsg", "sgsg", "ssss", "sgsg"), "z0dup": "ssgsg", "early32": 1, "fine": True, "sboost": 3.0,
+    "slast": [(A, 1024), (1024, 2048), (2048, 2560), (2560, 3072)],
+    "votes": ("aaa", "vvv", "mmm"),
+    "nk": ("aaa", "aaa"), "xcv": "gagaga", "clip": "vvvvvv",
+    "cyc": 0.87e-3, "gc": 1.56, "pe": 0.44e-3, "bw": 3.0e5, "hop": 0.1, "fix": 0.06, "dl": 2.2,
+    "arrive": 8.0, "urgent": 10.0, "slack": 0.15, "small": 0.2, "look": 0.6, "gap": 2.0, "aboost": 6.0, "pboost": 0.0, "cboost": 30.0, "hboost": 15.0, "mboost": 10.0, "gboost": 0.0,
 }
+OPT.update(pboost=0, gboost=0, arrive=10, hboost=12, cboost=30, fine=True, sboost=0, hdup="avav", small=0.3)
 
 
 def R(name, c0=None, c1=None, step=1, rows=None, lane=None):
+    name = SHARED.get(name, name)
     if c0 is None:
         c0, c1 = 0, SCRATCH[name][1][1]
     return {"n": name, "c0": c0, "c1": c1, "st": step, "rows": rows, "lane": lane}
+
+
+def row(name, i):
+    return R(name, rows=slice(i, 128, 16), lane=i)
 
 
 def G(win, off):
@@ -71,17 +80,25 @@ def width(r):
     return len(range(r["c0"], r["c1"], r["st"]))
 
 
+def size(r):
+    return 2 if SCRATCH[r["n"]][2] in (BF, U16) else 4
+
+
 def two(*rs):
-    return all(SCRATCH[r["n"]][2] in (BF, U16) for r in rs)
+    return all(size(r) == 2 for r in rs)
 
 
 def psum(r):
     return SCRATCH[r["n"]][0] == "psum"
 
 
+def banks(c):
+    return [(max(c[0], b[0]), min(c[1], b[1])) for b in C6 if c[0] < b[1] and b[0] < c[1]]
+
+
 def build(rank, T, topo):
     ops = []
-    state = {"dma": 0, "ex": 0, "pb": 0}
+    state = {"dma": 0, "ex": 0, "pb": 0, "lazy": True, "boost": 0.0}
     CYC, GC, PEC, BW = OPT["cyc"], OPT["gc"], OPT["pe"], OPT["bw"]
     ID, ABS, SIGN = AF.Identity, AF.Abs, AF.Sign
     ADD, SUB, MUL = ALU.add, ALU.subtract, ALU.mult
@@ -90,7 +107,8 @@ def build(rank, T, topo):
         return ap(T, x) if isinstance(x, dict) else x
 
     def add(eng, fn, rd, wr, dur, **kw):
-        o = {"eng": eng, "fn": fn, "rd": regs(rd), "wr": regs(wr), "dur": dur, "lat": 0.0, "kind": "c", "after": [], "bonus": 0.0, "id": len(ops)}
+        o = {"eng": eng, "fn": fn, "rd": regs(rd), "wr": regs(wr), "dur": dur, "lat": 0.0, "kind": "c", "after": [], "bonus": 0.0,
+             "id": len(ops), "lazy": state["lazy"], "boost": state["boost"]}
         o.update(kw)
         ops.append(o)
         return o
@@ -117,27 +135,30 @@ def build(rank, T, topo):
     def tr(out, a):
         return add("v", lambda e: e.transpose(ap(T, out), ap(T, a)), [a], [out], vdur(width(out), 1))
 
+    def fill(out, x):
+        return add("v", lambda e: e.memset(ap(T, out), x), [], [out], vdur(width(out), 0.5 if two(out) else 1))
+
     def act(out, a, func, bias=0.0, scale=1.0):
         c = GC if "win" in a else 1
-        return add("a", lambda e: e.activation(ap(T, out), ap(T, a), func, bias=bias, scale=scale), [a], [out], 0.02 + vdur(width(out), c))
+        return add("a", lambda e: e.activation(ap(T, out), ap(T, a), func, bias=val(bias), scale=val(scale)), [a, bias, scale], [out],
+                   0.02 + vdur(width(out), c))
+
+    def fetch(how, out, a):
+        return cp(out, a) if how == "v" else act(out, a, ID)
 
     def mm(out, terms, start=True, stop=True):
         def fn(e):
             for k, (l, r) in enumerate(terms):
                 ins = e.matmul(ap(T, out), ap(T, l), ap(T, r), start and k == 0, stop and k == len(terms) - 1)
             return ins
-        return add("t", fn, [x for t in terms for x in t], [out], 0.05 + sum(1 if two(l) else 4 for l, r in terms) * max(64, width(out)) * PEC)
+        return add("t", fn, [x for t in terms for x in t], [out], 0.03 + sum(1 if two(l) else 4 for l, r in terms) * max(64, width(out)) * PEC)
 
     def diag(mat, src, m0, m1):
         return [(R(mat, 15 - i, 143 - i), R(src, 16 * m0 + i, 16 * m1, 16)) for i in range(16)]
 
-    def exb():
-        state["ex"] ^= 1
-        return "ex%d" % state["ex"]
-
     def spare(m0, m1):
-        state["pb"] = (state["pb"] + 1) % 4
-        return R("pb", 512 * state["pb"] + m0, 512 * state["pb"] + m1)
+        state["ex"] ^= 1
+        return R("ex%d" % state["ex"], m0, m1)
 
     def iota(out, pattern, base, mult):
         if SCRATCH[out["n"]][2] != I32:
@@ -146,31 +167,26 @@ def build(rank, T, topo):
             fn = lambda e: e.iota(ap(T, out), pattern, base, mult)
         return add("g", fn, [], [out], 0.15 + 2 * width(out) * CYC)
 
-    def whole(out, x):
-        return iota(out, [[0, width(out)]], x, 0)
-
     def pick(out, a, step, op, other, mult):
         n = width(out)
         return add("g", lambda e: e.affine_select(ap(T, out), ap(T, a), [[step, n]], op, other, 0, mult), [a], [out], 0.2 + 2 * n * CYC)
 
     def mark_anchors(name, x):
-        return pick(R(name, 0, A), R("ones", 0, A), 0, ALU.not_equal, x, 0)
+        return pick(R(name, 0, A), R("ones"), 0, ALU.not_equal, x, 0)
 
     def dma(q, out, in_, nbytes, after=(), bonus=0.0):
         rd = [in_] if isinstance(in_, dict) else []
         wr = [out] if isinstance(out, dict) else []
         k = state["dma"]
         state["dma"] += 1
-        return add(q, lambda e: e.dma_start(val(out), val(in_)), rd, wr, 0.1, kind="d", lat=OPT["dl"] + nbytes / BW, xfer=nbytes / BW, bonus=bonus,
-                   sem="dma%d" % k, after=list(after))
+        return add(q, lambda e: e.dma_start(val(out), val(in_)), rd, wr, 0.1, kind="d", lat=OPT["dl"] + nbytes / BW, xfer=nbytes / BW,
+                   bonus=bonus, sem="dma%d" % k, after=list(after))
 
     def dup(how, out, a):
         if how == "s":
-            return dma("s", out, a, 128 * width(a) * (2 if two(a) else 4))
-        if how == "a":
-            return act(out, a, ID)
-        if how == "v":
-            return cp(out, a)
+            return dma("s", out, a, 128 * width(a) * size(a))
+        if how in "av":
+            return fetch(how, out, a)
         return pick(out, a, 0, ALU.is_ge, 0.0, 0)
 
     me = T.cores[rank]
@@ -186,183 +202,180 @@ def build(rank, T, topo):
     def arrive(frm, buf, sem, after, lat):
         return add("x", None, [], [buf], 0.0, kind="r", lat=lat, sem=sem, n=len(topo.engines(T.cores[frm], me)), after=list(after))
 
+    def off(name, c, base=0):
+        return R(name, base + c[0] // 16, base + c[1] // 16)
+
     sends, gets = rank < NR - 1, rank > 0
     later = range(NR - 1, rank, -1)
 
     dma("s", R("pari"), T.par[:], 98304, bonus=300.0)
-    dma("a", R("h0", A, 1536), T.hf[:, A:1536], 380000, bonus=80.0)
-    dma("s", R("h0", 1536, V), T.hf[:, 1536:V], 380000, bonus=80.0)
-    dma("s", R("an", 0, A), T.hf[:, 0:A], 32768)
-    dma("s", R("an", A, 2 * A), T.bt[:, 0:A], 32768)
+    for c in C3N:
+        dma("s", R("h0", *c), T.hf[:, c[0]:c[1]], 262144, bonus=80.0)
+    dma("a", R("an", 0, A), T.hf[:, 0:A], 32768)
+    dma("a", R("an", A, 2 * A), T.bt[:, 0:A], 32768)
     if gets:
-        dma("s", R("upi"), T.up[:], 4096)
+        dma("a", R("upi"), T.up[:], 4096)
 
+    state["boost"] = OPT["cboost"]
     iota(R("ci", 0, 1), [[0, 1]], 0, 1)
-    iota(R("iw", 0, 24), [[16, 12], [0, 2]], 0, 0)
-    iota(R("iw", 24, 36), [[16, 12]], 0, 0)
+    fill(R("ones"), 1.0)
+    pick(R("idp"), R("ones"), -1, ALU.is_equal, 0.0, 1)
+    for name, w in (("idn", -1.0), ("idk", KK), ("idb", 512.0), ("idl", float(LL)), ("idf", 1.0)):
+        act(R(name), R("idp"), ID, scale=w)
     iota(R("iw", 36, 44), [[1, 8]], 0, 0)
     iota(R("iw", 44, 68), [[1, 12], [0, 2]], 0, 0)
     iota(R("iw", 68, 80), [[32, 12]], 0, 0)
-    add("v", lambda e: e.memset(ap(T, R("pw")), 0.0), [], [R("pw")], vdur(V, 0.5))
-    for k, x in ((1, 15), (2, 16), (3, 31)):
+    fill(R("pw"), 0.0)
+    for k, x in ((2, 15), (3, 31)):
         ts(R("ci", k, k + 1), R("ci", 0, 1), x, ALU.bitwise_and)
     ts(R("ci", 4, 5), R("ci", 0, 1), 4, ALU.arith_shift_right)
-    cp(R("cf", 1, 5), R("ci", 1, 5))
-    age, odd, m32, grp = R("cf", 1, 2), R("cf", 2, 3), R("cf", 3, 4), R("cf", 4, 5)
-    ts(R("f1"), R("iw", 0, 24), age, ADD)
-    ts(R("s1", 0, 12), R("iw", 24, 36), age, ADD)
-    ts(R("s3", 0, 12), R("s1", 0, 12), -5.5, ADD, 1.0 / 12.0, MUL)
-    cp(R("s2", 0, 12), R("s3", 0, 12))
-    ts(R("s1", 12, 24), R("s2", 0, 12), -383.0, MUL, odd, ADD)
-    ts(R("s1", 24, 36), R("s1", 0, 12), 32.0, MUL)
-    tt(R("s1", 36, 48), R("s1", 12, 24), R("s1", 24, 36), ADD)
-    cp(R("f2"), R("s1", 36, 48))
-    ts(R("cf", 5, 6), age, 12.0, MUL)
+    cp(R("cf", 2, 5), R("ci", 2, 5))
+    age, m32, grp = R("cf", 2, 3), R("cf", 3, 4), R("cf", 4, 5)
+    act(R("cf", 5, 6), age, ID, scale=12.0)
     ts(R("cf", 6, 7), age, 1.0, ALU.is_le)
     ts(R("cf", 7, 8), age, 2.0, ALU.is_equal)
     ts(R("f3"), R("iw", 44, 68), R("cf", 5, 6), ADD)
     ts(R("f4"), R("iw", 68, 80), m32, ADD)
     for name, w in (("msel", R("cf", 6, 7)), ("mdep", R("cf", 7, 8)), ("msum", 1.0)):
-        whole(R(name), 0)
+        fill(R(name), 0.0)
         ts(R(name, 15, 143, 16), R("iw", 36, 44), grp, ALU.is_equal, w, MUL)
     act(R("mneg"), R("msum"), ID, scale=-1.0)
-    whole(R("ones", 0, A), 1)
-    mark_anchors("h0", 0.5)
-    pick(R("idp"), R("ones", 0, A), -1, ALU.is_equal, 0.0, 1)
-    for name, w in (("idn", -1.0), ("idk", KK), ("idb", 512.0), ("idf", 1.0)):
-        act(R(name), R("idp"), ID, scale=w)
-    whole(R("ones", A, 512), 1)
-    whole(R("c64"), -int(KK) // 128)
-    mark_anchors("gs", 0.5)
-    whole(R("za", 0, A), 0)
+    act(R("mtwo"), R("msum"), ID, scale=2.0)
+    mark_anchors("h0", 2.0)
+    state["boost"] = 0.0
+    mark_anchors("gs", 2.0)
     if sends:
-        whole(R("z0", A, 2 * A), 0)
+        fill(R("msg"), 0.0)
 
     def rows_from(blk, how):
-        dup(how, R("hi"), blk)
         tt(R("lo"), blk, R("hi"), SUB)
-        dma("s", R("pw", rows=slice(0, 128, 16), lane=0), R("hi"), 49152)
-        dma("s", R("pw", rows=slice(1, 128, 16), lane=1), R("lo"), 49152)
+        dma("s", row("pw", 0), R("hi"), 49152)
+        dma(how, row("pw", 1), R("lo"), 49152)
 
-    for j, c in enumerate(C6N):
+    sch = OPT["sch"]
+    for j, c in enumerate(sch):
         dup(OPT["hdup"][j], R("vd", *c), R("h0", *c))
-    rows_from(R("pari"), "v")
-    cp(R("t1"), G(R("pari"), R("f1")))
-    tr(R("t2"), R("t1"))
-    cp(R("l1"), G(R("t2"), R("f2")))
-    cp(R("pv"), G(R("t2"), R("f2")))
+    act(R("hi"), R("pari"), ID)
+    rows_from(R("pari"), "a")
+    for c in C3:
+        x = off("pb", c, c[0])
+        mm(x, diag("msel", "pw", c[0] // 16, c[1] // 16))
+        cp(off("l1", c), x)
+        cp(off("pv", c), x)
+    cp(R("l32", 0, 8), R("l1", 0, 8))
 
     if gets:
         send([rank - 1], R("upn"), R("upi"), "aup", None)
         send([rank - 1], R("ann"), R("an"), "aan", None)
     if sends:
-        arrive(rank + 1, R("upn"), "aup", [], 16.0)
-        arrive(rank + 1, R("ann"), "aan", [], 17.0)
+        arrive(rank + 1, R("upn"), "aup", [], 12.0)
+        arrive(rank + 1, R("ann"), "aan", [], 13.0)
         cp(R("lh", 0, 8), R("upn"))
 
-    def off(name, c, base=0):
-        return R(name, base + c[0] // 16, base + c[1] // 16)
-
-    def compose(hwin, zwin, p16, e256, k, zout):
-        tt(R("uu", 256 * k, 256 * k + 256), G(hwin, p16), e256, MUL)
-        tt(zout, G(zwin, R(p16["n"], p16["c0"], p16["c0"] + 8)), R("uu", 256 * k + A, 256 * k + 256), ADD)
-        return R("uu", 256 * k, 256 * k + A)
-
     lists = ["l1", "l2", "l4", "l8", "l16", "l32"]
-    wins = ["pw", "j2", "j4", "j8", "j16"]
+    wins = ["pw", "j2", "j4", "j8", "j16", "j32"]
+
+    def pointers(r, c, after):
+        for b in banks(c) if r == 4 and OPT["fine"] else [c]:
+            act(R(wins[r + 1], *b), G(R(wins[r]), off(lists[r], b)), ID)["after"] = after
+        x = spare(c[0] // 16, c[1] // 16)
+        mm(x, diag("msel", wins[r + 1], x["c0"], x["c1"]))
+        cp(off(lists[r + 1], c), x)
+
     own = OPT["zch"]
     edge = own[-1][1]
+    state["lazy"] = False
     for e in range(EP):
         first = e == 0
-        whole(R("zb", 0, A), 0)
         tail = {}
         if not first:
             for c in C3N:
-                act(R("xp", *c), G(R("xw"), off("l1", c)), ID)
-                tt(R("yy", *c), G(R("hs"), off("l1", c)), R("d0", *c), MUL)
-            for c in C6N:
-                mm(R("pb", *c), [(R("idp"), R("yy", *c)), (R("idp"), R("xw", *c)), (R("idn"), R("xp", *c)), (R("idb"), R("gs", *c))])
-            for c in C3N:
-                act(R("pb", *c), R("pb", *c), ABS)
-                act(R("pb", *c), R("pb", *c), ID, bias=-512.0)
+                act(R("xp", *c), G(R("xd"), off("l1", c)), ID)
+                tt(R("qd", *c), G(R("hs"), off("l1", c)), R("d0", *c), MUL)
         vw = "h0" if first else "gs"
         for r in range(5):
-            if first:
-                cp(R(lists[r + 1], 0, 8), R("pv", 0, 8))
-            if r < 4:
-                if first:
-                    dup("g", R(wins[r + 1], 0, A), R("pw", 0, A))
-                for c in C3N:
-                    act(R(wins[r + 1], *c), G(R(wins[r]), off(lists[r], c)), ID)
-                    x = off(exb(), c)
-                    mm(x, diag("msel", wins[r + 1], x["c0"], x["c1"]))
-                    cp(off(lists[r + 1], c), x)
+            if first and r < 4:
+                dup("g", R(wins[r + 1], 0, A), R("pw", 0, A))
+            for c in C3N if r < 4 else C3N[:OPT["early32"]]:
+                pointers(r, c, [])
             vn = "va" if r % 2 == 0 else "vb"
-            mark_anchors(vn, 0.5 ** (2 ** (r + 1)))
-            for j, c in enumerate(C6N):
+            mark_anchors(vn, 2.0 ** (2 ** (r + 1)))
+            for j, c in enumerate(sch if r < 4 else OPT["slast"]):
                 o = tt(R(vn, *c), G(R(vw), off(lists[r], c)), R("vd", *c), MUL)
-                if first and r == 0:
-                    dma("s", R("b0", *c), T.bt[:, c[0]:c[1]], 131072, after=[o])
-                if first and r == 1 and j in (0, 3):
-                    k = j // 3
-                    dma("s", R("nbi", NW * k, NW * k + NW), T.nb[:, NW * k:NW * k + NW], 98304, after=[o])
-                    cp(R("ln", NW * k, NW * k + NW), R("nbi", NW * k, NW * k + NW))
-                if first and r == 2:
-                    dma("s", R("d0", *c), T.dr[:, c[0]:c[1]], 131072, after=[o])
                 if r < 4:
                     dup(OPT["vdup"][j], R("vd", *c), R(vn, *c))
+                if first and r == 0:
+                    dma("s", R("b0", *c), T.bt[:, c[0]:c[1]], 190000, after=[o])
+                if first and r == 2 and j in (0, 2):
+                    n = (NW * j // 2, NW * j // 2 + NW)
+                    dma("s", R("nbi", *n), T.nb[:, n[0]:n[1]], 98304, after=[o])
+                    cp(R("ln", *n), R("nbi", *n))
+                if first and r == 4:
+                    dma("s", R("d0", *c), T.dr[:, c[0]:c[1]], 190000, after=[o])
             vw = vn
-        if first:
-            for c in C6N:
-                mm(R("pb", *c), [(R("idp"), R("b0", *c)), (R("idk"), R("h0", *c)), (R("c64"), R("ones", 0, c[1] - c[0]))])
-            for c in C3N:
-                act(R("pb", *c), R("pb", *c), ABS)
+        smark = o
+        state["boost"] = OPT["pboost"]
+        for c in C6N:
+            if first:
+                mm(R("pb", *c), [(R("idp"), R("b0", *c)), (R("idk"), R("h0", *c))])
+            else:
+                mm(R("pb", *c), [(R("idp"), R("qd", *c)), (R("idp"), R("xd", *c)), (R("idn"), R("xp", *c)), (R("idb"), R("gs", *c))])
+            act(R("zb", *c), R("pb", *c), ABS, bias=-KK if first else 0.0)
+            mm(R("pb", *c), [(R("idf"), R("zb", *c))], True, False)
+        state["boost"] = 0.0
+        mark_anchors("za", float(LL))
         for j, c in enumerate(C6N):
-            act(R("yy", *c), R("va", *c), SIGN)
-            tt(R("za", *c), R("yy", *c), R("pb", *c), MUL)
+            if OPT["clip"][j] == "v":
+                ts(R("hm", *c), R("va", *c), 1.0, ALU.min, -1.0, ALU.max)
+            else:
+                act(R("hm", *c), R("va", *c), SIGN)
+            mm(R("pb", *c), [(R("idl"), R("hm", *c))], False, True)
+            zmark = act(R("za", *c), R("pb", *c), ABS)
             if c[0] < edge:
-                dup(OPT["zdup"][j], R("zd", c[0], min(c[1], edge)), R("za", c[0], min(c[1], edge)))
-        dma("s", R("pw", rows=slice(2, 128, 16), lane=2), R("va", rows=slice(2, 128, 16)), 49152)
-        mh, mz, mp = R("msg", 256 * e, 256 * e + A), R("msg", 256 * e + A, 256 * e + 256), R("ptr", 16 * e, 16 * e + 16)
+                dup(OPT["z0dup"][j], R("zd", c[0], min(c[1], edge)), R("za", c[0], min(c[1], edge)))
+        dma("s", row("pw", 2), row("va", 2), 49152)
+        mh = R("msg", MS * e, MS * e + A)
         if sends:
+            state["boost"] = OPT["hboost"]
             act(R("sj", 0, A), G(R("j8"), R("lh", 0, 8)), ID)
-            act(R("sj", A, 2 * A), G(R("j16"), R("lh", 0, 8)), ID)
-            x = exb()
-            mm(R(x, 0, 16), diag("msel", "sj", 0, 16))
-            cp(R("lh", 8, 24), R(x, 0, 16))
+            act(R("sj", A, 2 * A), G(R("j16"), R("lh", 0, 8)), ID)["boost"] = 0.0
+            x = spare(0, 16)
+            mm(x, diag("msel", "sj", 0, 16))
+            cp(R("lh", 8, 24), x)
             act(R("sk", 0, A), G(R("j8"), R("lh", 16, 24)), ID)
             act(R("sk", A, 2 * A), G(R("j16"), R("lh", 16, 24)), ID)
-            x = exb()
-            mm(R(x, 0, 16), diag("msel", "sk", 0, 16))
-            cp(R("lh", 24, 32), R(x, 0, 8))
-            cp(R("ptr", 16 * e, 16 * e + 8), R(x, 8, 16))
-            cp(R("ptr", 16 * e + 8, 16 * e + 16), R(x, 8, 16))
+            x = spare(0, 16)
+            mm(x, diag("msel", "sk", 0, 16))
+            cp(R("lh", 24, 32), R(x["n"], 0, 8))
+            act(R("msg", MS * e + A, MS * e + A + 8), R(x["n"], 8, 16), ID)
             act(R("hu"), G(R("va"), R("lh", 0, 8)), SIGN)
-            hdst = R("ee", 0, A) if rank == 0 else mh
-            if first:
-                tt(hdst, R("hu"), R("ann", 0, A), MUL)
-                tt(R("z0", 0, A), R("hu"), R("ann", A, 2 * A), MUL)
+            tt(R("ez"), R("hu"), R("ann", A, 2 * A) if first else R("qq"), MUL)
+            if rank == 0:
+                cp(R("pu", 0, 8), R(x["n"], 8, 16))
+                act(R("au"), G(R("an", A, 2 * A), R("pu", 0, 8)), ID)
+            if rank == 0 and first:
+                act(R("cu"), G(R("an", 0, A), R("pu", 0, 8)), ID)
+                tt(R("qq"), R("cu"), R("hu"), MUL)
+                tt(mh, R("qq"), R("ann", 0, A), MUL)
+            elif first:
+                tt(mh, R("hu"), R("ann", 0, A), MUL)
             else:
-                act(hdst, R("hu"), ID)
-                tt(R("z0", 0, A), R("hu"), R("qq"), MUL)
-            if rank > 0:
-                send(later, R("lptr", 16 * (5 * e + rank), 16 * (5 * e + rank) + 16), mp, "ap%d_%d" % (e, rank), tail)
+                act(mh, R("hu"), ID)
+            s = MS * (5 * e + rank)
+            send(later, R("lsg", s, s + MS), R("msg", MS * e, MS * e + MS), "as%d_%d" % (e, rank), tail)
+            state["boost"] = 0.0
+        for c in C3N[OPT["early32"]:]:
+            pointers(4, c, [zmark])
         for c in C3N:
-            m0, m1 = c[0] // 16, c[1] // 16
-            act(R("j32", *c), G(R("j16"), off("l16", c)), ID)
-            x = spare(m0, m1)
-            mm(x, diag("msel", "j32", m0, m1))
-            cp(off("l32", c), x)
-        for c in C3N:
-            m0, m1 = c[0] // 16, c[1] // 16
-            x = spare(m0, m1)
-            mm(x, diag("mdep", "va", m0, m1))
+            x = spare(c[0] // 16, c[1] // 16)
+            mm(x, diag("mdep", "va", x["c0"], x["c1"]))
             act(off("dv", c), x, ABS)
         for k in range(2):
             nk, qk = "n%d" % k, "q%d" % k
-            for c in C3N:
+            for j, c in enumerate(C3N):
                 m0, m1 = c[0] // 16, c[1] // 16
-                act(R(nk, *c), G(R("pw"), off("ln", c, NW * k)), ID)
+                for b in banks(c) if OPT["fine"] else [c]:
+                    fetch(OPT["nk"][k][j], R(nk, *b), G(R("pw"), off("ln", b, NW * k)))
                 x = spare(m0, m1)
                 mm(x, diag("msel", nk, m0, m1))
                 cp(off("lc%d" % k, c), x)
@@ -371,117 +384,125 @@ def build(rank, T, topo):
                 mm(x, diag("mdep", nk, m0, m1))
                 act(off(qk, c), x, ABS)
             x = spare(8, NW)
-            mm(x, [(R("idp"), R(qk, 8, NW)), (R("idn"), R("dv", 8, NW))])
+            mm(x, [(R("idn"), R(qk, 8, NW)), (R("idp"), R("dv", 8, NW))])
             act(R("pen%d" % k, 8, NW), x, AF.Relu, scale=PEN)
         if first:
+            state["boost"] = OPT["gboost"]
             for c in C3N:
                 act(R("gs", *c), R("d0", *c), SIGN, bias=127.5, scale=-1.0)
-                dup("s", R("vd", *c), R("gs", *c))
+                dup(OPT["gdup"], R("vd", *c), R("gs", *c))
+            state["boost"] = 0.0
         zw = "za"
         mark = None
-        base = (R("an", 0, A), R("an", A, 2 * A)) if first else (R("ones", 0, A), R("xa"))
         for r in range(5):
             zn = "zb" if r % 2 == 0 else "za"
+            mark_anchors(zn, float(LL * 2 ** (r + 1)))
+            state["boost"] = OPT["sboost"]
             for j, c in enumerate(OPT["share"]):
                 zg = R("zg", 512 * j, 512 * j + c[1] - c[0])
                 act(zg, G(R(zw), off(lists[r], c)), ID)
                 mm(R("pb", *c), [(R("idf"), R(zw, *c))], True, False)
                 mm(R("pb", *c), [(R("idf"), zg)], False, True)
                 act(R(zn, *c), R("pb", *c), ID)
+            state["boost"] = 0.0
             for j, c in enumerate(own):
                 o = tt(R(zn, *c), G(R(zw), off(lists[r], c)), R("zd", *c), ADD)
                 if r < 4:
-                    dup(OPT["zdup"][j], R("zd", *c), R(zn, *c))
+                    dup(OPT["zdup"][r][j], R("zd", *c), R(zn, *c))
             zw = zn
             if r == 2:
                 mark = o
                 if sends:
-                    tt(R("z1"), G(R(zw), R("lh", 0, 16)), R("z0"), ADD)
-                    tt(R("z2"), G(R(zw), R("lh", 16, 32)), R("z1"), ADD)
-                    if rank == 0:
-                        tt(R("ee", A, 2 * A), R("z2", 0, A), R("z2", A, 2 * A), ADD)
-                        act(mh, compose(base[0], base[1], mp, R("ee"), 0, R("yi")), ID)
+                    state["boost"] = OPT["mboost"]
+                    act(R("zq"), G(R(zw), R("lh")), ID)
+                    x = R("pb", 0, A)
+                    mm(x, [(R("idp"), R("ez"))] + ([(R("idp"), R("au"))] if rank == 0 and not first else [])
+                       + [(R("idf"), R("zq", A * k, A * k + A)) for k in range(4)])
+                    if rank == 0 and first:
+                        tt(R("ze"), x, R("cu"), MUL)
+                        tt(R("yi"), R("ze"), R("au"), ADD)
                     else:
-                        tt(R("yi"), R("z2", 0, A), R("z2", A, 2 * A), ADD)
-                    ts(R("yj"), R("yi"), 255, ALU.bitwise_and)
-                    cp(mz, R("yj"))
-                    s = 256 * (5 * e + rank)
-                    send(later, R("lmsg", s, s + 256), R("msg", 256 * e, 256 * e + 256), "am%d_%d" % (e, rank), tail)
-        hw, zt = base
+                        cp(R("yi"), x)
+                    ts(R("yi"), R("yi"), 255, ALU.bitwise_and)
+                    mz = R("mz", A * e, A * e + A)
+                    act(mz, R("yi"), ID)
+                    s = A * (5 * e + rank)
+                    send(later, R("lz", s, s + A), mz, "am%d_%d" % (e, rank), tail)
+                    state["boost"] = 0.0
         if gets:
             for f in range(rank):
                 s = 5 * e + f
-                arrive(f, R("lmsg", 256 * s, 256 * s + 256), "am%d_%d" % (e, f), [mark], OPT["arrive"])
-                if f > 0:
-                    arrive(f, R("lptr", 16 * s, 16 * s + 16), "ap%d_%d" % (e, f), [mark], 1.0)
-            s = 256 * 5 * e
-            hw, zt = R("lmsg", s, s + A), R("lmsg", s + A, s + 256)
-            for f in range(1, rank):
+                arrive(f, R("lsg", MS * s, MS * s + MS), "as%d_%d" % (e, f), [smark], 14.0)
+                arrive(f, R("lz", A * s, A * s + A), "am%d_%d" % (e, f), [mark], OPT["arrive"])
+            for f in range(rank):
                 s = 5 * e + f
-                zo = R("zi") if f == rank - 1 else R("zz", A * f, A * f + A)
-                hw = compose(hw, zt, R("lptr", 16 * s, 16 * s + 16), R("lmsg", 256 * s, 256 * s + 256), f, zo)
-                zt = zo
-            if rank > 1:
-                ts(R("zj"), R("zi"), 255, ALU.bitwise_and)
-                zt = R("zj")
-        if first:
-            act(R("kh"), hw, ID, bias=MID, scale=KK)
-            tail["op"] = tt(R("zanc"), zt, R("kh"), ADD)
+                u, y = R("uu", A * f, A * f + A), R("zz", A * f, A * f + A)
+                if f == 0:
+                    act(u, R("lz", A * s, A * s + A), ID, bias=float(LL))
+                else:
+                    cp(R("lp", 8 * f, 8 * f + 8), R("lsg", MS * s + A, MS * s + A + 8))
+                    tt(u, G(yw, R("lp", 8 * f, 8 * f + 8)), R("lz", A * s, A * s + A), ADD)
+                tt(y, u, R("lsg", MS * s, MS * s + A), MUL)
+                yw = y
         else:
-            tail["op"] = ts(R("zanc"), zt, MID, ADD)
+            yw = R("zz", A * e, A * e + A)
+            act(R("y0"), R("an", A, 2 * A), ID, bias=float(LL))
+            tt(yw, R("y0"), R("an", 0, A) if first else R("ones"), MUL)
         for j, c in enumerate(C6):
-            tt(R("za", *c), G(hw, off("l32", c)), R("zb", *c), MUL)
-            tt(R("zb", *c), G(R("zanc"), off("l32", c)), R("za", *c), ADD)
-            act(R("yy", *c), R("zb", *c), ID, bias=-127.5)
-            if j in OPT["x_act"]:
-                mm(R("pb", *c), [(R("idf"), R("zb", *c))], True, False)
-                mm(R("pb", *c), [(R("idn"), R("yy", *c))], False, True)
-                act(R("xw", *c), R("pb", *c), ID)
-            else:
-                mm(R("pb", *c), [(R("idp"), R("yy", *c))])
-                tt(R("xw", *c), R("zb", *c), R("pb", *c), SUB)
-            dup(OPT["xdup"][j], R("xd", max(c[0], A), c[1]), R("xw", max(c[0], A), c[1]))
+            o = tt(R("za", *c), G(yw, off("l32", c)), R("zb", *c), ADD)
+            tail.setdefault("op", o)
+            act(R("ui", *c), R("za", *c), ABS, bias=(KK if first else 0.0) - 32.0 * LL)
+            ts(R("xi", *c), R("ui", *c), 255, ALU.bitwise_and)["boost"] = OPT["aboost"]
+            dup(OPT["xcv"][j], R("xd", *c), R("xi", *c))
         if first:
             for c in C3:
-                act(R("hs", *c), R("zb", *c), SIGN, bias=-MID)
-            if rank == 0:
-                act(R("xa"), R("xw", 0, A), ID)
+                act(R("hs", *c), R("ui", *c), SIGN, bias=-float(LL))
             if sends:
                 tt(R("qq"), G(R("hs"), R("lh", 0, 8)), R("ann", A, 2 * A), MUL)
         else:
             for c in C3:
-                dma("s", T.yx[:, c[0]:c[1]], R("xw", *c), 262144)
-        for j, c in enumerate(C3N):
-            if j in OPT["c_act"]:
-                act(R("dc", *c), G(R("xw"), off("lc1", c)), ID)
-                for b in C6N[2 * j:2 * j + 2]:
-                    mm(R("pb", *b), [(R("idp"), R("dc", *b)), (R("idn"), R("xw", *b))])
-        for name, l in (("da", "l1"), ("db", "lc0"), ("dc", "lc1")):
+                dma("s", T.yx[:, c[0]:c[1]], R("xd", *c), 262144)
+        sums = {}
+        for k, (name, l, pos) in enumerate((("da", "l1", "n0"), ("db", "lc0", "n1"), ("dc", "lc1", "hm"))):
             for j, c in enumerate(C3N):
-                if name == "dc" and j in OPT["c_act"]:
-                    act(R("dc", *c), R("pb", *c), ABS)
-                else:
-                    tt(R(name, *c), G(R("xw"), off(l, c)), R("xd", *c), SUB)
+                how = OPT["votes"][k][j]
+                m0, m1 = c[0] // 16, c[1] // 16
+                sums[k, j] = diag("msum", name, m0, m1)
+                if how == "a":
+                    act(R(name, *c), G(R("xd"), off(l, c)), ID)
+                    for b in banks(c):
+                        mm(R("pb", *b), [(R("idp"), R(name, *b)), (R("idn"), R("xd", *b))])
+                    act(R(name, *c), R("pb", *c), ABS)
+                    continue
+                tt(R(name, *c), G(R("xi"), off(l, c)), R("xd", *c), SUB)
+                if how == "m":
                     act(R(name, *c), R(name, *c), ABS)
-        for k, name in enumerate(("db", "dc")):
-            for c in C3N:
-                x = off("ex%d" % k, c)
-                mm(x, [(R("idp"), off("pen%d" % k, c))] + diag("mneg", "da", x["c0"], x["c1"]), True, False)
-                mm(x, diag("msum", name, x["c0"], x["c1"]), False, True)
+                else:
+                    ts(R(pos, *c), R(name, *c), 0.0, ALU.max)
+                    sums[k, j] = diag("mneg", name, m0, m1) + diag("mtwo", pos, m0, m1)
+        for j, c in enumerate(C3N):
+            x = off("pb", c)
+            mm(x, sums[0, j])
+            act(off("dp", c), x, ID)
+        for k in range(2):
+            for j, c in enumerate(C3N):
+                mm(off("ex%d" % k, c), [(R("idp"), off("pen%d" % k, c))] + sums[k + 1, j])
         n = (8, NW)
-        ta, tb = R("pb", 2568, 2752), R("pb", 2824, 3008)
-        ts(ta, R("ex0", *n), 0.0, ALU.is_lt)
-        ts(R("mm", *n), R("ex0", *n), 0.0, ALU.min)
-        tt(tb, ta, R("e0", *n), MUL)
-        tt(R("cc", *n), R("pv", *n), tb, ADD)
-        tt(ta, R("e1", *n), tb, SUB)
-        tt(R("w1", *n), R("ex1", *n), R("mm", *n), ALU.is_lt)
-        tt(tb, ta, R("w1", *n), MUL)
-        tt(R("pv", *n), R("cc", *n), tb, ADD)
+        ta, tb = R("ex0", 256 + 8, 256 + NW), R("ex1", 256 + 8, 256 + NW)
+        tt(R("w1c", *n), R("ex0", *n), R("dp", *n), ALU.is_lt)
+        tt(R("mn", *n), R("ex0", *n), R("dp", *n), ALU.min)
+        tt(ta, R("w1c", *n), R("e0", *n), MUL)
+        tt(R("cc", *n), ta, R("pv", *n), ADD)
+        tt(ta, ta, R("e1", *n), SUB)
+        tt(R("w1c", *n), R("ex1", *n), R("mn", *n), ALU.is_lt)
+        tt(tb, ta, R("w1c", *n), MUL)
+        tt(R("pv", *n), R("cc", *n), tb, SUB)
         if first:
             cp(R("l1", *n), R("pv", *n))
         act(R("t1"), G(R("pv"), R("f3")), ID)
         tr(R("t2"), R("t1"))
+        if first:
+            act(R("hi"), G(R("t2"), R("f4")), ID)
         act(R("blk"), G(R("t2"), R("f4")), ID)
         if first:
             rows_from(R("blk"), "a")
@@ -532,7 +553,11 @@ def schedule(ops):
         t0 = min(ops[k]["est"] for k in ready)
         eng = [ops[k]["eng"] for k in ready if ops[k]["est"] == t0][0]
         cand = [ops[k] for k in ready if ops[k]["eng"] == eng and ops[k]["est"] <= t0 + OPT["slack"]]
-        best = max(cand, key=lambda o: (t0 > 8.0 and o["dur"] < OPT["small"], o["prio"], -o["id"]))
+        best = max(cand, key=lambda o: (not o["lazy"] and o["dur"] < OPT["small"], o["prio"] + o["boost"], -o["id"]))
+        soon = [ops[k] for k in ready if ops[k]["eng"] == eng and ops[k]["est"] < best["est"] + OPT["look"] * best["dur"]
+                and ops[k]["prio"] + ops[k]["boost"] > best["prio"] + best["boost"] + OPT["gap"]]
+        if soon:
+            best = max(soon, key=lambda o: o["prio"] + o["boost"])
         if eng != "x":
             free[eng] = best["est"] + best["dur"]
         best["end"] = best["est"] + best["dur"] + best["lat"]

@@ -5,27 +5,27 @@ V, A, NR, EP = 3072, 128, 6, 2
 NW = V // 16
 KK = 16384.0
 LL = 65536
-PEN = 4096.0
+PEN = 2.0 ** 45
 MS = A + 16
 
-BF, F32, I32, U16 = "bfloat16", "float32", "int32", "uint16"
+BF, F16, F32, I32, U16 = "bfloat16", "float16", "float32", "int32", "uint16"
 SCRATCH = {}
 for _d, _w, _names in (
-        (BF, V, "h0 b0 d0 gs va vb vd pw j2 j4 j8 j16 j32 n0 n1 da db dc xd hs hm"), (F32, V, "za zb zd"), (I32, V, "ui xi"),
-        (U16, NW, "l1 l2 l4 l8 l16 l32 lc0 lc1"), (F32, NW, "pv e0 e1 w1c mn cc blk dp"), (BF, NW, "hi lo pen0 pen1 q0 q1 dv"),
-        (I32, NW, "pari"), (I32, 2 * NW, "nbi"), (U16, 2 * NW, "ln"), (F32, 2 * NW, "t1 t2"), (U16, 24, "f3"), (U16, 12, "f4"),
-        (I32, 16, "ci"), (F32, 16, "cf"), (F32, 80, "iw"), (BF, 144, "msel mdep msum mneg mtwo"),
-        (BF, A, "idp idn idk idb idl ones hu qq ez cu au"), (F32, A, "idf ze y0"), (F32, 1024, "zg"), (F32, 512, "zq"),
-        (I32, 8, "upi upn"), (BF, 256, "an ann sj sk"), (U16, 32, "lh"), (U16, 16, "pu"), (I32, A, "yi"),
-        (BF, EP * MS, "msg"), (BF, EP * A, "mz"), (BF, EP * 5 * MS, "lsg"), (BF, EP * 5 * A, "lz"), (U16, 5 * 8, "lp"),
+        (BF, V, "h0 d0 gs va vb vd pw j2 j4 j8 j16 n0 n1 da db dc xd hs hm"), (F32, V, "za zb zc zd"), (I32, V, "ui xi"),
+        (U16, NW, "l1 l2 l4 l8 l16 lc0 lc1"), (F32, NW, "pv e0 e1 w1c mn cc blk dp"), (BF, NW, "hi lo pen0 pen1 q0 q1 dv"),
+        (I32, NW, "pari"), (I32, 2 * NW, "nbi"), (U16, 2 * NW, "ln"), (F32, 2 * NW, "t1 t2"), (U16, 24, "f1 f3"), (U16, 12, "f2 f4"),
+        (I32, 16, "ci s2"), (F32, 16, "cf"), (F32, 48, "s1"), (F32, 80, "iw"), (BF, 144, "msel mdep msum mneg mtwo"),
+        (BF, A, "idp idn idk idb idc idl ones hu qq cu"), (F16, A, "idh"), (F16, V, "pp"), (BF, 256, "ez a0"), (F32, A, "idf idg"), (F32, 256, "y0"), (F32, 1024, "zq"), (F32, 512, "zg"), (BF, 512, "sl"),
+        (I32, 8, "upi upn"), (BF, 256, "an ann sj sk"), (U16, 64, "lh"), (I32, A, "yi"),
+        (F16, EP * MS, "msg"), (BF, A, "mo"), (F16, EP * 5 * MS, "lsg"), (BF, 5 * A, "ms"), (U16, 5 * 8, "lp"),
         (F32, 5 * A, "uu zz")):
     for _n in _names.split():
         SCRATCH[_n] = ("sbuf", [128, _w], _d)
 SCRATCH.update({"pb": ("psum", [128, V], F32), "ex0": ("psum", [128, 512], F32), "ex1": ("psum", [128, 512], F32)})
-SHARED = {"qd": "n0", "xp": "n1"}
+SHARED = {"qd": "n0", "xp": "n1", "b0": "da"}
 NDMA = 120
-SEMAPHORES = (["qv", "qa", "qt", "qg", "sent", "aup", "aan"] + ["dma%d" % i for i in range(NDMA)]
-              + ["am%d_%d" % (e, r) for e in range(EP) for r in range(5)] + ["as%d_%d" % (e, r) for e in range(EP) for r in range(5)])
+SEMAPHORES = (["qv", "qa", "qt", "qg", "sent", "aup", "aan", "aa0"] + ["dma%d" % i for i in range(NDMA)]
+              + ["am%d_%d" % (e, r) for e in range(EP) for r in range(5)])
 
 C3 = [(0, 1024), (1024, 2048), (2048, 3072)]
 C3N = [(A, 1024), (1024, 2048), (2048, 3072)]
@@ -37,11 +37,19 @@ OPT = {
     "zch": [(A, 768), (768, 1408), (1408, 1984), (1984, 2560)], "zdup": ("sgsg", "sgsg", "ssss", "sgsg"), "z0dup": "ssgsg", "early32": 1, "fine": True, "sboost": 3.0,
     "slast": [(A, 1024), (1024, 2048), (2048, 2560), (2560, 3072)],
     "votes": ("aaa", "vvv", "mmm"),
-    "nk": ("aaa", "aaa"), "xcv": "gagaga", "clip": "vvvvvv",
+    "nk": ("aaa", "aaa"), "xcv": "gagaga", "final": "vavvav", "sround": 1, "kboost": 3.0,
     "cyc": 0.87e-3, "gc": 1.56, "pe": 0.44e-3, "bw": 3.0e5, "hop": 0.1, "fix": 0.06, "dl": 2.2,
     "arrive": 8.0, "urgent": 10.0, "slack": 0.15, "small": 0.2, "look": 0.6, "gap": 2.0, "aboost": 6.0, "pboost": 0.0, "cboost": 30.0, "hboost": 15.0, "mboost": 10.0, "gboost": 0.0,
 }
-OPT.update(pboost=0, gboost=0, arrive=10, hboost=12, cboost=30, fine=True, sboost=0, hdup="avav", small=0.3)
+OPT.update(pboost=0, gboost=0, arrive=7, fine=True, sboost=0, hdup="avav", final="vvavaa", upper="vvvvaa", xcv="gggggg", compose=2.0, sarr=5.0,
+           cyc=0.83e-3, pe=0.42e-3, fix=0.05, hop=0.07, dl=1.7, bw=3.5e5, passes=2, shake=0.5, small=0.3, hboost=12, cboost=30, mboost=10,
+           aboost=6, kboost=3, uboost=4, lead=4.0, stretch=1.3, mix=0.0)
+OPT.update(compose=5.0, shake=0.0, small=0.4, pch=C6N, vch=C3N, z0dup="sgsg", slast=[(A, 1024)] + C6[2:], arrive=6.0, lp="g", head=12.0, vboost=(0.0, 0.0, 0.0), nboost=2.0, hold=((0, 2), (1, 0)), bload=1, zdup=("sgsg", "sgsg", "ssss", "ssss"), cboost=3, hop=0.1, rules=[(s, m, l, 2.0) for s in (0.08, 0.2) for m in (0.25, 0.45) for l in (0.3, 0.6)], first=3.0, vdup="ssss", pe=0.47e-3,
+           nch=[(A, 1600), (1600, V)], ngather=[(A, 864), (864, 1600), (1600, 2336), (2336, V)], hdup="aava",
+           upper=[((0, 1024), "v"), ((1024, 2048), "v"), (C6[4], "a"), (C6[5], "a")],
+           final=[((0, 768), "v"), ((768, 1536), "v"), (C6[3], "a"), (C6[4], "a"), (C6[5], "a")])
+OPT.update(nboost=0, arrive=5.5, head=0, lead=2, compose=3.5, gc=1.7, votes=("aaa", "vvm", "mmm"), hop=0.13, pch=C3N,
+           rules=[(0.08, 0.25, 0.3, 2.0), (0.2, 0.45, 0.6, 2.0), (0.15, 0.4, 0.6, 2.0), (0.08, 0.45, 0.6, 2.0)])
 
 
 def R(name, c0=None, c1=None, step=1, rows=None, lane=None):
@@ -81,7 +89,7 @@ def width(r):
 
 
 def size(r):
-    return 2 if SCRATCH[r["n"]][2] in (BF, U16) else 4
+    return 2 if SCRATCH[r["n"]][2] in (BF, F16, U16) else 4
 
 
 def two(*rs):
@@ -191,13 +199,13 @@ def build(rank, T, topo):
 
     me = T.cores[rank]
 
-    def send(tos, out, in_, sem, tail):
+    def send(tos, out, in_, sem, tail, dur=0.8):
         dsts = [T.cores[to] for to in tos]
         mask = topo.mask(me, dsts[0])
         ids = [DstId(rid=topo.addr(d)[0], pnc=topo.addr(d)[1]) for d in dsts]
         fn = lambda e: e.remote_dma_fused([RemoteDMATransfer(dst_ids=ids, dma_engine_mask=mask, remote_sem=T.sem[sem], srcs=[ap(T, in_)],
                                                              dsts=[ap(T, out) for d in dsts])], local_sem=T.sem["sent"])
-        return add("g", fn, [in_], [], 0.3, kind="s", tail=tail, n=len(topo.engines(me, dsts[0])))
+        return add("g", fn, [in_], [], dur, kind="s", tail=tail, n=len(topo.engines(me, dsts[0])))
 
     def arrive(frm, buf, sem, after, lat):
         return add("x", None, [], [buf], 0.0, kind="r", lat=lat, sem=sem, n=len(topo.engines(T.cores[frm], me)), after=list(after))
@@ -218,19 +226,28 @@ def build(rank, T, topo):
 
     state["boost"] = OPT["cboost"]
     iota(R("ci", 0, 1), [[0, 1]], 0, 1)
-    fill(R("ones"), 1.0)
+    one = fill(R("ones"), 1.0)
     pick(R("idp"), R("ones"), -1, ALU.is_equal, 0.0, 1)
-    for name, w in (("idn", -1.0), ("idk", KK), ("idb", 512.0), ("idl", float(LL)), ("idf", 1.0)):
-        act(R(name), R("idp"), ID, scale=w)
+    for name, w in (("idn", -1.0), ("idk", -KK), ("idb", 1024.0), ("idc", 512.0), ("idl", 2.0 * LL), ("idf", 1.0), ("idg", -1.0), ("idh", 1.0)):
+        made = act(R(name), R("idp"), ID, scale=w)
+    iota(R("iw", 24, 36), [[16, 12]], 0, 0)
+    iota(R("iw", 0, 24), [[16, 12], [0, 2]], 0, 0)
     iota(R("iw", 36, 44), [[1, 8]], 0, 0)
     iota(R("iw", 44, 68), [[1, 12], [0, 2]], 0, 0)
     iota(R("iw", 68, 80), [[32, 12]], 0, 0)
-    fill(R("pw"), 0.0)
-    for k, x in ((2, 15), (3, 31)):
+    fill(R("pw"), 0.0)["after"] = [one]
+    for k, x in ((1, 16), (2, 15), (3, 31)):
         ts(R("ci", k, k + 1), R("ci", 0, 1), x, ALU.bitwise_and)
     ts(R("ci", 4, 5), R("ci", 0, 1), 4, ALU.arith_shift_right)
-    cp(R("cf", 2, 5), R("ci", 2, 5))
-    age, m32, grp = R("cf", 2, 3), R("cf", 3, 4), R("cf", 4, 5)
+    cp(R("cf", 1, 5), R("ci", 1, 5))
+    odd, age, m32, grp = (R("cf", k, k + 1) for k in (1, 2, 3, 4))
+    ts(R("f1"), R("iw", 0, 24), age, ADD)
+    act(R("s1", 0, 12), R("iw", 24, 36), ID, bias=age)
+    act(R("s2", 0, 12), R("s1", 0, 12), ID, bias=-5.5 / 12.0, scale=1.0 / 12.0)
+    act(R("s1", 12, 24), R("s2", 0, 12), ID, bias=odd, scale=-383.0)
+    act(R("s1", 24, 36), R("s1", 0, 12), ID, scale=32.0)
+    tt(R("s1", 36, 48), R("s1", 12, 24), R("s1", 24, 36), ADD)
+    cp(R("f2"), R("s1", 36, 48))
     act(R("cf", 5, 6), age, ID, scale=12.0)
     ts(R("cf", 6, 7), age, 1.0, ALU.is_le)
     ts(R("cf", 7, 8), age, 2.0, ALU.is_equal)
@@ -243,9 +260,11 @@ def build(rank, T, topo):
     act(R("mtwo"), R("msum"), ID, scale=2.0)
     mark_anchors("h0", 2.0)
     state["boost"] = 0.0
-    mark_anchors("gs", 2.0)
+    mark_anchors("gs", 1.0)
     if sends:
-        fill(R("msg"), 0.0)
+        for e in range(EP):
+            act(R("msg", MS * e + A + 8, MS * e + MS), R("ones", 0, 8), ID)
+        fill(R("ez", A, 2 * A), 0.0)
 
     def rows_from(blk, how):
         tt(R("lo"), blk, R("hi"), SUB)
@@ -255,86 +274,88 @@ def build(rank, T, topo):
     sch = OPT["sch"]
     for j, c in enumerate(sch):
         dup(OPT["hdup"][j], R("vd", *c), R("h0", *c))
+    state["boost"] = 40.0
     act(R("hi"), R("pari"), ID)
     rows_from(R("pari"), "a")
-    for c in C3:
-        x = off("pb", c, c[0])
-        mm(x, diag("msel", "pw", c[0] // 16, c[1] // 16))
-        cp(off("l1", c), x)
-        cp(off("pv", c), x)
-    cp(R("l32", 0, 8), R("l1", 0, 8))
+    state["boost"] = 0.0
+    cp(R("t1"), G(R("pari"), R("f1")))
+    tr(R("t2"), R("t1"))
+    cp(R("l1"), G(R("t2"), R("f2")))
+    dup("g", R("pv"), R("l1"))
+    cp(R("l16", 0, 8), R("l1", 0, 8))
+    mark_anchors("zd", 16.0 * LL)
 
+    lists = ["l1", "l2", "l4", "l8", "l16"]
+    wins = ["pw", "j2", "j4", "j8", "j16"]
+    marks = [dup("g", R(name, 0, A), R("pw", 0, A)) for name in wins[1:]] + [mark_anchors("va", 4.0), mark_anchors("vb", 16.0)]
+    state["lazy"] = False
+    head = {"lag": OPT["head"]}
     if gets:
-        send([rank - 1], R("upn"), R("upi"), "aup", None)
-        send([rank - 1], R("ann"), R("an"), "aan", None)
+        send([rank - 1], R("upn"), R("upi"), "aup", head, OPT["first"])["after"] = marks
+        send([rank - 1], R("ann"), R("an"), "aan", head)["after"] = marks
+        arrive(0, R("a0"), "aa0", [], 20.0)
+    else:
+        send(later, R("a0"), R("an"), "aa0", head, OPT["first"])["after"] = marks
     if sends:
-        arrive(rank + 1, R("upn"), "aup", [], 12.0)
-        arrive(rank + 1, R("ann"), "aan", [], 13.0)
+        arrive(rank + 1, R("upn"), "aup", [], 16.0)
+        arrive(rank + 1, R("ann"), "aan", [], 17.0)
         cp(R("lh", 0, 8), R("upn"))
-
-    lists = ["l1", "l2", "l4", "l8", "l16", "l32"]
-    wins = ["pw", "j2", "j4", "j8", "j16", "j32"]
-
-    def pointers(r, c, after):
-        for b in banks(c) if r == 4 and OPT["fine"] else [c]:
-            act(R(wins[r + 1], *b), G(R(wins[r]), off(lists[r], b)), ID)["after"] = after
-        x = spare(c[0] // 16, c[1] // 16)
-        mm(x, diag("msel", wins[r + 1], x["c0"], x["c1"]))
-        cp(off(lists[r + 1], c), x)
+    a0 = "a0" if gets else "an"
+    act(R("y0", A, 2 * A), R(a0, A, 2 * A), ID, bias=float(LL))
+    tt(R("y0", 0, A), R("y0", A, 2 * A), R(a0, 0, A), MUL)
 
     own = OPT["zch"]
     edge = own[-1][1]
-    state["lazy"] = False
     for e in range(EP):
         first = e == 0
-        tail = {}
+        tail = {"lag": OPT["arrive"] + OPT["compose"] + (0.0 if gets else OPT["lead"])}
         if not first:
             for c in C3N:
                 act(R("xp", *c), G(R("xd"), off("l1", c)), ID)
                 tt(R("qd", *c), G(R("hs"), off("l1", c)), R("d0", *c), MUL)
         vw = "h0" if first else "gs"
         for r in range(5):
-            if first and r < 4:
-                dup("g", R(wins[r + 1], 0, A), R("pw", 0, A))
-            for c in C3N if r < 4 else C3N[:OPT["early32"]]:
-                pointers(r, c, [])
+            for c in C3N if r < 4 else []:
+                act(R(wins[r + 1], *c), G(R(wins[r]), off(lists[r], c)), ID)
+                x = spare(c[0] // 16, c[1] // 16)
+                mm(x, diag("msel", wins[r + 1], x["c0"], x["c1"]))
+                cp(off(lists[r + 1], c), x)
             vn = "va" if r % 2 == 0 else "vb"
-            mark_anchors(vn, 2.0 ** (2 ** (r + 1)))
+            if first != (r < 2):
+                mark_anchors(vn, 2.0 ** (2 ** (r + 1)) if first else 1.0)
             for j, c in enumerate(sch if r < 4 else OPT["slast"]):
                 o = tt(R(vn, *c), G(R(vw), off(lists[r], c)), R("vd", *c), MUL)
                 if r < 4:
                     dup(OPT["vdup"][j], R("vd", *c), R(vn, *c))
-                if first and r == 0:
+                if first and r == OPT["bload"]:
                     dma("s", R("b0", *c), T.bt[:, c[0]:c[1]], 190000, after=[o])
                 if first and r == 2 and j in (0, 2):
                     n = (NW * j // 2, NW * j // 2 + NW)
                     dma("s", R("nbi", *n), T.nb[:, n[0]:n[1]], 98304, after=[o])
-                    cp(R("ln", *n), R("nbi", *n))
+                    dup("g", R("ln", *n), R("nbi", *n))
                 if first and r == 4:
                     dma("s", R("d0", *c), T.dr[:, c[0]:c[1]], 190000, after=[o])
             vw = vn
-        smark = o
+            if r == 1:
+                head.setdefault("op", o)
         state["boost"] = OPT["pboost"]
-        for c in C6N:
-            if first:
-                mm(R("pb", *c), [(R("idp"), R("b0", *c)), (R("idk"), R("h0", *c))])
-            else:
-                mm(R("pb", *c), [(R("idp"), R("qd", *c)), (R("idp"), R("xd", *c)), (R("idn"), R("xp", *c)), (R("idb"), R("gs", *c))])
-            act(R("zb", *c), R("pb", *c), ABS, bias=-KK if first else 0.0)
-            mm(R("pb", *c), [(R("idf"), R("zb", *c))], True, False)
+        terms = (("idp", "b0"), ("idc", "h0")) if first else (("idp", "qd"), ("idp", "xd"), ("idn", "xp"), ("idb", "gs"))
+        for c in OPT["pch"]:
+            for b in banks(c):
+                mm(R("pb", *b), [(R(m), R(name, *b)) for m, name in terms])
+            act(R("pp", *c), R("pb", *c), ABS)
+            for b in banks(c):
+                mm(R("pb", *b), [(R("idh"), R("pp", *b))] + ([(R("idk"), R("h0", *b))] if first else []), True, False)
         state["boost"] = 0.0
         mark_anchors("za", float(LL))
-        for j, c in enumerate(C6N):
-            if OPT["clip"][j] == "v":
-                ts(R("hm", *c), R("va", *c), 1.0, ALU.min, -1.0, ALU.max)
-            else:
-                act(R("hm", *c), R("va", *c), SIGN)
-            mm(R("pb", *c), [(R("idl"), R("hm", *c))], False, True)
-            zmark = act(R("za", *c), R("pb", *c), ABS)
+        for j, c in enumerate(OPT["slast"]):
+            ts(R("hm", *c), R("va", *c), 0.0, ALU.is_gt, 0.5, SUB)["boost"] = OPT["kboost"]
+            for b in banks(c):
+                mm(R("pb", *b), [(R("idl"), R("hm", *b))], False, True)
+            act(R("za", *c), R("pb", *c), ABS, bias=(KK if first else 0.0) - 512.0)
             if c[0] < edge:
                 dup(OPT["z0dup"][j], R("zd", c[0], min(c[1], edge)), R("za", c[0], min(c[1], edge)))
         dma("s", row("pw", 2), row("va", 2), 49152)
-        mh = R("msg", MS * e, MS * e + A)
         if sends:
             state["boost"] = OPT["hboost"]
             act(R("sj", 0, A), G(R("j8"), R("lh", 0, 8)), ID)
@@ -348,53 +369,52 @@ def build(rank, T, topo):
             mm(x, diag("msel", "sk", 0, 16))
             cp(R("lh", 24, 32), R(x["n"], 0, 8))
             act(R("msg", MS * e + A, MS * e + A + 8), R(x["n"], 8, 16), ID)
+            if OPT["sround"] == 1:
+                act(R("sl"), G(R("j4"), R("lh", 0, 32)), ID)
+                y = spare(0, 32)
+                mm(y, diag("msel", "sl", 0, 32))
+                cp(R("lh", 32, 64), y)
             act(R("hu"), G(R("va"), R("lh", 0, 8)), SIGN)
-            tt(R("ez"), R("hu"), R("ann", A, 2 * A) if first else R("qq"), MUL)
-            if rank == 0:
-                cp(R("pu", 0, 8), R(x["n"], 8, 16))
-                act(R("au"), G(R("an", A, 2 * A), R("pu", 0, 8)), ID)
-            if rank == 0 and first:
-                act(R("cu"), G(R("an", 0, A), R("pu", 0, 8)), ID)
-                tt(R("qq"), R("cu"), R("hu"), MUL)
-                tt(mh, R("qq"), R("ann", 0, A), MUL)
-            elif first:
+            tt(R("ez", 0, A), R("hu"), R("ann", A, 2 * A) if first else R("qq"), MUL)
+            mh = R("hu")
+            if first:
+                mh = R("cu")
                 tt(mh, R("hu"), R("ann", 0, A), MUL)
-            else:
-                act(mh, R("hu"), ID)
-            s = MS * (5 * e + rank)
-            send(later, R("lsg", s, s + MS), R("msg", MS * e, MS * e + MS), "as%d_%d" % (e, rank), tail)
+            act(R("mo"), mh, ID, bias=256.0, scale=256.0)
             state["boost"] = 0.0
-        for c in C3N[OPT["early32"]:]:
-            pointers(4, c, [zmark])
-        for c in C3N:
+        state["lazy"], state["boost"] = False, OPT["nboost"]
+        for c in OPT["nch"]:
             x = spare(c[0] // 16, c[1] // 16)
             mm(x, diag("mdep", "va", x["c0"], x["c1"]))
             act(off("dv", c), x, ABS)
         for k in range(2):
             nk, qk = "n%d" % k, "q%d" % k
-            for j, c in enumerate(C3N):
+            for c in OPT["ngather"]:
+                act(R(nk, *c), G(R("pw"), off("ln", c, NW * k)), ID)
+            for c in OPT["nch"]:
                 m0, m1 = c[0] // 16, c[1] // 16
-                for b in banks(c) if OPT["fine"] else [c]:
-                    fetch(OPT["nk"][k][j], R(nk, *b), G(R("pw"), off("ln", b, NW * k)))
                 x = spare(m0, m1)
                 mm(x, diag("msel", nk, m0, m1))
                 cp(off("lc%d" % k, c), x)
-                tt(off("e%d" % k, c), x, off("pv", c), SUB)
+                act(off("e%d" % k, c), x, ID)
                 x = spare(m0, m1)
                 mm(x, diag("mdep", nk, m0, m1))
                 act(off(qk, c), x, ABS)
             x = spare(8, NW)
             mm(x, [(R("idn"), R(qk, 8, NW)), (R("idp"), R("dv", 8, NW))])
             act(R("pen%d" % k, 8, NW), x, AF.Relu, scale=PEN)
+        s0 = R("ex0", 256 + 8, 256 + NW)
+        mm(s0, [(R("idf"), R("e0", 8, NW)), (R("idg"), R("pv", 8, NW))])
+        state["lazy"], state["boost"] = False, 0.0
         if first:
             state["boost"] = OPT["gboost"]
             for c in C3N:
-                act(R("gs", *c), R("d0", *c), SIGN, bias=127.5, scale=-1.0)
+                ts(R("gs", *c), R("d0", *c), 128.0, ALU.is_lt, 0.5, SUB)
                 dup(OPT["gdup"], R("vd", *c), R("gs", *c))
             state["boost"] = 0.0
         zw = "za"
         mark = None
-        for r in range(5):
+        for r in range(4):
             zn = "zb" if r % 2 == 0 else "za"
             mark_anchors(zn, float(LL * 2 ** (r + 1)))
             state["boost"] = OPT["sboost"]
@@ -407,51 +427,59 @@ def build(rank, T, topo):
             state["boost"] = 0.0
             for j, c in enumerate(own):
                 o = tt(R(zn, *c), G(R(zw), off(lists[r], c)), R("zd", *c), ADD)
-                if r < 4:
-                    dup(OPT["zdup"][r][j], R("zd", *c), R(zn, *c))
+                dup(OPT["zdup"][r][j], R("zd", *c), R(zn, *c))
             zw = zn
-            if r == 2:
+            if r == OPT["sround"]:
                 mark = o
                 if sends:
                     state["boost"] = OPT["mboost"]
-                    act(R("zq"), G(R(zw), R("lh")), ID)
                     x = R("pb", 0, A)
-                    mm(x, [(R("idp"), R("ez"))] + ([(R("idp"), R("au"))] if rank == 0 and not first else [])
-                       + [(R("idf"), R("zq", A * k, A * k + A)) for k in range(4)])
-                    if rank == 0 and first:
-                        tt(R("ze"), x, R("cu"), MUL)
-                        tt(R("yi"), R("ze"), R("au"), ADD)
-                    else:
-                        cp(R("yi"), x)
+                    for k in (2, 3):
+                        act(R("zq", 256 * k, 256 * k + 256), G(R(zw), R("lh", 16 * k, 16 * k + 16)), ID)
+                        mm(x, [(R("idf"), R("zq", A * i, A * i + A)) for i in (2 * k, 2 * k + 1)], k == 2, False)
+                    tt(R("zq", 0, 256), G(R(zw), R("lh", 0, 16)), R("ez"), ADD)
+                    tt(R("zq", 256, 512), G(R(zw), R("lh", 16, 32)), R("zq", 0, 256), ADD)
+                    mm(x, [(R("idf"), R("zq", A * i, A * i + A)) for i in (2, 3)], False, True)
+                    tt(R("yi"), x, mh, MUL)
                     ts(R("yi"), R("yi"), 255, ALU.bitwise_and)
-                    mz = R("mz", A * e, A * e + A)
-                    act(mz, R("yi"), ID)
-                    s = A * (5 * e + rank)
-                    send(later, R("lz", s, s + A), mz, "am%d_%d" % (e, rank), tail)
+                    tt(R("msg", MS * e, MS * e + A), R("yi"), R("mo"), ADD)
+                    s = MS * (5 * e + rank)
+                    mark = send(later, R("lsg", s, s + MS), R("msg", MS * e, MS * e + MS), "am%d_%d" % (e, rank), tail)
                     state["boost"] = 0.0
         if gets:
             for f in range(rank):
-                s = 5 * e + f
-                arrive(f, R("lsg", MS * s, MS * s + MS), "as%d_%d" % (e, f), [smark], 14.0)
-                arrive(f, R("lz", A * s, A * s + A), "am%d_%d" % (e, f), [mark], OPT["arrive"])
+                s = MS * (5 * e + f)
+                arrive(f, R("lsg", s, s + MS), "am%d_%d" % (e, f), [mark], OPT["arrive"] + (0.0 if sends else 2.8))
+            yw = R("y0", A * e, A * e + A)
             for f in range(rank):
-                s = 5 * e + f
-                u, y = R("uu", A * f, A * f + A), R("zz", A * f, A * f + A)
-                if f == 0:
-                    act(u, R("lz", A * s, A * s + A), ID, bias=float(LL))
-                else:
-                    cp(R("lp", 8 * f, 8 * f + 8), R("lsg", MS * s + A, MS * s + A + 8))
-                    tt(u, G(yw, R("lp", 8 * f, 8 * f + 8)), R("lz", A * s, A * s + A), ADD)
-                tt(y, u, R("lsg", MS * s, MS * s + A), MUL)
+                s = MS * (5 * e + f)
+                u, y = R("uu", A * f, A * f + A), R("zz", A * f, A * f + A) if f < rank - 1 else R("zb", 0, A)
+                act(R("ms", A * f, A * f + A), R("lsg", s, s + A), SIGN, bias=-384.0)
+                dup(OPT["lp"], R("lp", 8 * f, 8 * f + 8), R("lsg", s + A, s + A + 8))
+                tt(u, G(yw, R("lp", 8 * f, 8 * f + 8)), R("ms", A * f, A * f + A), MUL)
+                tt(y, u, R("lsg", s, s + A), ADD)
                 yw = y
         else:
-            yw = R("zz", A * e, A * e + A)
-            act(R("y0"), R("an", A, 2 * A), ID, bias=float(LL))
-            tt(yw, R("y0"), R("an", 0, A) if first else R("ones"), MUL)
-        for j, c in enumerate(C6):
-            o = tt(R("za", *c), G(yw, off("l32", c)), R("zb", *c), ADD)
+            act(R("zb", 0, A), R("y0", A * e, A * e + A), ID)
+        for c, how in OPT["upper"]:
+            if how == "v":
+                o = tt(R("zc", *c), G(R("zb"), off("l16", c)), R("zd", *c), ADD)
+            else:
+                o = act(R("zd", *c), G(R("zb"), off("l16", c)), ID)
+                mm(R("pb", *c), [(R("idf"), R("za", *c))], True, False)
+                mm(R("pb", *c), [(R("idf"), R("zd", *c))], False, True)
+                act(R("zc", *c), R("pb", *c), ID)
             tail.setdefault("op", o)
-            act(R("ui", *c), R("za", *c), ABS, bias=(KK if first else 0.0) - 32.0 * LL)
+        for j, (c, how) in enumerate(OPT["final"]):
+            if how == "v":
+                x = R("zb", *c)
+                tt(x, G(R("zc"), off("l16", c)), R("zd", *c), ADD)
+            else:
+                x = R("pb", *c)
+                act(R("zd", *c), G(R("zc"), off("l16", c)), ID)
+                mm(x, [(R("idf"), R("za", *c))], True, False)
+                mm(x, [(R("idf"), R("zd", *c))], False, True)
+            act(R("ui", *c), x, ABS, bias=(KK if first else 0.0) - 32.0 * LL)["boost"] = OPT["uboost"]
             ts(R("xi", *c), R("ui", *c), 255, ALU.bitwise_and)["boost"] = OPT["aboost"]
             dup(OPT["xcv"][j], R("xd", *c), R("xi", *c))
         if first:
@@ -464,12 +492,13 @@ def build(rank, T, topo):
                 dma("s", T.yx[:, c[0]:c[1]], R("xd", *c), 262144)
         sums = {}
         for k, (name, l, pos) in enumerate((("da", "l1", "n0"), ("db", "lc0", "n1"), ("dc", "lc1", "hm"))):
-            for j, c in enumerate(C3N):
+            for j, c in enumerate(OPT["vch"]):
                 how = OPT["votes"][k][j]
+                state["boost"] = OPT["vboost"][k]
                 m0, m1 = c[0] // 16, c[1] // 16
                 sums[k, j] = diag("msum", name, m0, m1)
                 if how == "a":
-                    act(R(name, *c), G(R("xd"), off(l, c)), ID)
+                    act(R(name, *c), G(R("xi"), off(l, c)), ID)
                     for b in banks(c):
                         mm(R("pb", *b), [(R("idp"), R(name, *b)), (R("idn"), R("xd", *b))])
                     act(R(name, *c), R("pb", *c), ABS)
@@ -480,23 +509,28 @@ def build(rank, T, topo):
                 else:
                     ts(R(pos, *c), R(name, *c), 0.0, ALU.max)
                     sums[k, j] = diag("mneg", name, m0, m1) + diag("mtwo", pos, m0, m1)
-        for j, c in enumerate(C3N):
+        state["boost"] = 0.0
+        for j, c in enumerate(OPT["vch"]):
             x = off("pb", c)
-            mm(x, sums[0, j])
+            o = mm(x, sums[0, j])
             act(off("dp", c), x, ID)
         for k in range(2):
-            for j, c in enumerate(C3N):
-                mm(off("ex%d" % k, c), [(R("idp"), off("pen%d" % k, c))] + sums[k + 1, j])
+            for j, c in enumerate(OPT["vch"]):
+                last = mm(off("ex%d" % k, c), [(R("idp"), off("pen%d" % k, c))] + sums[k + 1, j])
+                if (k, j) in OPT["hold"]:
+                    last["after"] = [o]
+            o = last
         n = (8, NW)
-        ta, tb = R("ex0", 256 + 8, 256 + NW), R("ex1", 256 + 8, 256 + NW)
+        s1, cc, w1 = (R("pb", 512 * k + 8, 512 * k + NW) for k in (1, 2, 3))
+        mm(s1, [(R("idf"), R("e1", *n)), (R("idg"), R("pv", *n))])["lazy"] = True
         tt(R("w1c", *n), R("ex0", *n), R("dp", *n), ALU.is_lt)
+        tt(R("cc", *n), s0, R("w1c", *n), MUL)
         tt(R("mn", *n), R("ex0", *n), R("dp", *n), ALU.min)
-        tt(ta, R("w1c", *n), R("e0", *n), MUL)
-        tt(R("cc", *n), ta, R("pv", *n), ADD)
-        tt(ta, ta, R("e1", *n), SUB)
-        tt(R("w1c", *n), R("ex1", *n), R("mn", *n), ALU.is_lt)
-        tt(tb, ta, R("w1c", *n), MUL)
-        tt(R("pv", *n), R("cc", *n), tb, SUB)
+        mm(cc, [(R("idf"), R("pv", *n)), (R("idf"), R("cc", *n))])
+        tt(R("e1", *n), s1, R("cc", *n), SUB)
+        tt(w1, R("ex1", *n), R("mn", *n), ALU.is_lt)
+        tt(R("e0", *n), w1, R("e1", *n), MUL)
+        tt(R("pv", *n), cc, R("e0", *n), ADD)
         if first:
             cp(R("l1", *n), R("pv", *n))
         act(R("t1"), G(R("pv"), R("f3")), ID)
@@ -532,45 +566,116 @@ def schedule(ops):
         o["pre"] = pre
         for r, w in acc:
             seen.setdefault(r["n"], []).append((r, w, o))
-    hop = OPT["hop"]
-    nxt = [[] for _ in ops]
-    for o in ops:
-        for p in o["pre"]:
-            nxt[p].append(o["id"])
+    real = len(ops)
+    rest = [0.0] * real
     for o in reversed(ops):
-        tail = 0.0
         if o["kind"] == "s":
-            tail = 250.0 if o["tail"] is None else OPT["urgent"] + o["tail"]["op"]["prio"]
-        o["prio"] = o["bonus"] + o["dur"] + o["lat"] + max([tail] + [hop + ops[k]["prio"] for k in nxt[o["id"]]])
-    left = [len(o["pre"]) for o in ops]
-    ready = [o["id"] for o in ops if not o["pre"]]
-    free = {}
-    order = []
-    while ready:
-        for k in ready:
-            o = ops[k]
-            o["est"] = max([free.get(o["eng"], 0.0)] + [ops[p]["end"] + hop for p in o["pre"]])
-        t0 = min(ops[k]["est"] for k in ready)
-        eng = [ops[k]["eng"] for k in ready if ops[k]["est"] == t0][0]
-        cand = [ops[k] for k in ready if ops[k]["eng"] == eng and ops[k]["est"] <= t0 + OPT["slack"]]
-        best = max(cand, key=lambda o: (not o["lazy"] and o["dur"] < OPT["small"], o["prio"] + o["boost"], -o["id"]))
-        soon = [ops[k] for k in ready if ops[k]["eng"] == eng and ops[k]["est"] < best["est"] + OPT["look"] * best["dur"]
-                and ops[k]["prio"] + ops[k]["boost"] > best["prio"] + best["boost"] + OPT["gap"]]
-        if soon:
-            best = max(soon, key=lambda o: o["prio"] + o["boost"])
-        if eng != "x":
-            free[eng] = best["est"] + best["dur"]
-        best["end"] = best["est"] + best["dur"] + best["lat"]
-        if best["kind"] == "d":
-            best["end"] = max(best["end"], free.get("dma", 0.0) + best["xfer"])
-            free["dma"] = best["end"]
-        order.append(best)
-        ready.remove(best["id"])
-        for k in nxt[best["id"]]:
-            left[k] -= 1
-            if left[k] == 0:
-                ready.append(k)
-    return order
+            rest[o["id"]] = max(rest[o["id"]], o["tail"]["lag"] + rest[o["tail"]["op"]["id"]])
+        rest[o["id"]] += o["dur"] + o["lat"]
+        for p in o["pre"]:
+            rest[p] = max(rest[p], rest[o["id"]] + OPT["hop"])
+    ops = ops + [{"eng": "x", "kind": "r", "pre": [o["id"]], "dur": 0.0, "lat": OPT["stretch"] * rest[o["id"]],
+                  "bonus": 0.0, "boost": 0.0, "lazy": True} for o in ops if o["kind"] == "s"]
+    n = len(ops)
+    span = [o["dur"] + o["lat"] for o in ops]
+    back = [[(p, 0.0 if ops[p]["eng"] == o["eng"] == "t" else OPT["hop"]) for p in o["pre"]] for o in ops]
+    forth = [[] for _ in ops]
+    for k in range(n):
+        for p, lag in back[k]:
+            forth[p].append((k, lag))
+    holds = []
+    for o in ops:
+        h = [] if o["eng"] == "x" else [(o["eng"], 0.0, o["dur"])]
+        if o["kind"] == "d":
+            h.append(("dma", o["dur"] + 0.6 * OPT["dl"], o["xfer"]))
+        holds.append(h)
+
+    def seek(b, t):
+        lo, hi = 0, len(b)
+        while lo < hi:
+            mid = (lo + hi) // 2
+            if b[mid][1] <= t + 1e-9:
+                lo = mid + 1
+            else:
+                hi = mid
+        return lo
+
+    def place(key, before, after, mirror):
+        left = [len(x) for x in before]
+        ready = [k for k in range(n) if not left[k]]
+        busy, start = {}, [0.0] * n
+        while ready:
+            k = min(ready, key=lambda k: (key[k], k))
+            ready.remove(k)
+            t = max([0.0] + [start[p] + span[p] + lag for p, lag in before[k]])
+            hs = [(q, span[k] - a - d if mirror else a, d) for q, a, d in holds[k]]
+            moved = True
+            while moved:
+                moved = False
+                for q, a, d in hs:
+                    b = busy.setdefault(q, [])
+                    i = seek(b, t + a)
+                    while i < len(b) and b[i][0] < t + a + d - 1e-9:
+                        t, moved = b[i][1] - a, len(hs) > 1
+                        i += 1
+            for q, a, d in hs:
+                busy[q].insert(seek(busy[q], t + a), (t + a, t + a + d))
+            start[k] = t
+            for m, lag in after[k]:
+                left[m] -= 1
+                if not left[m]:
+                    ready.append(m)
+        return start, max(start[k] + span[k] for k in range(n))
+
+    prio = [0.0] * n
+    for k in reversed(range(n)):
+        prio[k] = ops[k]["bonus"] + span[k] + max([0.0] + [lag + prio[m] for m, lag in forth[k]])
+    rank = [prio[k] + ops[k]["boost"] for k in range(n)]
+
+    def first_order(slack, small, look, gap):
+        left = [len(x) for x in back]
+        ready = [k for k in range(n) if not left[k]]
+        free, key, est = {}, [0.0] * n, [0.0] * n
+        while ready:
+            for k in ready:
+                est[k] = max([free.get(ops[k]["eng"], 0.0)] + [key[p] + span[p] + lag for p, lag in back[k]])
+            k0 = min(ready, key=lambda k: est[k])
+            mine = [k for k in ready if ops[k]["eng"] == ops[k0]["eng"]]
+            k = max([k for k in mine if est[k] <= est[k0] + slack], key=lambda k: (not ops[k]["lazy"] and ops[k]["dur"] < small, rank[k], -k))
+            soon = [m for m in mine if est[m] < est[k] + look * ops[k]["dur"] and rank[m] > rank[k] + gap]
+            if soon:
+                k = max(soon, key=lambda m: rank[m])
+            if ops[k]["kind"] == "d":
+                est[k] = max(est[k], free.get("dma", 0.0) - holds[k][1][1])
+                free["dma"] = est[k] + holds[k][1][1] + holds[k][1][2]
+            if ops[k]["eng"] != "x":
+                free[ops[k]["eng"]] = est[k] + ops[k]["dur"]
+            key[k] = est[k]
+            ready.remove(k)
+            for m, lag in forth[k]:
+                left[m] -= 1
+                if not left[m]:
+                    ready.append(m)
+        return key
+
+    writes = [ops[ops[k]["pre"][0]] for k in range(real, n)]
+    best = None
+    for rule in OPT["rules"]:
+        key = first_order(*rule)
+        end = max(key[k] + span[k] for k in range(real))
+        for k, o in enumerate(writes):
+            span[real + k] = end - key[o["tail"]["op"]["id"]] + o["tail"]["lag"]
+        for i in range(OPT["passes"]):
+            start, end = place(key, back, forth, False)
+            end = max(start[k] + span[k] for k in range(real)) + sum(
+                max(0.0, start[o["id"]] + o["tail"]["lag"] - start[o["tail"]["op"]["id"]]) for o in writes)
+            if best is None or end < best[1]:
+                best = (start, end)
+            late, end = place([-start[k] - span[k] for k in range(n)], forth, back, True)
+            key = [end - late[k] - span[k] if not ops[k]["lazy"] else min(start[k], end - late[k] - span[k]) for k in range(n)]
+    for o in ops[:real]:
+        o["est"], o["end"] = best[0][o["id"]], best[0][o["id"]] + span[o["id"]]
+    return sorted(ops[:real], key=lambda o: (o["est"], o["id"]))
 
 
 def rank_program(g, core, T, topo):
@@ -595,21 +700,22 @@ def rank_program(g, core, T, topo):
             continue
         total[o["sig"][0]] = o["sig"][1]
     waited = {}
+    known = {q: {} for q in "vatgs"}
     for o in order:
         if o["kind"] == "r":
+            o["knows"] = {}
             continue
-        q = queue[o["eng"]]
-        need = {}
-        for p in o["pre"]:
-            p = ops[p]
+        q, mine = queue[o["eng"]], known[o["eng"]]
+        for p in sorted((ops[p] for p in o["pre"]), key=lambda p: -p["est"]):
             if p["eng"] == "t" and o["eng"] == "t":
                 continue
             s, n = p["sig"]
-            need[s] = max(need.get(s, 0), n)
-        for s in sorted(need):
-            if waited.get((o["eng"], s), 0) < need[s]:
-                q.wait_ge(T.sem[s], need[s])
-                waited[(o["eng"], s)] = need[s]
+            if mine.get(s, 0) < n:
+                q.wait_ge(T.sem[s], n)
+                waited[(o["eng"], s)] = mine[s] = n
+                for s, n in p["knows"].items():
+                    mine[s] = max(mine.get(s, 0), n)
+        o["knows"] = dict(mine)
         ins = o["fn"](q)
         if o["kind"] == "c":
             ins.then_inc(T.sem[o["sig"][0]], 1)

@@ -3,64 +3,60 @@ from concourse.mybir import AluOpType as ALU, ActivationFunctionType as AF
 
 V, A, NR, EP = 3072, 128, 6, 2
 NW = V // 16
-KK = 16384.0
-LL = 65536
-PEN = 2.0 ** 45
+LT = 2048
+KK = 32768.0
+LL = 131072
+PEN = 4096.0
+ODD = 0x55555555
 MS = A + 16
 
 BF, F16, F32, I32, U16 = "bfloat16", "float16", "float32", "int32", "uint16"
 SCRATCH = {}
 for _d, _w, _names in (
-        (BF, V, "h0 d0 gs va vb vd pw j2 j4 j8 j16 n0 n1 da db dc xd hs hm"), (F32, V, "za zb zc zd"), (I32, V, "ui xi"),
-        (U16, NW, "l1 l2 l4 l8 l16 lc0 lc1"), (F32, NW, "pv e0 e1 w1c mn cc blk dp"), (BF, NW, "hi lo pen0 pen1 q0 q1 dv"),
-        (I32, NW, "pari"), (I32, 2 * NW, "nbi"), (U16, 2 * NW, "ln"), (F32, 2 * NW, "t1 t2"), (U16, 24, "f1 f3"), (U16, 12, "f2 f4"),
-        (I32, 16, "ci s2"), (F32, 16, "cf"), (F32, 48, "s1"), (F32, 80, "iw"), (BF, 144, "msel mdep msum mneg mtwo"),
-        (BF, A, "idp idn idk idb idc idl ones hu qq cu"), (F16, A, "idh"), (F16, V, "pp"), (BF, 256, "ez a0"), (F32, A, "idf idg"), (F32, 256, "y0"), (F32, 1024, "zq"), (F32, 512, "zg"), (BF, 512, "sl"),
-        (I32, 8, "upi upn"), (BF, 256, "an ann sj sk"), (U16, 64, "lh"), (I32, A, "yi"),
-        (F16, EP * MS, "msg"), (BF, A, "mo"), (F16, EP * 5 * MS, "lsg"), (BF, 5 * A, "ms"), (U16, 5 * 8, "lp"),
-        (F32, 5 * A, "uu zz")):
+        (BF, V, "h0 d0 gs va vd wx j2 j4 j8 j16 n0 n1 xd g0 hm"), (F16, V, "pp pg"), (F32, V, "za zb zc zd"), (I32, V, "ui xi"), (F32, 2048, "ze"),
+        (U16, NW, "l1 l2 l4 l8 l16 lc0 lc1"), (F32, NW, "e0 e1 w1c mn cc blk dp"), (BF, NW, "hi lo one2 pen0 pen1 dv"),
+        (I32, NW, "pari"), (I32, 2 * NW, "nbi wi"), (U16, 2 * NW, "ln"), (F32, 2 * NW, "t1 t2"), (BF, 2 * NW, "ce ch cw"),
+        (U16, 24, "f1"), (U16, 12, "f2"), (I32, 16, "ci s2"), (F32, 32, "cf"), (F32, 48, "s1 iw"),
+        (BF, 144, "msel msum mneg mtwo mx"), (BF, 1024, "mr"), (BF, 3 * NW, "q0 q1"), (BF, A, "idp idn idq idr idl ids idt ones nil cnt hu qq cu"),
+        (F16, A, "idh"), (BF, 256, "a0 an ann sj sk"), (F32, A, "idf"), (F32, 256, "y0"), (F32, 1024, "zg"), (F16, 1024, "zq"), (BF, 512, "sl"),
+        (I32, 8, "upi upn"), (U16, 64, "lh"), (I32, A, "yi"), (F16, EP * MS, "msg"), (F16, EP * 5 * MS, "lsg"), (BF, 5 * A, "ms"),
+        (U16, 5 * 8, "lp"), (F32, 5 * A, "uu zz")):
     for _n in _names.split():
         SCRATCH[_n] = ("sbuf", [128, _w], _d)
 SCRATCH.update({"pb": ("psum", [128, V], F32), "ex0": ("psum", [128, 512], F32), "ex1": ("psum", [128, 512], F32)})
-SHARED = {"qd": "n0", "xp": "n1", "b0": "da"}
+SHARED = {"qd": "n0", "xp": "n1", "b0": "n1", "da": "j16", "db": "j8", "dc": "j4", "hs": "h0"}
 NDMA = 120
 SEMAPHORES = (["qv", "qa", "qt", "qg", "sent", "aup", "aan", "aa0"] + ["dma%d" % i for i in range(NDMA)]
               + ["am%d_%d" % (e, r) for e in range(EP) for r in range(5)])
 
 C3 = [(0, 1024), (1024, 2048), (2048, 3072)]
 C3N = [(A, 1024), (1024, 2048), (2048, 3072)]
+C4N = [(A, 864), (864, 1600), (1600, 2336), (2336, V)]
 C6 = [(512 * i, 512 * i + 512) for i in range(6)]
-C6N = [(A, 512)] + C6[1:]
+PTR, HOST, REST = (0, 8), (4, 8), ((1, 2), (2, 4))
 OPT = {
-    "sch": [(A, 864), (864, 1600), (1600, 2336), (2336, 3072)], "hdup": "aaga", "vdup": "ssgs", "gdup": "s",
-    "share": [(2560, 3072)],
-    "zch": [(A, 768), (768, 1408), (1408, 1984), (1984, 2560)], "zdup": ("sgsg", "sgsg", "ssss", "sgsg"), "z0dup": "ssgsg", "early32": 1, "fine": True, "sboost": 3.0,
-    "slast": [(A, 1024), (1024, 2048), (2048, 2560), (2560, 3072)],
-    "votes": ("aaa", "vvv", "mmm"),
-    "nk": ("aaa", "aaa"), "xcv": "gagaga", "final": "vavvav", "sround": 1, "kboost": 3.0,
-    "cyc": 0.87e-3, "gc": 1.56, "pe": 0.44e-3, "bw": 3.0e5, "hop": 0.1, "fix": 0.06, "dl": 2.2,
-    "arrive": 8.0, "urgent": 10.0, "slack": 0.15, "small": 0.2, "look": 0.6, "gap": 2.0, "aboost": 6.0, "pboost": 0.0, "cboost": 30.0, "hboost": 15.0, "mboost": 10.0, "gboost": 0.0,
+    "sch": C4N, "slast": [(A, 1024)] + C6[2:], "jch": [(A, 1600), (1600, V)], "lcp": "aaaaaaaa", "hdup": "vaaa", "vdup": ["aaaa"] + ["ssss"] * 7,
+    "pch": C3N, "xpr": "vaa", "qdr": "vva",
+    "share": [(2688, V)], "zch": [(A, 800), (800, 1440), (1440, 2080), (2080, 2688)], "zdup": ("gssg", "gsgs", "gssg"), "z0dup": "gsgsg",
+    "upper": [((0, 896), "v"), ((896, 1792), "v"), ((1792, 2560), "v"), (C6[5], "a")],
+    "final": [((0, 768), "v"), ((768, 1536), "v"), (C6[3], "a"), (C6[4], "a"), (C6[5], "a")], "shift": 1536, "xcv": "gggggg", "zer": "a",
+    "nch": [(A, 1600), (1600, V)], "ngather": [(0, 768), (768, 1536), (1536, 2304), (2304, V)], "lcr": "a", "wrap": "av", "dload": 3, "nload": 3,
+    "zqv": 512,
+    "votes": ([((A, 1152), "a"), ((1152, 2112), "a"), ((2112, V), "a")], [((A, 1152), "m"), ((1152, 2112), "v"), ((2112, V), "m")],
+              [((A, 1152), "m"), ((1152, 2112), "v"), ((2112, 2688), "v"), ((2688, V), "v")]),
+    "cyc": 0.83e-3, "gc": 1.5, "pe": 0.45e-3, "bw": 3.0e5, "hop": 0.12, "fix": 0.05, "dl": 1.9, "gdma": 0.5, "arrive": 5.5, "compose": 3.5,
+    "first": 3.0, "head": 0, "lead": 2, "aboost": 6, "cboost": 3, "hboost": 4, "mboost": 10, "kboost": 10, "uboost": 4,
+    "sets": [(1.12, 0.09, 1.8, 3.0e5, 0.0), (1.5, 0.10, 1.9, 3.0e5, 0.0), (1.9, 0.08, 1.6, 3.3e5, -0.5)],
+    "seed": (4, 1, 4, 4, 1, 2), "look": 0.4, "steps": 250, "by": 0.1, "warm": 0.2, "tries": 3000, "turn": 7, "pull": 0.3, "ends": 14, "peek": 40, "far": 6,
+    "keep": 15, "last": 900, "wide": 150,
 }
-OPT.update(pboost=0, gboost=0, arrive=7, fine=True, sboost=0, hdup="avav", final="vvavaa", upper="vvvvaa", xcv="gggggg", compose=2.0, sarr=5.0,
-           cyc=0.83e-3, pe=0.42e-3, fix=0.05, hop=0.07, dl=1.7, bw=3.5e5, passes=2, shake=0.5, small=0.3, hboost=12, cboost=30, mboost=10,
-           aboost=6, kboost=3, uboost=4, lead=4.0, stretch=1.3, mix=0.0)
-OPT.update(compose=5.0, shake=0.0, small=0.4, pch=C6N, vch=C3N, z0dup="sgsg", slast=[(A, 1024)] + C6[2:], arrive=6.0, lp="g", head=12.0, vboost=(0.0, 0.0, 0.0), nboost=2.0, hold=((0, 2), (1, 0)), bload=1, zdup=("sgsg", "sgsg", "ssss", "ssss"), cboost=3, hop=0.1, rules=[(s, m, l, 2.0) for s in (0.08, 0.2) for m in (0.25, 0.45) for l in (0.3, 0.6)], first=3.0, vdup="ssss", pe=0.47e-3,
-           nch=[(A, 1600), (1600, V)], ngather=[(A, 864), (864, 1600), (1600, 2336), (2336, V)], hdup="aava",
-           upper=[((0, 1024), "v"), ((1024, 2048), "v"), (C6[4], "a"), (C6[5], "a")],
-           final=[((0, 768), "v"), ((768, 1536), "v"), (C6[3], "a"), (C6[4], "a"), (C6[5], "a")])
-OPT.update(nboost=0, arrive=5.5, head=0, lead=2, compose=3.5, gc=1.7, votes=("aaa", "vvm", "mmm"), hop=0.13, pch=C3N,
-           rules=[(0.08, 0.25, 0.3, 2.0), (0.2, 0.45, 0.6, 2.0), (0.15, 0.4, 0.6, 2.0), (0.08, 0.45, 0.6, 2.0)])
 
 
-def R(name, c0=None, c1=None, step=1, rows=None, lane=None):
+def R(name, c0=None, c1=None, step=1, rows=None):
     name = SHARED.get(name, name)
     if c0 is None:
         c0, c1 = 0, SCRATCH[name][1][1]
-    return {"n": name, "c0": c0, "c1": c1, "st": step, "rows": rows, "lane": lane}
-
-
-def row(name, i):
-    return R(name, rows=slice(i, 128, 16), lane=i)
+    return {"n": name, "c0": c0, "c1": c1, "st": step, "rows": rows}
 
 
 def G(win, off):
@@ -70,7 +66,7 @@ def G(win, off):
 def ap(T, r):
     if "win" in r:
         return ap(T, r["win"]).indirect(ap(T, r["off"]))
-    rows = slice(None) if r["rows"] is None else r["rows"]
+    rows = slice(None) if r["rows"] is None else slice(r["rows"][0], 128, r["rows"][1])
     if r["st"] == 1:
         return T[r["n"]][rows, r["c0"]:r["c1"]]
     return T[r["n"]][rows, r["c0"]:r["c1"]:r["st"]]
@@ -106,20 +102,27 @@ def banks(c):
 
 def build(rank, T, topo):
     ops = []
-    state = {"dma": 0, "ex": 0, "pb": 0, "lazy": True, "boost": 0.0}
+    state = {"dma": 0, "ex": 0, "boost": 0.0}
     CYC, GC, PEC, BW = OPT["cyc"], OPT["gc"], OPT["pe"], OPT["bw"]
-    ID, ABS, SIGN = AF.Identity, AF.Abs, AF.Sign
-    ADD, SUB, MUL = ALU.add, ALU.subtract, ALU.mult
+    ID, ABS, SIGN, RELU = AF.Identity, AF.Abs, AF.Sign, AF.Relu
+    ADD, SUB, MUL, EQ, AND = ALU.add, ALU.subtract, ALU.mult, ALU.is_equal, ALU.bitwise_and
 
     def val(x):
         return ap(T, x) if isinstance(x, dict) else x
 
     def add(eng, fn, rd, wr, dur, **kw):
-        o = {"eng": eng, "fn": fn, "rd": regs(rd), "wr": regs(wr), "dur": dur, "lat": 0.0, "kind": "c", "after": [], "bonus": 0.0,
-             "id": len(ops), "lazy": state["lazy"], "boost": state["boost"]}
+        o = {"eng": eng, "fn": fn, "rd": regs(rd), "wr": regs(wr), "dur": dur, "lat": 0.0, "kind": "c", "after": [], "behind": [], "queue": [],
+             "bonus": 0.0, "id": len(ops), "boost": state["boost"], "ng": 0, "mile": False}
         o.update(kw)
+        if any(isinstance(r, dict) and "win" in r for r in rd):
+            o["ng"] = width(wr[0])
         ops.append(o)
         return o
+
+    def follow(a, b):
+        if a:
+            b["queue"].append(a["id"])
+        return b
 
     def vdur(n, c):
         return OPT["fix"] + max(n * c, 64) * CYC
@@ -129,7 +132,7 @@ def build(rank, T, topo):
         return add("v", lambda e: e.tensor_tensor(ap(T, out), ap(T, a), ap(T, b), op), [a, b], [out], vdur(width(out), c))
 
     def ts(out, a, s1, op0, s2=None, op1=None):
-        c = 0.5 if two(out, a) else 1
+        c = GC if "win" in a else (0.5 if two(out, a) else 1)
         if op1 is None:
             fn = lambda e: e.tensor_scalar(ap(T, out), ap(T, a), val(s1), None, op0)
         else:
@@ -154,15 +157,26 @@ def build(rank, T, topo):
     def fetch(how, out, a):
         return cp(out, a) if how == "v" else act(out, a, ID)
 
-    def mm(out, terms, start=True, stop=True):
+    def mms(whole, terms, start, stop):
         def fn(e):
-            for k, (l, r) in enumerate(terms):
+            for k, (out, l, r) in enumerate(terms):
                 ins = e.matmul(ap(T, out), ap(T, l), ap(T, r), start and k == 0, stop and k == len(terms) - 1)
             return ins
-        return add("t", fn, [x for t in terms for x in t], [out], 0.03 + sum(1 if two(l) else 4 for l, r in terms) * max(64, width(out)) * PEC)
+        return add("t", fn, [x for t in terms for x in t[1:]], [whole], 0.03 + sum((1 if two(l) else 4) * max(64, width(r)) for o, l, r in terms) * PEC)
+
+    def mm(out, terms, start=True, stop=True):
+        return mms(out, [(out, l, r) for l, r in terms], start, stop)
+
+    def total(c, terms, start=True, stop=True):
+        for b in banks(c):
+            mm(R("pb", *b), [(R(m), R(name, *b)) for m, name in terms], start, stop)
 
     def diag(mat, src, m0, m1):
         return [(R(mat, 15 - i, 143 - i), R(src, 16 * m0 + i, 16 * m1, 16)) for i in range(16)]
+
+    def blocks(out, mat, src, c):
+        return [(R(out, max(c[0] - NW * i, 0), NW), R(mat, 15 - i, 143 - i), R(src, max(NW * i, c[0]), NW * i + NW))
+                for i in reversed(range(c[0] // NW, c[1] // NW))]
 
     def spare(m0, m1):
         state["ex"] ^= 1
@@ -182,13 +196,19 @@ def build(rank, T, topo):
     def mark_anchors(name, x):
         return pick(R(name, 0, A), R("ones"), 0, ALU.not_equal, x, 0)
 
-    def dma(q, out, in_, nbytes, after=(), bonus=0.0):
-        rd = [in_] if isinstance(in_, dict) else []
-        wr = [out] if isinstance(out, dict) else []
+    def dmas(q, pairs, nbytes, after=(), bonus=0.0, adding=False):
         k = state["dma"]
         state["dma"] += 1
-        return add(q, lambda e: e.dma_start(val(out), val(in_)), rd, wr, 0.1, kind="d", lat=OPT["dl"] + nbytes / BW, xfer=nbytes / BW,
-                   bonus=bonus, sem="dma%d" % k, after=list(after))
+        how = {"accum_op": ADD} if adding else {}
+        return add(q, lambda e: [e.dma_start(val(o), val(i), **how) for o, i in pairs], [i for o, i in pairs], [o for o, i in pairs],
+                   OPT["gdma"] if q == "g" else 0.07 * len(pairs) + 0.03, kind="d", lat=OPT["dl"] + nbytes / BW, xfer=nbytes / BW, bonus=bonus,
+                   sem="dma%d" % k, after=list(after), n=len(pairs))
+
+    def dma(q, out, in_, nbytes, after=(), bonus=0.0):
+        return dmas(q, [(out, in_)], nbytes, after, bonus)
+
+    def hbm(t, c, rows):
+        return t[rows[0]:128:rows[1], c[0]:c[1]]
 
     def dup(how, out, a):
         if how == "s":
@@ -205,7 +225,7 @@ def build(rank, T, topo):
         ids = [DstId(rid=topo.addr(d)[0], pnc=topo.addr(d)[1]) for d in dsts]
         fn = lambda e: e.remote_dma_fused([RemoteDMATransfer(dst_ids=ids, dma_engine_mask=mask, remote_sem=T.sem[sem], srcs=[ap(T, in_)],
                                                              dsts=[ap(T, out) for d in dsts])], local_sem=T.sem["sent"])
-        return add("g", fn, [in_], [], dur, kind="s", tail=tail, n=len(topo.engines(me, dsts[0])))
+        return add("g", fn, [in_], [], dur, kind="s", tail=tail, tos=list(tos), semname=sem, n=len(topo.engines(me, dsts[0])))
 
     def arrive(frm, buf, sem, after, lat):
         return add("x", None, [], [buf], 0.0, kind="r", lat=lat, sem=sem, n=len(topo.engines(T.cores[frm], me)), after=list(after))
@@ -213,93 +233,146 @@ def build(rank, T, topo):
     def off(name, c, base=0):
         return R(name, base + c[0] // 16, base + c[1] // 16)
 
+    def by_scalar(win, l, own, c, tmp, base, shift=0):
+        o = act(R(tmp, c[0] - base, c[1] - base), G(R(win), off(l, c)), ID)
+        for b in banks((c[0] - shift, c[1] - shift)):
+            s = (b[0] + shift, b[1] + shift)
+            mm(R("pb", *b), [(R(m), R(name, *s)) for m, name in own], True, False)
+            mm(R("pb", *b), [(R("idf"), R(tmp, s[0] - base, s[1] - base))], False, True)
+        return o
+
+    def col(k):
+        return R("cf", k, k + 1)
+
+    odd, age, m32, m8, grp, oct_ = (col(k) for k in range(1, 7))
+    isptr, notptr, ishost, is0, is2, lift, plain, spot, wl = (col(k) for k in range(9, 18))
+
+    def rows_from(blk, win):
+        tt(R("lo"), blk, R("hi"), SUB)
+        return dmas("s", [(R(win, rows=(0, 16)), R("hi")), (R(win, rows=(8, 16)), R("lo"))], 98304)
+
+    def hosts(wins):
+        tt(R("ch"), R("ch"), R("ce"), MUL)
+        ts(R("ch", 0, A), R("ch", 0, A), notptr, MUL, isptr, ADD)
+        return dmas("s", [(R(name, rows=HOST), R("ch")) for name in wins], 98304 * len(wins))
+
+    def wrap(blk, how):
+        fetch(how[0], R("t1"), G(blk, R("f1")))
+        tr(R("t2"), R("t1"))
+        return fetch(how[1], R("l1"), G(R("t2"), R("f2")))
+
+    def mark_round(name, r):
+        return act(R(name, 0, A), R("cnt"), ID, scale=is0, bias=col(24 + r))
+
+    def copy_own(how, name, c):
+        if how == "s":
+            return dmas("s", [(R("vd", *c, rows=w), R(name, *c, rows=w)) for w in REST + (HOST,)], 224 * (c[1] - c[0]))
+        if how == "v":
+            return ts(R("vd", *c), R(name, *c), notptr, MUL, isptr, ADD)
+        return act(R("vd", *c), R(name, *c), ID, scale=notptr, bias=isptr)
+
     sends, gets = rank < NR - 1, rank > 0
     later = range(NR - 1, rank, -1)
+    ALL = (0, V)
+    sch = OPT["sch"]
 
-    dma("s", R("pari"), T.par[:], 98304, bonus=300.0)
-    for c in C3N:
-        dma("s", R("h0", *c), T.hf[:, c[0]:c[1]], 262144, bonus=80.0)
-    dma("a", R("an", 0, A), T.hf[:, 0:A], 32768)
-    dma("a", R("an", A, 2 * A), T.bt[:, 0:A], 32768)
-    if gets:
-        dma("a", R("upi"), T.up[:], 4096)
+    dmas("s", [(R("ce"), hbm(T.hf, ALL, PTR)), (R("ch"), hbm(T.hf, ALL, HOST))], 196608, bonus=320.0)
+    dma("a", R("pari"), T.par[:], 98304, bonus=300.0)
+    dmas("s", [(R("wx", A, V, rows=w), hbm(T.hf, (A, V), w)) for w in REST], 565000, bonus=80.0)
 
-    state["boost"] = OPT["cboost"]
+    state["boost"] = 100.0
     iota(R("ci", 0, 1), [[0, 1]], 0, 1)
-    one = fill(R("ones"), 1.0)
-    pick(R("idp"), R("ones"), -1, ALU.is_equal, 0.0, 1)
-    for name, w in (("idn", -1.0), ("idk", -KK), ("idb", 1024.0), ("idc", 512.0), ("idl", 2.0 * LL), ("idf", 1.0), ("idg", -1.0), ("idh", 1.0)):
-        made = act(R(name), R("idp"), ID, scale=w)
     iota(R("iw", 24, 36), [[16, 12]], 0, 0)
+    iota(R("cnt"), [[1, A]], 0, 0)
     iota(R("iw", 0, 24), [[16, 12], [0, 2]], 0, 0)
-    iota(R("iw", 36, 44), [[1, 8]], 0, 0)
-    iota(R("iw", 44, 68), [[1, 12], [0, 2]], 0, 0)
-    iota(R("iw", 68, 80), [[32, 12]], 0, 0)
-    fill(R("pw"), 0.0)["after"] = [one]
-    for k, x in ((1, 16), (2, 15), (3, 31)):
-        ts(R("ci", k, k + 1), R("ci", 0, 1), x, ALU.bitwise_and)
-    ts(R("ci", 4, 5), R("ci", 0, 1), 4, ALU.arith_shift_right)
-    cp(R("cf", 1, 5), R("ci", 1, 5))
-    odd, age, m32, grp = (R("cf", k, k + 1) for k in (1, 2, 3, 4))
+    for k, x in ((2, 15), (1, 16), (4, 7), (3, 31)):
+        ts(R("ci", k, k + 1), R("ci", 0, 1), x, AND)
+    for k, x in ((5, 4), (6, 3)):
+        ts(R("ci", k, k + 1), R("ci", 0, 1), x, ALU.arith_shift_right)
+    cp(R("cf", 1, 7), R("ci", 1, 7))
+    ts(notptr, m8, 0.0, ALU.not_equal)
+    ts(is2, age, 2.0, EQ)
+    ts(is0, age, 0.0, EQ)
+    ts(isptr, m8, 0.0, EQ)
     ts(R("f1"), R("iw", 0, 24), age, ADD)
     act(R("s1", 0, 12), R("iw", 24, 36), ID, bias=age)
     act(R("s2", 0, 12), R("s1", 0, 12), ID, bias=-5.5 / 12.0, scale=1.0 / 12.0)
     act(R("s1", 12, 24), R("s2", 0, 12), ID, bias=odd, scale=-383.0)
-    act(R("s1", 24, 36), R("s1", 0, 12), ID, scale=32.0)
+    act(col(24), is2, ID, bias=notptr)
+    mark_round("wx", 0)
+    ts(R("s1", 24, 36), R("s1", 0, 12), 32.0, MUL)
     tt(R("s1", 36, 48), R("s1", 12, 24), R("s1", 24, 36), ADD)
     cp(R("f2"), R("s1", 36, 48))
-    act(R("cf", 5, 6), age, ID, scale=12.0)
-    ts(R("cf", 6, 7), age, 1.0, ALU.is_le)
-    ts(R("cf", 7, 8), age, 2.0, ALU.is_equal)
-    ts(R("f3"), R("iw", 44, 68), R("cf", 5, 6), ADD)
-    ts(R("f4"), R("iw", 68, 80), m32, ADD)
-    for name, w in (("msel", R("cf", 6, 7)), ("mdep", R("cf", 7, 8)), ("msum", 1.0)):
+    ts(R("ce"), R("ce"), -0.5, MUL, 1.5, ADD)
+    act(R("hi"), R("pari"), ID)
+    rows = [hosts(["wx"]), rows_from(R("pari"), "wx")]
+    gate = wrap(R("pari"), "vv")
+    for j, c in enumerate(sch):
+        copy_own(OPT["hdup"][j], "wx", c)
+
+    state["boost"] = OPT["cboost"]
+    rest = len(ops)
+    fill(R("ones"), 1.0)
+    for name, w in (("msel", isptr), ("msum", 1.0)):
         fill(R(name), 0.0)
-        ts(R(name, 15, 143, 16), R("iw", 36, 44), grp, ALU.is_equal, w, MUL)
+        ts(R(name, 15, 143, 16), R("cnt", 0, 8), grp, EQ, w, MUL)
+    act(plain, is2, ID, scale=-1.0, bias=notptr)
+    for r, name in enumerate(("gs", "j2", "j4", "j8", "j16", "va")):
+        if r:
+            act(col(24 + r), is2, ID, scale=2.0 ** (2 ** r), bias=plain)
+        mark_round(name, r)
+    fill(R("one2"), 1.0)
+    for name in ("idp", "idh", "idf"):
+        pick(R(name), R("ones"), -1, EQ, 0.0, 1)
+    ts(ishost, m8, 4.0, EQ)
+    ts(lift, age, 8.0, EQ, 16.0, MUL)
+    act(spot, m8, ID, scale=16.0, bias=oct_)
+    act(wl, notptr, ID, scale=LT / KK)
+    fill(R("nil"), 0.0)
+    for name, w in (("idq", 512.0), ("idr", 1024.0), ("idn", -1.0), ("idt", 256.0), ("ids", -16.0)):
+        pick(R(name), R("nil"), -1, ALU.not_equal, w, 1)
+    act(R("idl"), R("idp"), ID, scale=wl)
     act(R("mneg"), R("msum"), ID, scale=-1.0)
     act(R("mtwo"), R("msum"), ID, scale=2.0)
-    mark_anchors("h0", 2.0)
+    fill(R("mx"), 0.0)
+    ts(R("mx", 7, 135, 8), R("cnt", 0, 16), oct_, EQ, ishost, MUL)
+    fill(R("mr"), 0.0)
+    ts(R("mr", 0, 1024, 8), R("cnt"), spot, EQ, LT / KK, MUL)
+    act(R("hm", 0, A), R("ones"), ID, scale=2.0 * KK)
     state["boost"] = 0.0
-    mark_anchors("gs", 1.0)
     if sends:
         for e in range(EP):
             act(R("msg", MS * e + A + 8, MS * e + MS), R("ones", 0, 8), ID)
-        fill(R("ez", A, 2 * A), 0.0)
-
-    def rows_from(blk, how):
-        tt(R("lo"), blk, R("hi"), SUB)
-        dma("s", row("pw", 0), R("hi"), 49152)
-        dma(how, row("pw", 1), R("lo"), 49152)
-
-    sch = OPT["sch"]
-    for j, c in enumerate(sch):
-        dup(OPT["hdup"][j], R("vd", *c), R("h0", *c))
-    state["boost"] = 40.0
-    act(R("hi"), R("pari"), ID)
-    rows_from(R("pari"), "a")
-    state["boost"] = 0.0
-    cp(R("t1"), G(R("pari"), R("f1")))
-    tr(R("t2"), R("t1"))
-    cp(R("l1"), G(R("t2"), R("f2")))
-    dup("g", R("pv"), R("l1"))
+    dup("g", R("blk"), R("pari"))
     cp(R("l16", 0, 8), R("l1", 0, 8))
-    mark_anchors("zd", 16.0 * LL)
+    for c in C3N:
+        dmas("s", [(R("b0", *c), T.bt[:, c[0]:c[1]]), (R("h0", *c), T.hf[:, c[0]:c[1]])], 500000, bonus=20.0)
+    dma("a", R("an", 0, A), T.hf[:, 0:A], 32768)
+    dma("a", R("an", A, 2 * A), T.bt[:, 0:A], 32768)
+    if gets:
+        dma("a", R("upi"), T.up[:], 4096)
+    for o in ops[rest + 1:]:
+        if o["eng"] == "v" and o["wr"][0]["n"] != "nil":
+            o["behind"] = [gate]
+        if o["kind"] == "d":
+            o["after"] = [gate]
+            for p in rows if o["eng"] == "s" else []:
+                follow(p, o)
+    marks = [mark_anchors("zd", 8.0 * LT), mark_anchors("zc", 512.0)]
 
     lists = ["l1", "l2", "l4", "l8", "l16"]
-    wins = ["pw", "j2", "j4", "j8", "j16"]
-    marks = [dup("g", R(name, 0, A), R("pw", 0, A)) for name in wins[1:]] + [mark_anchors("va", 4.0), mark_anchors("vb", 16.0)]
-    state["lazy"] = False
     head = {"lag": OPT["head"]}
     if gets:
         send([rank - 1], R("upn"), R("upi"), "aup", head, OPT["first"])["after"] = marks
         send([rank - 1], R("ann"), R("an"), "aan", head)["after"] = marks
-        arrive(0, R("a0"), "aa0", [], 20.0)
+        arrive(0, R("a0"), "aa0", [], 22.0)
     else:
         send(later, R("a0"), R("an"), "aa0", head, OPT["first"])["after"] = marks
     if sends:
-        arrive(rank + 1, R("upn"), "aup", [], 16.0)
-        arrive(rank + 1, R("ann"), "aan", [], 17.0)
-        cp(R("lh", 0, 8), R("upn"))
+        arrive(rank + 1, R("upn"), "aup", [], 18.0)
+        arrive(rank + 1, R("ann"), "aan", [], 19.0)
+        dup("g", R("lh", 0, 8), R("upn"))
+        tt(R("qq"), R("ann", 0, A), R("ann", A, 2 * A), MUL)
     a0 = "a0" if gets else "an"
     act(R("y0", A, 2 * A), R(a0, A, 2 * A), ID, bias=float(LL))
     tt(R("y0", 0, A), R("y0", A, 2 * A), R(a0, 0, A), MUL)
@@ -308,181 +381,208 @@ def build(rank, T, topo):
     edge = own[-1][1]
     for e in range(EP):
         first = e == 0
+        win = "wx" if first else "gs"
+        wins = [win, "j2", "j4", "j8", "j16", "va"]
         tail = {"lag": OPT["arrive"] + OPT["compose"] + (0.0 if gets else OPT["lead"])}
-        if not first:
-            for c in C3N:
-                act(R("xp", *c), G(R("xd"), off("l1", c)), ID)
-                tt(R("qd", *c), G(R("hs"), off("l1", c)), R("d0", *c), MUL)
-        vw = "h0" if first else "gs"
         for r in range(5):
-            for c in C3N if r < 4 else []:
-                act(R(wins[r + 1], *c), G(R(wins[r]), off(lists[r], c)), ID)
-                x = spare(c[0] // 16, c[1] // 16)
-                mm(x, diag("msel", wins[r + 1], x["c0"], x["c1"]))
-                cp(off(lists[r + 1], c), x)
-            vn = "va" if r % 2 == 0 else "vb"
-            if first != (r < 2):
-                mark_anchors(vn, 2.0 ** (2 ** (r + 1)) if first else 1.0)
             for j, c in enumerate(sch if r < 4 else OPT["slast"]):
-                o = tt(R(vn, *c), G(R(vw), off(lists[r], c)), R("vd", *c), MUL)
+                o = follow(o if j else None, tt(R(wins[r + 1], *c), G(R(wins[r]), off(lists[r], c)), R("vd", *c), MUL))
                 if r < 4:
-                    dup(OPT["vdup"][j], R("vd", *c), R(vn, *c))
-                if first and r == OPT["bload"]:
-                    dma("s", R("b0", *c), T.bt[:, c[0]:c[1]], 190000, after=[o])
-                if first and r == 2 and j in (0, 2):
-                    n = (NW * j // 2, NW * j // 2 + NW)
+                    copy_own(OPT["vdup"][4 * e + r][j], wins[r + 1], c)
+                if first and r == OPT["nload"] and j < 2:
+                    n = (NW * j, NW * j + NW)
                     dma("s", R("nbi", *n), T.nb[:, n[0]:n[1]], 98304, after=[o])
                     dup("g", R("ln", *n), R("nbi", *n))
-                if first and r == 4:
+                if first and r == OPT["dload"]:
                     dma("s", R("d0", *c), T.dr[:, c[0]:c[1]], 190000, after=[o])
-            vw = vn
+            for c in OPT["jch"] if r < 4 else []:
+                x = spare(c[0] // 16, c[1] // 16)
+                mm(x, diag("msel", wins[r + 1], x["c0"], x["c1"]))
+                fetch(OPT["lcp"][4 * e + r], off(lists[r + 1], c), x)["boost"] = 5.0
+            o["mile"] = True
             if r == 1:
                 head.setdefault("op", o)
-        state["boost"] = OPT["pboost"]
-        terms = (("idp", "b0"), ("idc", "h0")) if first else (("idp", "qd"), ("idp", "xd"), ("idn", "xp"), ("idb", "gs"))
+        if not first:
+            mark_anchors("zc", 512.0)
+        for j, c in enumerate(OPT["pch"]):
+            terms, lifted = [("idq", "h0"), ("idp", "b0")], 0.0
+            if not first:
+                if OPT["xpr"][j] == "v":
+                    tt(R("xp", *c), G(R("xd"), off("l1", c)), R("xi", *c), SUB)
+                    terms = [("idq", "g0"), ("idn", "xp")]
+                else:
+                    act(R("xp", *c), G(R("xd"), off("l1", c)), ID)
+                    terms = [("idq", "g0"), ("idp", "xd"), ("idn", "xp")]
+                if OPT["qdr"][j] == "v":
+                    tt(R("qd", *c), G(R("hs"), off("l1", c)), R("d0", *c), MUL)
+                    terms += [("idp", "qd")]
+                else:
+                    act(R("qd", *c), G(R("hs"), off("l1", c)), ID)
+                    total(c, [("idp", "d0"), ("idq", "qd")])
+                    act(R("pp", *c), R("pb", *c), ABS)
+                    terms, lifted = terms + [("idh", "pp")], 512.0
+            total(c, terms)
+            act(R("zc", *c), R("pb", *c), ABS, bias=-lifted)
+            if not first:
+                dup("g", R("pp", *c), R("zc", *c))
         for c in OPT["pch"]:
-            for b in banks(c):
-                mm(R("pb", *b), [(R(m), R(name, *b)) for m, name in terms])
-            act(R("pp", *c), R("pb", *c), ABS)
-            for b in banks(c):
-                mm(R("pb", *b), [(R("idh"), R("pp", *b))] + ([(R("idk"), R("h0", *b))] if first else []), True, False)
-        state["boost"] = 0.0
-        mark_anchors("za", float(LL))
-        for j, c in enumerate(OPT["slast"]):
-            ts(R("hm", *c), R("va", *c), 0.0, ALU.is_gt, 0.5, SUB)["boost"] = OPT["kboost"]
-            for b in banks(c):
-                mm(R("pb", *b), [(R("idl"), R("hm", *b))], False, True)
-            act(R("za", *c), R("pb", *c), ABS, bias=(KK if first else 0.0) - 512.0)
-            if c[0] < edge:
-                dup(OPT["z0dup"][j], R("zd", c[0], min(c[1], edge)), R("za", c[0], min(c[1], edge)))
-        dma("s", row("pw", 2), row("va", 2), 49152)
+            act(R("pg", *c), G(R("zc"), off("l1", c)), ID)
+            total(c, ([("idr", "h0"), ("idp", "b0")] if first else [("idr", "g0")]) + [("idh", "pg")])
+            act(R("pg", *c), R("pb", *c), ABS, bias=-512.0)
+            total(c, ([] if first else [("idh", "pp")]) + [("idh", "pg")], True, False)
         if sends:
             state["boost"] = OPT["hboost"]
             act(R("sj", 0, A), G(R("j8"), R("lh", 0, 8)), ID)
             act(R("sj", A, 2 * A), G(R("j16"), R("lh", 0, 8)), ID)["boost"] = 0.0
-            x = spare(0, 16)
+            x = R("ex0", 0, 16)
             mm(x, diag("msel", "sj", 0, 16))
-            cp(R("lh", 8, 24), x)
+            act(R("lh", 8, 24), x, ID)
             act(R("sk", 0, A), G(R("j8"), R("lh", 16, 24)), ID)
             act(R("sk", A, 2 * A), G(R("j16"), R("lh", 16, 24)), ID)
-            x = spare(0, 16)
             mm(x, diag("msel", "sk", 0, 16))
-            cp(R("lh", 24, 32), R(x["n"], 0, 8))
-            act(R("msg", MS * e + A, MS * e + A + 8), R(x["n"], 8, 16), ID)
-            if OPT["sround"] == 1:
-                act(R("sl"), G(R("j4"), R("lh", 0, 32)), ID)
-                y = spare(0, 32)
-                mm(y, diag("msel", "sl", 0, 32))
-                cp(R("lh", 32, 64), y)
-            act(R("hu"), G(R("va"), R("lh", 0, 8)), SIGN)
-            tt(R("ez", 0, A), R("hu"), R("ann", A, 2 * A) if first else R("qq"), MUL)
+            act(R("lh", 24, 32), R("ex0", 0, 8), ID)
+            act(R("msg", MS * e + A, MS * e + A + 8), R("ex0", 8, 16), ID)
+            act(R("sl"), G(R("j4"), R("lh", 0, 32)), ID)
+            x = R("ex0", 0, 32)
+            mm(x, diag("msel", "sl", 0, 32))
+            act(R("lh", 32, 64), x, ID)
+            state["boost"] = 0.0
+        mark_anchors("za", float(LT))
+        made = []
+        for j, c in enumerate(OPT["slast"]):
+            state["boost"] = OPT["kboost"]
+            ts(R("hm", *c), R("va", *c), 0.0, ALU.is_gt, 2.0 * KK, MUL)
+            x = R("ex1", c[0] // 8, c[1] // 8)
+            w = [R(name, x["c0"], x["c1"]) for name in ("wi", "cw")]
+            for b in banks(c):
+                n = (b[1] - b[0]) // 8
+                mm(R(x["n"], b[0] // 8, b[1] // 8), [(R("mx", 7 - i, 135 - i), R("va", b[0] + n * i, b[0] + n * i + n)) for i in range(8)])
+            act(w[0], x, ABS, scale=0.5)
+            ts(w[0], w[0], ODD, AND)
+            act(w[1], w[0], RELU, bias=2.0 * KK, scale=-2.0 * KK)
+            for b in banks(c):
+                n = (b[1] - b[0]) // 8
+                total(b, [("idl", "hm")], False, False)
+                mms(R("pb", *b), [(R("pb", b[0] + n * i, b[0] + n * i + n), R("mr", A * i, A * i + A), R("cw", b[0] // 8, b[1] // 8))
+                                  for i in range(8)], False, True)
+            dmas("s", [(R("hm", *b, rows=PTR), R("cw", b[0] // 8, b[1] // 8)) for b in banks(c)], 32 * (c[1] - c[0]))
+            state["boost"] = 0.0
+            made.append(act(R("za", *c), R("pb", *c), ABS, bias=-(1024.0 if first else 1536.0) - LT))
+            if c[0] < edge:
+                dup(OPT["z0dup"][j], R("zd", c[0], min(c[1], edge)), R("za", c[0], min(c[1], edge)))
+        dma("s", R(win, rows=(2, 16)), R("va", rows=(2, 16)), 49152)
+        if sends:
+            state["boost"] = OPT["hboost"]
+            act(R("hu"), G(R("hm"), R("lh", 0, 8)), SIGN, bias=-KK)
             mh = R("hu")
             if first:
                 mh = R("cu")
                 tt(mh, R("hu"), R("ann", 0, A), MUL)
-            act(R("mo"), mh, ID, bias=256.0, scale=256.0)
             state["boost"] = 0.0
-        state["lazy"], state["boost"] = False, OPT["nboost"]
-        for c in OPT["nch"]:
-            x = spare(c[0] // 16, c[1] // 16)
-            mm(x, diag("mdep", "va", x["c0"], x["c1"]))
-            act(off("dv", c), x, ABS)
+        dma("s", R("dv"), R("va", rows=(2, 16)), 49152)
+        act(R("dv"), R("dv"), ABS)
         for k in range(2):
-            nk, qk = "n%d" % k, "q%d" % k
+            nk = "n%d" % k
             for c in OPT["ngather"]:
-                act(R(nk, *c), G(R("pw"), off("ln", c, NW * k)), ID)
+                o = act(R(nk, *c), G(R(win), off("ln", c, NW * k)), ABS, bias=lift)
+                for p in made:
+                    follow(p, o)
             for c in OPT["nch"]:
-                m0, m1 = c[0] // 16, c[1] // 16
-                x = spare(m0, m1)
-                mm(x, diag("msel", nk, m0, m1))
-                cp(off("lc%d" % k, c), x)
-                act(off("e%d" % k, c), x, ID)
-                x = spare(m0, m1)
-                mm(x, diag("mdep", nk, m0, m1))
-                act(off(qk, c), x, ABS)
-            x = spare(8, NW)
-            mm(x, [(R("idn"), R(qk, 8, NW)), (R("idp"), R("dv", 8, NW))])
-            act(R("pen%d" % k, 8, NW), x, AF.Relu, scale=PEN)
-        s0 = R("ex0", 256 + 8, 256 + NW)
-        mm(s0, [(R("idf"), R("e0", 8, NW)), (R("idg"), R("pv", 8, NW))])
-        state["lazy"], state["boost"] = False, 0.0
+                x = R("ex1", c[0] // 16, c[1] // 16)
+                mm(x, diag("msel", nk, x["c0"], x["c1"]))
+                if OPT["lcr"] == "a":
+                    act(off("lc%d" % k, c), x, ID, bias=-16.0)
+                else:
+                    ts(off("lc%d" % k, c), x, -16.0, ADD)
+            q = [R("q%d" % k, NW * i, NW * i + NW) for i in range(3)]
+            dmas("s", [(q[i], R(nk, rows=(w, 16))) for i, w in enumerate((0, 8, 2))], 147456)
+            mm(R("ex%d" % k, 256, 256 + NW), [(R("idn"), R("hi")), (R("idn"), R("lo")), (R("ids"), R("one2")), (R("idp"), q[0]), (R("idp"), q[1])])
+            x = R("ex0", 0, NW)
+            mm(x, [(R("idp"), R("dv")), (R("idn"), q[2])])
+            act(R("pen%d" % k), x, RELU, scale=PEN)
         if first:
-            state["boost"] = OPT["gboost"]
             for c in C3N:
-                ts(R("gs", *c), R("d0", *c), 128.0, ALU.is_lt, 0.5, SUB)
-                dup(OPT["gdup"], R("vd", *c), R("gs", *c))
-            state["boost"] = 0.0
+                act(R("g0", *c), R("d0", *c), SIGN, bias=127.5, scale=-1.0)
         zw = "za"
         mark = None
-        for r in range(4):
-            zn = "zb" if r % 2 == 0 else "za"
-            mark_anchors(zn, float(LL * 2 ** (r + 1)))
-            state["boost"] = OPT["sboost"]
-            for j, c in enumerate(OPT["share"]):
-                zg = R("zg", 512 * j, 512 * j + c[1] - c[0])
-                act(zg, G(R(zw), off(lists[r], c)), ID)
-                mm(R("pb", *c), [(R("idf"), R(zw, *c))], True, False)
-                mm(R("pb", *c), [(R("idf"), zg)], False, True)
+        for r in range(1, 4):
+            zn = "zb" if r % 2 else "za"
+            mark_anchors(zn, float(LT * 2 ** r))
+            for c in OPT["share"]:
+                by_scalar(zw, lists[r], [("idf", zw)], c, "zg", edge)
                 act(R(zn, *c), R("pb", *c), ID)
-            state["boost"] = 0.0
             for j, c in enumerate(own):
-                o = tt(R(zn, *c), G(R(zw), off(lists[r], c)), R("zd", *c), ADD)
-                dup(OPT["zdup"][r][j], R("zd", *c), R(zn, *c))
+                o = follow(o if j else None, tt(R(zn, *c), G(R(zw), off(lists[r], c)), R("zd", *c), ADD))
+                dup(OPT["zdup"][r - 1][j], R("zd", *c), R(zn, *c))
             zw = zn
-            if r == OPT["sround"]:
+            o["mile"] = True
+            if r == 1:
                 mark = o
                 if sends:
                     state["boost"] = OPT["mboost"]
-                    x = R("pb", 0, A)
-                    for k in (2, 3):
-                        act(R("zq", 256 * k, 256 * k + 256), G(R(zw), R("lh", 16 * k, 16 * k + 16)), ID)
-                        mm(x, [(R("idf"), R("zq", A * i, A * i + A)) for i in (2 * k, 2 * k + 1)], k == 2, False)
-                    tt(R("zq", 0, 256), G(R(zw), R("lh", 0, 16)), R("ez"), ADD)
-                    tt(R("zq", 256, 512), G(R(zw), R("lh", 16, 32)), R("zq", 0, 256), ADD)
-                    mm(x, [(R("idf"), R("zq", A * i, A * i + A)) for i in (2, 3)], False, True)
+                    x, mo, n = R("pb", 0, A), R("pb", A, 2 * A), OPT["zqv"]
+                    mm(mo, [(R("idq"), mh), (R("idp"), R("qq")), (R("idq"), R("ones")), (R("idt"), R("ones"))])
+                    act(R("zq", n, 1024), G(R(zw), R("lh", n // 16, 64)), ID, bias=-2.0 * LT)
+                    ts(R("zq", 0, n), G(R(zw), R("lh", 0, n // 16)), -2.0 * LT, ADD)
+                    for k in range(2):
+                        mm(x, [(R("idh"), R("zq", A * i, A * i + A)) for i in range(4 * k, 4 * k + 4)], k == 0, k == 1)
                     tt(R("yi"), x, mh, MUL)
-                    ts(R("yi"), R("yi"), 255, ALU.bitwise_and)
-                    tt(R("msg", MS * e, MS * e + A), R("yi"), R("mo"), ADD)
+                    ts(R("yi"), R("yi"), 255, AND)
+                    tt(R("msg", MS * e, MS * e + A), R("yi"), mo, ADD)
                     s = MS * (5 * e + rank)
                     mark = send(later, R("lsg", s, s + MS), R("msg", MS * e, MS * e + MS), "am%d_%d" % (e, rank), tail)
+                    mark["mile"] = True
                     state["boost"] = 0.0
         if gets:
             for f in range(rank):
                 s = MS * (5 * e + f)
                 arrive(f, R("lsg", s, s + MS), "am%d_%d" % (e, f), [mark], OPT["arrive"] + (0.0 if sends else 2.8))
-            yw = R("y0", A * e, A * e + A)
+            shifts = [R("pb", 1536 + A * f, 1536 + A * f + A) for f in range(rank)]
             for f in range(rank):
                 s = MS * (5 * e + f)
-                u, y = R("uu", A * f, A * f + A), R("zz", A * f, A * f + A) if f < rank - 1 else R("zb", 0, A)
-                act(R("ms", A * f, A * f + A), R("lsg", s, s + A), SIGN, bias=-384.0)
-                dup(OPT["lp"], R("lp", 8 * f, 8 * f + 8), R("lsg", s + A, s + A + 8))
+                act(R("ms", A * f, A * f + A), R("lsg", s, s + A), SIGN, bias=-895.5)
+                dup("g", R("lp", 8 * f, 8 * f + 8), R("lsg", s + A, s + A + 8))
+                mm(shifts[f], [(R("idh"), R("lsg", s, s + A))])
+            yw = R("y0", A * e, A * e + A)
+            for f in range(rank):
+                u, y = R("uu", A * f, A * f + A), R("zz", A * f, A * f + A) if f < rank - 1 else R("za", 0, A)
                 tt(u, G(yw, R("lp", 8 * f, 8 * f + 8)), R("ms", A * f, A * f + A), MUL)
-                tt(y, u, R("lsg", s, s + A), ADD)
+                tt(y, u, shifts[f], ADD)
                 yw = y
         else:
-            act(R("zb", 0, A), R("y0", A * e, A * e + A), ID)
+            act(R("za", 0, A), R("y0", A * e, A * e + A), ID)
+        if first:
+            for c, how in OPT["final"]:
+                if how == "v":
+                    dup(OPT["zer"], R("ze", *c), R("hm", *c))
+                    c = (max(c[0], A), c[1])
+                    dmas("g", [(R("ze", *c), R("zb", *c))], 1024 * (c[1] - c[0]), adding=True)
+            mark_anchors("ze", 8.0 * LT + 2.0 * KK)
         for c, how in OPT["upper"]:
             if how == "v":
-                o = tt(R("zc", *c), G(R("zb"), off("l16", c)), R("zd", *c), ADD)
+                o = tt(R("zc", *c), G(R("za"), off("l16", c)), R("zd", *c), ADD)
             else:
-                o = act(R("zd", *c), G(R("zb"), off("l16", c)), ID)
-                mm(R("pb", *c), [(R("idf"), R("za", *c))], True, False)
-                mm(R("pb", *c), [(R("idf"), R("zd", *c))], False, True)
+                o = by_scalar("za", "l16", [("idf", "zb")], c, "zd", 0)
                 act(R("zc", *c), R("pb", *c), ID)
             tail.setdefault("op", o)
+        o["mile"] = True
         for j, (c, how) in enumerate(OPT["final"]):
             if how == "v":
-                x = R("zb", *c)
-                tt(x, G(R("zc"), off("l16", c)), R("zd", *c), ADD)
+                x = R("za", *c)
+                o = tt(x, G(R("zc"), off("l16", c)), R("ze" if first else "zd", *c), ADD)
             else:
-                x = R("pb", *c)
-                act(R("zd", *c), G(R("zc"), off("l16", c)), ID)
-                mm(x, [(R("idf"), R("za", *c))], True, False)
-                mm(x, [(R("idf"), R("zd", *c))], False, True)
-            act(R("ui", *c), x, ABS, bias=(KK if first else 0.0) - 32.0 * LL)["boost"] = OPT["uboost"]
-            ts(R("xi", *c), R("ui", *c), 255, ALU.bitwise_and)["boost"] = OPT["aboost"]
+                x = R("pb", c[0] - OPT["shift"], c[1] - OPT["shift"])
+                by_scalar("zc", "l16", [("idf", "zb")] + ([("idp", "hm")] if first else []), c, "zd", 0, OPT["shift"])
+            act(R("ui", *c), x, ABS, bias=-16.0 * LT - (KK if first else 0.0))["boost"] = OPT["uboost"]
+            ts(R("xi", *c), R("ui", *c), 255, AND).update(boost=OPT["aboost"], mile=j == len(OPT["final"]) - 1)
             dup(OPT["xcv"][j], R("xd", *c), R("xi", *c))
         if first:
+            for name in ("gs", "vd"):
+                dmas("s", [(R(name, A, V, rows=w), R("g0", A, V, rows=w)) for w in REST], 565000, after=[o])
+            dmas("s", [(R("ce"), hbm(T.dr, ALL, PTR)), (R("ch"), hbm(T.dr, ALL, HOST))], 196608, after=[tail["op"]])
+            ts(R("ce"), R("ce"), 128.0, ALU.is_ge, 1.0, ADD)
+            act(R("ch"), R("ch"), SIGN, bias=127.5, scale=-1.0)
+            hosts(["gs", "vd"])
             for c in C3:
                 act(R("hs", *c), R("ui", *c), SIGN, bias=-float(LL))
             if sends:
@@ -490,17 +590,13 @@ def build(rank, T, topo):
         else:
             for c in C3:
                 dma("s", T.yx[:, c[0]:c[1]], R("xd", *c), 262144)
-        sums = {}
-        for k, (name, l, pos) in enumerate((("da", "l1", "n0"), ("db", "lc0", "n1"), ("dc", "lc1", "hm"))):
-            for j, c in enumerate(OPT["vch"]):
-                how = OPT["votes"][k][j]
-                state["boost"] = OPT["vboost"][k]
-                m0, m1 = c[0] // 16, c[1] // 16
-                sums[k, j] = diag("msum", name, m0, m1)
+        sums = [[], [], []]
+        for k, (name, l, pos) in enumerate((("da", "l1", "n0"), ("db", "lc0", "n1"), ("dc", "lc1", "j2"))):
+            for c, how in OPT["votes"][k]:
+                sums[k].append((c, [("msum", name)]))
                 if how == "a":
                     act(R(name, *c), G(R("xi"), off(l, c)), ID)
-                    for b in banks(c):
-                        mm(R("pb", *b), [(R("idp"), R(name, *b)), (R("idn"), R("xd", *b))])
+                    total(c, [("idp", name), ("idn", "xd")])
                     act(R(name, *c), R("pb", *c), ABS)
                     continue
                 tt(R(name, *c), G(R("xi"), off(l, c)), R("xd", *c), SUB)
@@ -508,52 +604,46 @@ def build(rank, T, topo):
                     act(R(name, *c), R(name, *c), ABS)
                 else:
                     ts(R(pos, *c), R(name, *c), 0.0, ALU.max)
-                    sums[k, j] = diag("mneg", name, m0, m1) + diag("mtwo", pos, m0, m1)
-        state["boost"] = 0.0
-        for j, c in enumerate(OPT["vch"]):
-            x = off("pb", c)
-            o = mm(x, sums[0, j])
-            act(off("dp", c), x, ID)
-        for k in range(2):
-            for j, c in enumerate(OPT["vch"]):
-                last = mm(off("ex%d" % k, c), [(R("idp"), off("pen%d" % k, c))] + sums[k + 1, j])
-                if (k, j) in OPT["hold"]:
-                    last["after"] = [o]
-            o = last
-        n = (8, NW)
-        s1, cc, w1 = (R("pb", 512 * k + 8, 512 * k + NW) for k in (1, 2, 3))
-        mm(s1, [(R("idf"), R("e1", *n)), (R("idg"), R("pv", *n))])["lazy"] = True
-        tt(R("w1c", *n), R("ex0", *n), R("dp", *n), ALU.is_lt)
-        tt(R("cc", *n), s0, R("w1c", *n), MUL)
-        tt(R("mn", *n), R("ex0", *n), R("dp", *n), ALU.min)
-        mm(cc, [(R("idf"), R("pv", *n)), (R("idf"), R("cc", *n))])
-        tt(R("e1", *n), s1, R("cc", *n), SUB)
-        tt(w1, R("ex1", *n), R("mn", *n), ALU.is_lt)
-        tt(R("e0", *n), w1, R("e1", *n), MUL)
-        tt(R("pv", *n), cc, R("e0", *n), ADD)
+                    sums[k][-1] = (c, [("mneg", name), ("mtwo", pos)])
+        for k, bank in enumerate(("pb", "ex0", "ex1")):
+            for j, (c, parts) in enumerate(sums[k]):
+                x = R(bank, 0, NW)
+                pen = [(x, R("idp"), R("pen%d" % (k - 1)))] if k and j == 0 else []
+                mms(x, pen + [t for m, src in parts for t in blocks(bank, m, src, c)], j == 0, j == len(sums[k]) - 1)
+            if k == 0:
+                act(R("dp"), R("pb", 0, NW), ID)
+        s0, s1 = (R("ex%d" % k, 256, 256 + NW) for k in range(2))
+        cc, w1 = (R("pb", 512 * k, 512 * k + NW) for k in (1, 2))
+        d0, d1 = R("ex0", 0, NW), R("ex1", 0, NW)
+        tt(R("w1c"), d0, R("dp"), ALU.is_lt)
+        tt(R("cc"), s0, R("w1c"), MUL)
+        tt(R("mn"), d0, R("dp"), ALU.min)
+        tt(cc, R("blk"), R("cc"), ADD)
+        tt(R("e1"), s1, R("cc"), SUB)
+        tt(w1, d1, R("mn"), ALU.is_lt)
+        tt(R("e0"), w1, R("e1"), MUL)
+        tt(R("blk"), cc, R("e0"), ADD)["mile"] = True
         if first:
-            cp(R("l1", *n), R("pv", *n))
-        act(R("t1"), G(R("pv"), R("f3")), ID)
-        tr(R("t2"), R("t1"))
-        if first:
-            act(R("hi"), G(R("t2"), R("f4")), ID)
-        act(R("blk"), G(R("t2"), R("f4")), ID)
-        if first:
-            rows_from(R("blk"), "a")
+            state["boost"] = 10.0
+            tt(R("hi"), cc, R("e0"), ADD)
+            rows_from(R("blk"), "gs")
+            wrap(R("blk"), OPT["wrap"])
+            state["boost"] = 0.0
         else:
             dma("s", T.yp[:], R("blk"), 98304)
+    ops[0]["seed"] = OPT["seed"][rank]
     return ops
 
 
 def clash(a, b):
-    if a["lane"] is not None and b["lane"] is not None and a["lane"] != b["lane"]:
+    if a["rows"] and b["rows"] and not set(range(a["rows"][0], 16, a["rows"][1])) & set(range(b["rows"][0], 16, b["rows"][1])):
         return False
     if psum(a):
         return a["c0"] // 512 <= (b["c1"] - 1) // 512 and b["c0"] // 512 <= (a["c1"] - 1) // 512
     return a["c0"] < b["c1"] and b["c0"] < a["c1"]
 
 
-def schedule(ops):
+def deps(ops):
     seen = {}
     for o in ops:
         pre = set(p["id"] for p in o["after"])
@@ -563,119 +653,275 @@ def schedule(ops):
                 if (w or w2 or (psum(r) and o2["eng"] != o["eng"])) and clash(r, r2):
                     pre.add(o2["id"])
         pre.discard(o["id"])
-        o["pre"] = pre
+        o["all"] = pre
+        o["pre"] = pre | set(q for p in o["behind"] for q in p["all"]) | set(o["queue"])
         for r, w in acc:
             seen.setdefault(r["n"], []).append((r, w, o))
-    real = len(ops)
-    rest = [0.0] * real
-    for o in reversed(ops):
-        if o["kind"] == "s":
-            rest[o["id"]] = max(rest[o["id"]], o["tail"]["lag"] + rest[o["tail"]["op"]["id"]])
-        rest[o["id"]] += o["dur"] + o["lat"]
-        for p in o["pre"]:
-            rest[p] = max(rest[p], rest[o["id"]] + OPT["hop"])
-    ops = ops + [{"eng": "x", "kind": "r", "pre": [o["id"]], "dur": 0.0, "lat": OPT["stretch"] * rest[o["id"]],
-                  "bonus": 0.0, "boost": 0.0, "lazy": True} for o in ops if o["kind"] == "s"]
-    n = len(ops)
-    span = [o["dur"] + o["lat"] for o in ops]
-    back = [[(p, 0.0 if ops[p]["eng"] == o["eng"] == "t" else OPT["hop"]) for p in o["pre"]] for o in ops]
-    forth = [[] for _ in ops]
-    for k in range(n):
-        for p, lag in back[k]:
-            forth[p].append((k, lag))
-    holds = []
+    below = []
     for o in ops:
-        h = [] if o["eng"] == "x" else [(o["eng"], 0.0, o["dur"])]
-        if o["kind"] == "d":
-            h.append(("dma", o["dur"] + 0.6 * OPT["dl"], o["xfer"]))
-        holds.append(h)
+        far = 0
+        for p in o["pre"]:
+            far |= below[p]
+        o["pre"] = set(p for p in o["pre"] if not far >> p & 1)
+        for p in o["pre"]:
+            far |= 1 << p
+        below.append(far)
 
-    def seek(b, t):
-        lo, hi = 0, len(b)
-        while lo < hi:
-            mid = (lo + hi) // 2
-            if b[mid][1] <= t + 1e-9:
-                lo = mid + 1
-            else:
-                hi = mid
-        return lo
 
-    def place(key, before, after, mirror):
-        left = [len(x) for x in before]
-        ready = [k for k in range(n) if not left[k]]
-        busy, start = {}, [0.0] * n
-        while ready:
-            k = min(ready, key=lambda k: (key[k], k))
-            ready.remove(k)
-            t = max([0.0] + [start[p] + span[p] + lag for p, lag in before[k]])
-            hs = [(q, span[k] - a - d if mirror else a, d) for q, a, d in holds[k]]
-            moved = True
-            while moved:
-                moved = False
-                for q, a, d in hs:
-                    b = busy.setdefault(q, [])
-                    i = seek(b, t + a)
-                    while i < len(b) and b[i][0] < t + a + d - 1e-9:
-                        t, moved = b[i][1] - a, len(hs) > 1
-                        i += 1
-            for q, a, d in hs:
-                busy[q].insert(seek(busy[q], t + a), (t + a, t + a + d))
-            start[k] = t
-            for m, lag in after[k]:
-                left[m] -= 1
-                if not left[m]:
-                    ready.append(m)
-        return start, max(start[k] + span[k] for k in range(n))
+def lag_of(ops, p, o, hop):
+    same = ops[p]["eng"] == o["eng"]
+    if p not in o["all"]:
+        return -9.0 if same else 0.0
+    return 0.0 if same and o["eng"] == "t" else hop
 
-    prio = [0.0] * n
+
+def schedule(ops):
+    deps(ops)
+    n = len(ops)
+    writes = [o for o in ops if o["kind"] == "s"]
+    eng = [o["eng"] for o in ops]
+    isd = [o["kind"] == "d" for o in ops]
+    dur = [o["dur"] for o in ops]
+    lat = [o["lat"] for o in ops]
+    dl = OPT["dl"]
+    forth = [[] for _ in ops]
+    count = [len(o["pre"]) for o in ops]
+    for k, o in enumerate(ops):
+        for p in o["pre"]:
+            forth[p].append((k, lag_of(ops, p, o, OPT["hop"])))
+    for o in writes:
+        forth[o["id"]].append((o["tail"]["op"]["id"], o["tail"]["lag"] - o["dur"]))
+        count[o["tail"]["op"]["id"]] += 1
+    rank = [0.0] * n
     for k in reversed(range(n)):
-        prio[k] = ops[k]["bonus"] + span[k] + max([0.0] + [lag + prio[m] for m, lag in forth[k]])
-    rank = [prio[k] + ops[k]["boost"] for k in range(n)]
+        rank[k] = max([0.0] + [lag + rank[m] for m, lag in forth[k]]) + dur[k] + lat[k] + ops[k]["bonus"]
+    rank = [rank[k] + ops[k]["boost"] for k in range(n)]
 
-    def first_order(slack, small, look, gap):
-        left = [len(x) for x in back]
-        ready = [k for k in range(n) if not left[k]]
-        free, key, est = {}, [0.0] * n, [0.0] * n
-        while ready:
-            for k in ready:
-                est[k] = max([free.get(ops[k]["eng"], 0.0)] + [key[p] + span[p] + lag for p, lag in back[k]])
-            k0 = min(ready, key=lambda k: est[k])
-            mine = [k for k in ready if ops[k]["eng"] == ops[k0]["eng"]]
-            k = max([k for k in mine if est[k] <= est[k0] + slack], key=lambda k: (not ops[k]["lazy"] and ops[k]["dur"] < small, rank[k], -k))
-            soon = [m for m in mine if est[m] < est[k] + look * ops[k]["dur"] and rank[m] > rank[k] + gap]
-            if soon:
-                k = max(soon, key=lambda m: rank[m])
-            if ops[k]["kind"] == "d":
-                est[k] = max(est[k], free.get("dma", 0.0) - holds[k][1][1])
-                free["dma"] = est[k] + holds[k][1][1] + holds[k][1][2]
-            if ops[k]["eng"] != "x":
-                free[ops[k]["eng"]] = est[k] + ops[k]["dur"]
-            key[k] = est[k]
-            ready.remove(k)
+    def dispatch(rank):
+        left, can, who = list(count), [0.0] * n, [-1] * n
+        ready = {q: [] for q in "vatgsx"}
+        free, last = dict.fromkeys(ready, 0.0), dict.fromkeys(ready, -1)
+        start, end, why, order, line = [0.0] * n, [0.0] * n, [-1] * n, [], 0.0
+        for k in range(n):
+            if not left[k]:
+                ready[eng[k]].append(k)
+        while len(order) < n:
+            soon, q = min((min(max(can[k], free[q]) + OPT["look"] * dur[k] for k in r), q) for q, r in ready.items() if r)
+            k = max((k for k in ready[q] if can[k] <= soon), key=lambda k: rank[k])
+            ready[q].remove(k)
+            order.append(k)
+            if can[k] >= free[q] or q == "x":
+                t, why[k] = can[k], who[k]
+            else:
+                t, why[k] = free[q], last[q]
+            start[k], last[q] = t, k
+            free[q] = t = t + dur[k]
+            if isd[k]:
+                line = max(t + 0.6 * dl, line) + ops[k]["xfer"]
+                end[k] = t = line + 0.4 * dl
+            else:
+                end[k] = t = t + lat[k]
             for m, lag in forth[k]:
+                if t + lag > can[m]:
+                    can[m], who[m] = t + lag, k
                 left[m] -= 1
                 if not left[m]:
-                    ready.append(m)
-        return key
+                    ready[eng[m]].append(m)
+        k = max(range(n), key=lambda k: end[k])
+        return end[k], start, why, k, order
 
-    writes = [ops[ops[k]["pre"][0]] for k in range(real, n)]
-    best = None
-    for rule in OPT["rules"]:
-        key = first_order(*rule)
-        end = max(key[k] + span[k] for k in range(real))
-        for k, o in enumerate(writes):
-            span[real + k] = end - key[o["tail"]["op"]["id"]] + o["tail"]["lag"]
-        for i in range(OPT["passes"]):
-            start, end = place(key, back, forth, False)
-            end = max(start[k] + span[k] for k in range(real)) + sum(
-                max(0.0, start[o["id"]] + o["tail"]["lag"] - start[o["tail"]["op"]["id"]]) for o in writes)
-            if best is None or end < best[1]:
-                best = (start, end)
-            late, end = place([-start[k] - span[k] for k in range(n)], forth, back, True)
-            key = [end - late[k] - span[k] if not ops[k]["lazy"] else min(start[k], end - late[k] - span[k]) for k in range(n)]
-    for o in ops[:real]:
-        o["est"], o["end"] = best[0][o["id"]], best[0][o["id"]] + span[o["id"]]
-    return sorted(ops[:real], key=lambda o: (o["est"], o["id"]))
+    now = best = dispatch(rank)
+    seed = ops[0]["seed"]
+    for step in range(OPT["steps"]):
+        held, k = [], now[3]
+        while now[2][k] >= 0:
+            p = now[2][k]
+            if eng[p] == eng[k] and p not in ops[k]["pre"]:
+                held.append((p, k))
+            k = p
+        new = list(rank)
+        for trial in range(1 + step % 3):
+            seed = (seed * 1103515245 + 12345) % 2147483648
+            p, k = held[seed // 7 % len(held)]
+            by = 0.2 + seed // 1031 % 100 * OPT["by"]
+            if seed // 3 % 2:
+                new[k] = max(new[k], new[p]) + by
+                todo = [k]
+                while todo:
+                    m = todo.pop()
+                    for x in ops[m]["pre"]:
+                        if new[x] < new[m]:
+                            new[x] = new[m] + 0.01
+                            todo.append(x)
+            else:
+                new[p] = min(new[k], new[p]) - by
+        r = dispatch(new)
+        if r[0] < now[0] + OPT["warm"] * (1.0 - step / OPT["steps"]):
+            now, rank = r, new
+            if r[0] < best[0]:
+                best = r
+    place = {k: i for i, k in enumerate(best[4])}
+    return polish(ops, writes, sorted(range(n), key=lambda k: (best[1][k], place[k])))
+
+
+def polish(ops, writes, order):
+    n = len(ops)
+    eng = [o["eng"] for o in ops]
+    isd = [o["kind"] == "d" for o in ops]
+    sets = []
+    for gc, hop, dl, bw, late in OPT["sets"]:
+        dur = [o["dur"] + o["ng"] * (gc - OPT["gc"]) * OPT["cyc"] for o in ops]
+        lat = [o["xfer"] * OPT["bw"] / bw if isd[k] else o["lat"] + (late if o["kind"] == "r" and o["pre"] else 0.0) for k, o in enumerate(ops)]
+        pre = [[(p, lag_of(ops, p, o, hop)) for p in o["pre"]] for o in ops]
+        for o in writes:
+            pre[o["tail"]["op"]["id"]].append((o["id"], o["tail"]["lag"] + late - o["dur"]))
+        post = [[] for _ in ops]
+        for k in range(n):
+            for p, lag in pre[k]:
+                post[p].append((k, lag))
+        sets.append((dur, lat, pre, post, dl))
+    before = [[p for p, lag in x] for x in sets[0][2]]
+    after = [[p for p, lag in x] for x in sets[0][3]]
+
+    def heads(order, dur, lat, pre, post, dl):
+        free, last = dict.fromkeys("vatgsx", 0.0), dict.fromkeys("vatgsx", -1)
+        can, start, end, why, line, ahead, prev = [0.0] * n, [0.0] * n, [0.0] * n, [-1] * n, 0.0, {}, -1
+        for k in order:
+            q, t, w = eng[k], 0.0, -1
+            for p, lag in pre[k]:
+                if end[p] + lag > t:
+                    t, w = end[p] + lag, p
+            can[k] = t
+            if free[q] > t and q != "x":
+                t, w = free[q], last[q]
+            start[k], why[k], last[q] = t, w, k
+            free[q] = t = t + dur[k]
+            if isd[k]:
+                if line > t + 0.6 * dl:
+                    ahead[k] = prev
+                line, prev = max(t + 0.6 * dl, line) + lat[k], k
+                end[k] = line + 0.4 * dl
+            else:
+                end[k] = t + lat[k]
+        return max(end), can, start, end, why, ahead
+
+    def tails(order, goal, dur, lat, pre, post, dl):
+        far = -1e6 if goal >= 0 else 0.0
+        nxt, need, rest, line = dict.fromkeys("vatgsx", far), [far] * n, [far] * n, far
+        for k in reversed(order):
+            t = 0.0 if k == goal else far
+            for m, lag in post[k]:
+                if lag + rest[m] > t:
+                    t = lag + rest[m]
+            if isd[k]:
+                line = max(t, line) + lat[k]
+                need[k] = t = line + dl
+            else:
+                need[k] = t = t + lat[k]
+            if nxt[eng[k]] > t and eng[k] != "x":
+                t = nxt[eng[k]]
+            rest[k] = nxt[eng[k]] = t + dur[k]
+        return need, rest
+
+    def held_up(k, why, ahead):
+        out, landed = [], True
+        while True:
+            p = ahead[k] if landed and k in ahead else why[k]
+            if p < 0:
+                return out
+            landed = p in before[k] or p == ahead.get(k)
+            if eng[p] == eng[k] and p not in before[k]:
+                out.append((p, k))
+            k = p
+
+    def shifted(order, i, j, up):
+        take = {order[j if up else i]}
+        for x in (range(j - 1, i - 1, -1) if up else range(i + 1, j + 1)):
+            if any(s in take for s in (after if up else before)[order[x]]):
+                take.add(order[x])
+        moved, stay = [x for x in order[i:j + 1] if x in take], [x for x in order[i:j + 1] if x not in take]
+        return order[:i] + (moved + stay if up else stay + moved) + order[j + 1:]
+
+    def by_start(order, start):
+        place = {k: i for i, k in enumerate(order)}
+        return sorted(order, key=lambda k: (start[k], place[k]))
+
+    norm = [heads(order, *s)[0] for s in sets]
+    best, kept = 1e9, order
+    miles = [k for k, o in enumerate(ops) if o["mile"]]
+    seed, tabu = ops[0]["seed"], {}
+    for step in range(OPT["tries"]):
+        hs = [heads(order, *s) for s in sets]
+        total = sum((h[0] + OPT["pull"] * sum(h[3][m] for m in miles) / len(miles)) / w for h, w in zip(hs, norm))
+        if total < best:
+            best, kept = total, order
+        use = step // OPT["turn"] % len(sets)
+        span, can, start, end, why, ahead = hs[use]
+        dur = sets[use][0]
+        order = by_start(order, start)
+        turn = step // (OPT["turn"] * len(sets)) % (len(miles) + OPT["ends"])
+        goal = miles[turn] if turn < len(miles) else -1
+        need, rest = tails(order, goal, *sets[use])
+        lines = {q: [k for k in order if eng[k] == q] for q in "vatgs"}
+        at = {k: i for q in lines for i, k in enumerate(lines[q])}
+        held = held_up(goal if goal >= 0 else max(range(n), key=lambda k: end[k]), why, ahead)
+        choice = None
+        for trial in range(OPT["peek"] if held else 0):
+            seed = (seed * 1103515245 + 12345) % 2147483648
+            b = held[seed // 7 % len(held)][1]
+            line, up, far = lines[eng[b]], seed // 3 % 2, seed // 4099 % OPT["far"]
+            i, j = (max(at[b] - 1 - far, 0), at[b]) if up else (at[b] - 1, min(at[b] + far, len(line) - 1))
+            u, v = line[i], line[j]
+            if up and any(end[p] > start[u] + dur[u] for p in before[v]) or not up and any(start[m] < start[v] + dur[v] for m in after[u]):
+                continue
+            if up and any(x in before[v] for x in line[i:j]) or not up and any(x in after[u] for x in line[i + 1:j + 1]):
+                continue
+            seq = [v] + line[i:j] if up else line[i + 1:j + 1] + [u]
+            t, begins = start[line[i - 1]] + dur[line[i - 1]] if i else 0.0, []
+            for x in seq:
+                t = max(t, can[x])
+                begins.append(t)
+                t += dur[x]
+            t, guess = rest[line[j + 1]] if j + 1 < len(line) else -1e6, 0.0
+            for x, t0 in zip(reversed(seq), reversed(begins)):
+                t = dur[x] + max(t, need[x])
+                guess = max(guess, t0 + t)
+            pairs = [(v, x) for x in line[i:j]] if up else [(x, u) for x in line[i + 1:j + 1]]
+            if any(tabu.get(p, -1) > step for p in pairs):
+                continue
+            if choice is None or guess < choice[0]:
+                choice = (guess, up, u, v, pairs)
+        if choice is None:
+            continue
+        guess, up, u, v, pairs = choice
+        for x, y in pairs:
+            tabu[y, x] = step + OPT["keep"] + seed % 7
+        order = shifted(order, order.index(u), order.index(v), up)
+    order, left = kept, OPT["last"]
+    rs = [heads(order, *s) for s in sets]
+    best = sum(h[0] / w for h, w in zip(rs, norm))
+    while left > 0:
+        left -= 1
+        moves = set((p, k, up, far) for h in rs for p, k in held_up(max(range(n), key=lambda k: h[3][k]), h[4], h[5]) for up in (0, 1) for far in (0, 1, 3))
+        seed = (seed * 1103515245 + 12345) % 2147483648
+        moves = sorted(moves, key=lambda m: (m[0] * 7919 + m[1] * 31 + m[2] * 3 + m[3] + seed) * 2654435761 % 4294967296)
+        for u, v, up, far in moves[:OPT["wide"]]:
+            i, j = order.index(u), order.index(v)
+            for step in range(far):
+                if up:
+                    i = ([x for x in range(i - 1, -1, -1) if eng[order[x]] == eng[u]] + [i])[0]
+                else:
+                    j = ([x for x in range(j + 1, n) if eng[order[x]] == eng[u]] + [j])[0]
+            new = shifted(order, i, j, up)
+            left -= 1
+            hs = [heads(new, *s) for s in sets]
+            total = sum(h[0] / w for h, w in zip(hs, norm))
+            if total < best - 1e-6:
+                best, rs, order = total, hs, by_start(new, hs[0][2])
+                break
+    for i, k in enumerate(order):
+        ops[k]["est"] = i
+    return [ops[k] for k in order]
 
 
 def rank_program(g, core, T, topo):
@@ -692,7 +938,7 @@ def rank_program(g, core, T, topo):
             count[o["eng"]] += 1
             o["sig"] = ("q" + o["eng"], count[o["eng"]])
         elif o["kind"] == "d":
-            o["sig"] = (o["sem"], 16)
+            o["sig"] = (o["sem"], 16 * o["n"])
         elif o["kind"] == "r":
             o["sig"] = (o["sem"], o["n"])
         else:
@@ -706,7 +952,7 @@ def rank_program(g, core, T, topo):
             o["knows"] = {}
             continue
         q, mine = queue[o["eng"]], known[o["eng"]]
-        for p in sorted((ops[p] for p in o["pre"]), key=lambda p: -p["est"]):
+        for p in sorted((ops[p] for p in o["all"]), key=lambda p: -p["est"]):
             if p["eng"] == "t" and o["eng"] == "t":
                 continue
             s, n = p["sig"]
@@ -720,7 +966,8 @@ def rank_program(g, core, T, topo):
         if o["kind"] == "c":
             ins.then_inc(T.sem[o["sig"][0]], 1)
         elif o["kind"] == "d":
-            ins.then_inc(T.sem[o["sem"]], 16)
+            for i in ins:
+                i.then_inc(T.sem[o["sem"]], 16)
     for s in sorted(total):
         if not any(waited.get((q, s), 0) >= total[s] for q in "vatgs"):
             g.wait_ge(T.sem[s], total[s])

from concourse.bass import DstId, RemoteDMATransfer
from concourse.mybir import AluOpType as ALU, ActivationFunctionType as AF

V, A, NR, EP = 3072, 128, 6, 2
NW = V // 16
LT = 2048
KK = 32768.0
LL = 131072
PEN = 4096.0
ODD = 0x55555555
MS = A + 16

BF, F16, F32, I32, U16 = "bfloat16", "float16", "float32", "int32", "uint16"
SCRATCH = {}
for _d, _w, _names in (
        (BF, V, "h0 d0 gs va vd wx j2 j4 j8 j16 n0 n1 xd g0 hm"), (F16, V, "pp pg"), (F32, V, "za zb zc zd"), (I32, V, "ui xi"), (F32, 2048, "ze"),
        (U16, NW, "l1 l2 l4 l8 l16 lc0 lc1"), (F32, NW, "e0 e1 w1c mn cc blk dp"), (BF, NW, "hi lo one2 pen0 pen1 dv"),
        (I32, NW, "pari"), (I32, 2 * NW, "nbi wi"), (U16, 2 * NW, "ln"), (F32, 2 * NW, "t1 t2"), (BF, 2 * NW, "ce ch cw"),
        (U16, 24, "f1"), (U16, 12, "f2"), (I32, 16, "ci s2"), (F32, 32, "cf"), (F32, 48, "s1 iw"),
        (BF, 144, "msel msum mneg mtwo mx"), (BF, 1024, "mr"), (BF, 3 * NW, "q0 q1"), (BF, A, "idp idn idq idr idl ids idt ones nil cnt hu qq cu"),
        (F16, A, "idh"), (BF, 256, "a0 an ann sj sk"), (F32, A, "idf"), (F32, 256, "y0"), (F32, 1024, "zg"), (F16, 1024, "zq"), (BF, 512, "sl"),
        (I32, 8, "upi upn"), (U16, 64, "lh"), (I32, A, "yi"), (F16, EP * MS, "msg"), (F16, EP * 5 * MS, "lsg"), (BF, 5 * A, "ms"),
        (U16, 5 * 8, "lp"), (F32, 5 * A, "uu zz")):
    for _n in _names.split():
        SCRATCH[_n] = ("sbuf", [128, _w], _d)
SCRATCH.update({"pb": ("psum", [128, V], F32), "ex0": ("psum", [128, 512], F32), "ex1": ("psum", [128, 512], F32)})
SHARED = {"qd": "n0", "xp": "n1", "b0": "n1", "da": "j16", "db": "j8", "dc": "j4", "hs": "h0"}
NDMA = 120
SEMAPHORES = (["qv", "qa", "qt", "qg", "sent", "aup", "aan", "aa0"] + ["dma%d" % i for i in range(NDMA)]
              + ["am%d_%d" % (e, r) for e in range(EP) for r in range(5)])

C3 = [(0, 1024), (1024, 2048), (2048, 3072)]
C3N = [(A, 1024), (1024, 2048), (2048, 3072)]
C4N = [(A, 864), (864, 1600), (1600, 2336), (2336, V)]
C6 = [(512 * i, 512 * i + 512) for i in range(6)]
PTR, HOST, REST = (0, 8), (4, 8), ((1, 2), (2, 4))
OPT = {
    "sch": C4N, "slast": [(A, 1024)] + C6[2:], "jch": [(A, 1600), (1600, V)], "lcp": "aaaaaaaa", "hdup": "vaaa", "vdup": ["aaaa"] + ["ssss"] * 7,
    "pch": C3N, "xpr": "vaa", "qdr": "vva",
    "share": [(2688, V)], "zch": [(A, 800), (800, 1440), (1440, 2080), (2080, 2688)], "zdup": ("gssg", "gsgs", "gssg"), "z0dup": "gsgsg",
    "upper": [((0, 896), "v"), ((896, 1792), "v"), ((1792, 2560), "v"), (C6[5], "a")],
    "final": [((0, 768), "v"), ((768, 1536), "v"), (C6[3], "a"), (C6[4], "a"), (C6[5], "a")], "shift": 1536, "xcv": "gggggg", "zer": "a",
    "nch": [(A, 1600), (1600, V)], "ngather": [(0, 768), (768, 1536), (1536, 2304), (2304, V)], "lcr": "a", "wrap": "av", "dload": 3, "nload": 3,
    "zqv": 512,
    "votes": ([((A, 1152), "a"), ((1152, 2112), "a"), ((2112, V), "a")], [((A, 1152), "m"), ((1152, 2112), "v"), ((2112, V), "m")],
              [((A, 1152), "m"), ((1152, 2112), "v"), ((2112, 2688), "v"), ((2688, V), "v")]),
    "cyc": 0.83e-3, "gc": 1.5, "pe": 0.45e-3, "bw": 3.0e5, "hop": 0.12, "fix": 0.05, "dl": 1.9, "gdma": 0.5, "arrive": 5.5, "compose": 3.5,
    "first": 3.0, "head": 0, "lead": 2, "aboost": 6, "cboost": 3, "hboost": 4, "mboost": 10, "kboost": 10, "uboost": 4,
    "sets": [(1.12, 0.09, 1.8, 3.0e5, 0.0), (1.5, 0.10, 1.9, 3.0e5, 0.0), (1.9, 0.08, 1.6, 3.3e5, -0.5)],
    "seed": (4, 1, 4, 4, 1, 2), "look": 0.4, "steps": 250, "by": 0.1, "warm": 0.2, "tries": 3000, "turn": 7, "pull": 0.3, "ends": 14, "peek": 40, "far": 6,
    "keep": 15, "last": 900, "wide": 150,
}


def R(name, c0=None, c1=None, step=1, rows=None):
    name = SHARED.get(name, name)
    if c0 is None:
        c0, c1 = 0, SCRATCH[name][1][1]
    return {"n": name, "c0": c0, "c1": c1, "st": step, "rows": rows}


def G(win, off):
    return {"win": win, "off": off}


def ap(T, r):
    if "win" in r:
        return ap(T, r["win"]).indirect(ap(T, r["off"]))
    rows = slice(None) if r["rows"] is None else slice(r["rows"][0], 128, r["rows"][1])
    if r["st"] == 1:
        return T[r["n"]][rows, r["c0"]:r["c1"]]
    return T[r["n"]][rows, r["c0"]:r["c1"]:r["st"]]


def regs(rs):
    out = []
    for r in rs:
        if isinstance(r, dict):
            out += [r["win"], r["off"]] if "win" in r else [r]
    return out


def width(r):
    return len(range(r["c0"], r["c1"], r["st"]))


def size(r):
    return 2 if SCRATCH[r["n"]][2] in (BF, F16, U16) else 4


def two(*rs):
    return all(size(r) == 2 for r in rs)


def psum(r):
    return SCRATCH[r["n"]][0] == "psum"


def banks(c):
    return [(max(c[0], b[0]), min(c[1], b[1])) for b in C6 if c[0] < b[1] and b[0] < c[1]]


def build(rank, T, topo):
    ops = []
    state = {"dma": 0, "ex": 0, "boost": 0.0}
    CYC, GC, PEC, BW = OPT["cyc"], OPT["gc"], OPT["pe"], OPT["bw"]
    ID, ABS, SIGN, RELU = AF.Identity, AF.Abs, AF.Sign, AF.Relu
    ADD, SUB, MUL, EQ, AND = ALU.add, ALU.subtract, ALU.mult, ALU.is_equal, ALU.bitwise_and

    def val(x):
        return ap(T, x) if isinstance(x, dict) else x

    def add(eng, fn, rd, wr, dur, **kw):
        o = {"eng": eng, "fn": fn, "rd": regs(rd), "wr": regs(wr), "dur": dur, "lat": 0.0, "kind": "c", "after": [], "behind": [], "queue": [],
             "bonus": 0.0, "id": len(ops), "boost": state["boost"], "ng": 0, "mile": False}
        o.update(kw)
        if any(isinstance(r, dict) and "win" in r for r in rd):
            o["ng"] = width(wr[0])
        ops.append(o)
        return o

    def follow(a, b):
        if a:
            b["queue"].append(a["id"])
        return b

    def vdur(n, c):
        return OPT["fix"] + max(n * c, 64) * CYC

    def tt(out, a, b, op):
        c = GC if "win" in a else (1 if psum(a) or psum(b) else 2)
        return add("v", lambda e: e.tensor_tensor(ap(T, out), ap(T, a), ap(T, b), op), [a, b], [out], vdur(width(out), c))

    def ts(out, a, s1, op0, s2=None, op1=None):
        c = GC if "win" in a else (0.5 if two(out, a) else 1)
        if op1 is None:
            fn = lambda e: e.tensor_scalar(ap(T, out), ap(T, a), val(s1), None, op0)
        else:
            fn = lambda e: e.tensor_scalar(ap(T, out), ap(T, a), val(s1), val(s2), op0, op1)
        return add("v", fn, [a, s1, s2], [out], vdur(width(out), c))

    def cp(out, a):
        c = GC if "win" in a else (0.5 if two(out, a) else 1)
        return add("v", lambda e: e.tensor_copy(ap(T, out), ap(T, a)), [a], [out], vdur(width(out), c))

    def tr(out, a):
        return add("v", lambda e: e.transpose(ap(T, out), ap(T, a)), [a], [out], vdur(width(out), 1))

    def fill(out, x):
        return add("v", lambda e: e.memset(ap(T, out), x), [], [out], vdur(width(out), 0.5 if two(out) else 1))

    def act(out, a, func, bias=0.0, scale=1.0):
        c = GC if "win" in a else 1
        return add("a", lambda e: e.activation(ap(T, out), ap(T, a), func, bias=val(bias), scale=val(scale)), [a, bias, scale], [out],
                   0.02 + vdur(width(out), c))

    def fetch(how, out, a):
        return cp(out, a) if how == "v" else act(out, a, ID)

    def mms(whole, terms, start, stop):
        def fn(e):
            for k, (out, l, r) in enumerate(terms):
                ins = e.matmul(ap(T, out), ap(T, l), ap(T, r), start and k == 0, stop and k == len(terms) - 1)
            return ins
        return add("t", fn, [x for t in terms for x in t[1:]], [whole], 0.03 + sum((1 if two(l) else 4) * max(64, width(r)) for o, l, r in terms) * PEC)

    def mm(out, terms, start=True, stop=True):
        return mms(out, [(out, l, r) for l, r in terms], start, stop)

    def total(c, terms, start=True, stop=True):
        for b in banks(c):
            mm(R("pb", *b), [(R(m), R(name, *b)) for m, name in terms], start, stop)

    def diag(mat, src, m0, m1):
        return [(R(mat, 15 - i, 143 - i), R(src, 16 * m0 + i, 16 * m1, 16)) for i in range(16)]

    def blocks(out, mat, src, c):
        return [(R(out, max(c[0] - NW * i, 0), NW), R(mat, 15 - i, 143 - i), R(src, max(NW * i, c[0]), NW * i + NW))
                for i in reversed(range(c[0] // NW, c[1] // NW))]

    def spare(m0, m1):
        state["ex"] ^= 1
        return R("ex%d" % state["ex"], m0, m1)

    def iota(out, pattern, base, mult):
        if SCRATCH[out["n"]][2] != I32:
            fn = lambda e: e.iota(ap(T, out), pattern, base, mult, allow_small_or_imprecise_dtypes=True)
        else:
            fn = lambda e: e.iota(ap(T, out), pattern, base, mult)
        return add("g", fn, [], [out], 0.15 + 2 * width(out) * CYC)

    def pick(out, a, step, op, other, mult):
        n = width(out)
        return add("g", lambda e: e.affine_select(ap(T, out), ap(T, a), [[step, n]], op, other, 0, mult), [a], [out], 0.2 + 2 * n * CYC)

    def mark_anchors(name, x):
        return pick(R(name, 0, A), R("ones"), 0, ALU.not_equal, x, 0)

    def dmas(q, pairs, nbytes, after=(), bonus=0.0, adding=False):
        k = state["dma"]
        state["dma"] += 1
        how = {"accum_op": ADD} if adding else {}
        return add(q, lambda e: [e.dma_start(val(o), val(i), **how) for o, i in pairs], [i for o, i in pairs], [o for o, i in pairs],
                   OPT["gdma"] if q == "g" else 0.07 * len(pairs) + 0.03, kind="d", lat=OPT["dl"] + nbytes / BW, xfer=nbytes / BW, bonus=bonus,
                   sem="dma%d" % k, after=list(after), n=len(pairs))

    def dma(q, out, in_, nbytes, after=(), bonus=0.0):
        return dmas(q, [(out, in_)], nbytes, after, bonus)

    def hbm(t, c, rows):
        return t[rows[0]:128:rows[1], c[0]:c[1]]

    def dup(how, out, a):
        if how == "s":
            return dma("s", out, a, 128 * width(a) * size(a))
        if how in "av":
            return fetch(how, out, a)
        return pick(out, a, 0, ALU.is_ge, 0.0, 0)

    me = T.cores[rank]

    def send(tos, out, in_, sem, tail, dur=0.8):
        dsts = [T.cores[to] for to in tos]
        mask = topo.mask(me, dsts[0])
        ids = [DstId(rid=topo.addr(d)[0], pnc=topo.addr(d)[1]) for d in dsts]
        fn = lambda e: e.remote_dma_fused([RemoteDMATransfer(dst_ids=ids, dma_engine_mask=mask, remote_sem=T.sem[sem], srcs=[ap(T, in_)],
                                                             dsts=[ap(T, out) for d in dsts])], local_sem=T.sem["sent"])
        return add("g", fn, [in_], [], dur, kind="s", tail=tail, tos=list(tos), semname=sem, n=len(topo.engines(me, dsts[0])))

    def arrive(frm, buf, sem, after, lat):
        return add("x", None, [], [buf], 0.0, kind="r", lat=lat, sem=sem, n=len(topo.engines(T.cores[frm], me)), after=list(after))

    def off(name, c, base=0):
        return R(name, base + c[0] // 16, base + c[1] // 16)

    def by_scalar(win, l, own, c, tmp, base, shift=0):
        o = act(R(tmp, c[0] - base, c[1] - base), G(R(win), off(l, c)), ID)
        for b in banks((c[0] - shift, c[1] - shift)):
            s = (b[0] + shift, b[1] + shift)
            mm(R("pb", *b), [(R(m), R(name, *s)) for m, name in own], True, False)
            mm(R("pb", *b), [(R("idf"), R(tmp, s[0] - base, s[1] - base))], False, True)
        return o

    def col(k):
        return R("cf", k, k + 1)

    odd, age, m32, m8, grp, oct_ = (col(k) for k in range(1, 7))
    isptr, notptr, ishost, is0, is2, lift, plain, spot, wl = (col(k) for k in range(9, 18))

    def rows_from(blk, win):
        tt(R("lo"), blk, R("hi"), SUB)
        return dmas("s", [(R(win, rows=(0, 16)), R("hi")), (R(win, rows=(8, 16)), R("lo"))], 98304)

    def hosts(wins):
        tt(R("ch"), R("ch"), R("ce"), MUL)
        ts(R("ch", 0, A), R("ch", 0, A), notptr, MUL, isptr, ADD)
        return dmas("s", [(R(name, rows=HOST), R("ch")) for name in wins], 98304 * len(wins))

    def wrap(blk, how):
        fetch(how[0], R("t1"), G(blk, R("f1")))
        tr(R("t2"), R("t1"))
        return fetch(how[1], R("l1"), G(R("t2"), R("f2")))

    def mark_round(name, r):
        return act(R(name, 0, A), R("cnt"), ID, scale=is0, bias=col(24 + r))

    def copy_own(how, name, c):
        if how == "s":
            return dmas("s", [(R("vd", *c, rows=w), R(name, *c, rows=w)) for w in REST + (HOST,)], 224 * (c[1] - c[0]))
        if how == "v":
            return ts(R("vd", *c), R(name, *c), notptr, MUL, isptr, ADD)
        return act(R("vd", *c), R(name, *c), ID, scale=notptr, bias=isptr)

    sends, gets = rank < NR - 1, rank > 0
    later = range(NR - 1, rank, -1)
    ALL = (0, V)
    sch = OPT["sch"]

    dmas("s", [(R("ce"), hbm(T.hf, ALL, PTR)), (R("ch"), hbm(T.hf, ALL, HOST))], 196608, bonus=320.0)
    dma("a", R("pari"), T.par[:], 98304, bonus=300.0)
    dmas("s", [(R("wx", A, V, rows=w), hbm(T.hf, (A, V), w)) for w in REST], 565000, bonus=80.0)

    state["boost"] = 100.0
    iota(R("ci", 0, 1), [[0, 1]], 0, 1)
    iota(R("iw", 24, 36), [[16, 12]], 0, 0)
    iota(R("cnt"), [[1, A]], 0, 0)
    iota(R("iw", 0, 24), [[16, 12], [0, 2]], 0, 0)
    for k, x in ((2, 15), (1, 16), (4, 7), (3, 31)):
        ts(R("ci", k, k + 1), R("ci", 0, 1), x, AND)
    for k, x in ((5, 4), (6, 3)):
        ts(R("ci", k, k + 1), R("ci", 0, 1), x, ALU.arith_shift_right)
    cp(R("cf", 1, 7), R("ci", 1, 7))
    ts(notptr, m8, 0.0, ALU.not_equal)
    ts(is2, age, 2.0, EQ)
    ts(is0, age, 0.0, EQ)
    ts(isptr, m8, 0.0, EQ)
    ts(R("f1"), R("iw", 0, 24), age, ADD)
    act(R("s1", 0, 12), R("iw", 24, 36), ID, bias=age)
    act(R("s2", 0, 12), R("s1", 0, 12), ID, bias=-5.5 / 12.0, scale=1.0 / 12.0)
    act(R("s1", 12, 24), R("s2", 0, 12), ID, bias=odd, scale=-383.0)
    act(col(24), is2, ID, bias=notptr)
    mark_round("wx", 0)
    ts(R("s1", 24, 36), R("s1", 0, 12), 32.0, MUL)
    tt(R("s1", 36, 48), R("s1", 12, 24), R("s1", 24, 36), ADD)
    cp(R("f2"), R("s1", 36, 48))
    ts(R("ce"), R("ce"), -0.5, MUL, 1.5, ADD)
    act(R("hi"), R("pari"), ID)
    rows = [hosts(["wx"]), rows_from(R("pari"), "wx")]
    gate = wrap(R("pari"), "vv")
    for j, c in enumerate(sch):
        copy_own(OPT["hdup"][j], "wx", c)

    state["boost"] = OPT["cboost"]
    rest = len(ops)
    fill(R("ones"), 1.0)
    for name, w in (("msel", isptr), ("msum", 1.0)):
        fill(R(name), 0.0)
        ts(R(name, 15, 143, 16), R("cnt", 0, 8), grp, EQ, w, MUL)
    act(plain, is2, ID, scale=-1.0, bias=notptr)
    for r, name in enumerate(("gs", "j2", "j4", "j8", "j16", "va")):
        if r:
            act(col(24 + r), is2, ID, scale=2.0 ** (2 ** r), bias=plain)
        mark_round(name, r)
    fill(R("one2"), 1.0)
    for name in ("idp", "idh", "idf"):
        pick(R(name), R("ones"), -1, EQ, 0.0, 1)
    ts(ishost, m8, 4.0, EQ)
    ts(lift, age, 8.0, EQ, 16.0, MUL)
    act(spot, m8, ID, scale=16.0, bias=oct_)
    act(wl, notptr, ID, scale=LT / KK)
    fill(R("nil"), 0.0)
    for name, w in (("idq", 512.0), ("idr", 1024.0), ("idn", -1.0), ("idt", 256.0), ("ids", -16.0)):
        pick(R(name), R("nil"), -1, ALU.not_equal, w, 1)
    act(R("idl"), R("idp"), ID, scale=wl)
    act(R("mneg"), R("msum"), ID, scale=-1.0)
    act(R("mtwo"), R("msum"), ID, scale=2.0)
    fill(R("mx"), 0.0)
    ts(R("mx", 7, 135, 8), R("cnt", 0, 16), oct_, EQ, ishost, MUL)
    fill(R("mr"), 0.0)
    ts(R("mr", 0, 1024, 8), R("cnt"), spot, EQ, LT / KK, MUL)
    act(R("hm", 0, A), R("ones"), ID, scale=2.0 * KK)
    state["boost"] = 0.0
    if sends:
        for e in range(EP):
            act(R("msg", MS * e + A + 8, MS * e + MS), R("ones", 0, 8), ID)
    dup("g", R("blk"), R("pari"))
    cp(R("l16", 0, 8), R("l1", 0, 8))
    for c in C3N:
        dmas("s", [(R("b0", *c), T.bt[:, c[0]:c[1]]), (R("h0", *c), T.hf[:, c[0]:c[1]])], 500000, bonus=20.0)
    dma("a", R("an", 0, A), T.hf[:, 0:A], 32768)
    dma("a", R("an", A, 2 * A), T.bt[:, 0:A], 32768)
    if gets:
        dma("a", R("upi"), T.up[:], 4096)
    for o in ops[rest + 1:]:
        if o["eng"] == "v" and o["wr"][0]["n"] != "nil":
            o["behind"] = [gate]
        if o["kind"] == "d":
            o["after"] = [gate]
            for p in rows if o["eng"] == "s" else []:
                follow(p, o)
    marks = [mark_anchors("zd", 8.0 * LT), mark_anchors("zc", 512.0)]

    lists = ["l1", "l2", "l4", "l8", "l16"]
    head = {"lag": OPT["head"]}
    if gets:
        send([rank - 1], R("upn"), R("upi"), "aup", head, OPT["first"])["after"] = marks
        send([rank - 1], R("ann"), R("an"), "aan", head)["after"] = marks
        arrive(0, R("a0"), "aa0", [], 22.0)
    else:
        send(later, R("a0"), R("an"), "aa0", head, OPT["first"])["after"] = marks
    if sends:
        arrive(rank + 1, R("upn"), "aup", [], 18.0)
        arrive(rank + 1, R("ann"), "aan", [], 19.0)
        dup("g", R("lh", 0, 8), R("upn"))
        tt(R("qq"), R("ann", 0, A), R("ann", A, 2 * A), MUL)
    a0 = "a0" if gets else "an"
    act(R("y0", A, 2 * A), R(a0, A, 2 * A), ID, bias=float(LL))
    tt(R("y0", 0, A), R("y0", A, 2 * A), R(a0, 0, A), MUL)

    own = OPT["zch"]
    edge = own[-1][1]
    for e in range(EP):
        first = e == 0
        win = "wx" if first else "gs"
        wins = [win, "j2", "j4", "j8", "j16", "va"]
        tail = {"lag": OPT["arrive"] + OPT["compose"] + (0.0 if gets else OPT["lead"])}
        for r in range(5):
            for j, c in enumerate(sch if r < 4 else OPT["slast"]):
                o = follow(o if j else None, tt(R(wins[r + 1], *c), G(R(wins[r]), off(lists[r], c)), R("vd", *c), MUL))
                if r < 4:
                    copy_own(OPT["vdup"][4 * e + r][j], wins[r + 1], c)
                if first and r == OPT["nload"] and j < 2:
                    n = (NW * j, NW * j + NW)
                    dma("s", R("nbi", *n), T.nb[:, n[0]:n[1]], 98304, after=[o])
                    dup("g", R("ln", *n), R("nbi", *n))
                if first and r == OPT["dload"]:
                    dma("s", R("d0", *c), T.dr[:, c[0]:c[1]], 190000, after=[o])
            for c in OPT["jch"] if r < 4 else []:
                x = spare(c[0] // 16, c[1] // 16)
                mm(x, diag("msel", wins[r + 1], x["c0"], x["c1"]))
                fetch(OPT["lcp"][4 * e + r], off(lists[r + 1], c), x)["boost"] = 5.0
            o["mile"] = True
            if r == 1:
                head.setdefault("op", o)
        if not first:
            mark_anchors("zc", 512.0)
        for j, c in enumerate(OPT["pch"]):
            terms, lifted = [("idq", "h0"), ("idp", "b0")], 0.0
            if not first:
                if OPT["xpr"][j] == "v":
                    tt(R("xp", *c), G(R("xd"), off("l1", c)), R("xi", *c), SUB)
                    terms = [("idq", "g0"), ("idn", "xp")]
                else:
                    act(R("xp", *c), G(R("xd"), off("l1", c)), ID)
                    terms = [("idq", "g0"), ("idp", "xd"), ("idn", "xp")]
                if OPT["qdr"][j] == "v":
                    tt(R("qd", *c), G(R("hs"), off("l1", c)), R("d0", *c), MUL)
                    terms += [("idp", "qd")]
                else:
                    act(R("qd", *c), G(R("hs"), off("l1", c)), ID)
                    total(c, [("idp", "d0"), ("idq", "qd")])
                    act(R("pp", *c), R("pb", *c), ABS)
                    terms, lifted = terms + [("idh", "pp")], 512.0
            total(c, terms)
            act(R("zc", *c), R("pb", *c), ABS, bias=-lifted)
            if not first:
                dup("g", R("pp", *c), R("zc", *c))
        for c in OPT["pch"]:
            act(R("pg", *c), G(R("zc"), off("l1", c)), ID)
            total(c, ([("idr", "h0"), ("idp", "b0")] if first else [("idr", "g0")]) + [("idh", "pg")])
            act(R("pg", *c), R("pb", *c), ABS, bias=-512.0)
            total(c, ([] if first else [("idh", "pp")]) + [("idh", "pg")], True, False)
        if sends:
            state["boost"] = OPT["hboost"]
            act(R("sj", 0, A), G(R("j8"), R("lh", 0, 8)), ID)
            act(R("sj", A, 2 * A), G(R("j16"), R("lh", 0, 8)), ID)["boost"] = 0.0
            x = R("ex0", 0, 16)
            mm(x, diag("msel", "sj", 0, 16))
            act(R("lh", 8, 24), x, ID)
            act(R("sk", 0, A), G(R("j8"), R("lh", 16, 24)), ID)
            act(R("sk", A, 2 * A), G(R("j16"), R("lh", 16, 24)), ID)
            mm(x, diag("msel", "sk", 0, 16))
            act(R("lh", 24, 32), R("ex0", 0, 8), ID)
            act(R("msg", MS * e + A, MS * e + A + 8), R("ex0", 8, 16), ID)
            act(R("sl"), G(R("j4"), R("lh", 0, 32)), ID)
            x = R("ex0", 0, 32)
            mm(x, diag("msel", "sl", 0, 32))
            act(R("lh", 32, 64), x, ID)
            state["boost"] = 0.0
        mark_anchors("za", float(LT))
        made = []
        for j, c in enumerate(OPT["slast"]):
            state["boost"] = OPT["kboost"]
            ts(R("hm", *c), R("va", *c), 0.0, ALU.is_gt, 2.0 * KK, MUL)
            x = R("ex1", c[0] // 8, c[1] // 8)
            w = [R(name, x["c0"], x["c1"]) for name in ("wi", "cw")]
            for b in banks(c):
                n = (b[1] - b[0]) // 8
                mm(R(x["n"], b[0] // 8, b[1] // 8), [(R("mx", 7 - i, 135 - i), R("va", b[0] + n * i, b[0] + n * i + n)) for i in range(8)])
            act(w[0], x, ABS, scale=0.5)
            ts(w[0], w[0], ODD, AND)
            act(w[1], w[0], RELU, bias=2.0 * KK, scale=-2.0 * KK)
            for b in banks(c):
                n = (b[1] - b[0]) // 8
                total(b, [("idl", "hm")], False, False)
                mms(R("pb", *b), [(R("pb", b[0] + n * i, b[0] + n * i + n), R("mr", A * i, A * i + A), R("cw", b[0] // 8, b[1] // 8))
                                  for i in range(8)], False, True)
            dmas("s", [(R("hm", *b, rows=PTR), R("cw", b[0] // 8, b[1] // 8)) for b in banks(c)], 32 * (c[1] - c[0]))
            state["boost"] = 0.0
            made.append(act(R("za", *c), R("pb", *c), ABS, bias=-(1024.0 if first else 1536.0) - LT))
            if c[0] < edge:
                dup(OPT["z0dup"][j], R("zd", c[0], min(c[1], edge)), R("za", c[0], min(c[1], edge)))
        dma("s", R(win, rows=(2, 16)), R("va", rows=(2, 16)), 49152)
        if sends:
            state["boost"] = OPT["hboost"]
            act(R("hu"), G(R("hm"), R("lh", 0, 8)), SIGN, bias=-KK)
            mh = R("hu")
            if first:
                mh = R("cu")
                tt(mh, R("hu"), R("ann", 0, A), MUL)
            state["boost"] = 0.0
        dma("s", R("dv"), R("va", rows=(2, 16)), 49152)
        act(R("dv"), R("dv"), ABS)
        for k in range(2):
            nk = "n%d" % k
            for c in OPT["ngather"]:
                o = act(R(nk, *c), G(R(win), off("ln", c, NW * k)), ABS, bias=lift)
                for p in made:
                    follow(p, o)
            for c in OPT["nch"]:
                x = R("ex1", c[0] // 16, c[1] // 16)
                mm(x, diag("msel", nk, x["c0"], x["c1"]))
                if OPT["lcr"] == "a":
                    act(off("lc%d" % k, c), x, ID, bias=-16.0)
                else:
                    ts(off("lc%d" % k, c), x, -16.0, ADD)
            q = [R("q%d" % k, NW * i, NW * i + NW) for i in range(3)]
            dmas("s", [(q[i], R(nk, rows=(w, 16))) for i, w in enumerate((0, 8, 2))], 147456)
            mm(R("ex%d" % k, 256, 256 + NW), [(R("idn"), R("hi")), (R("idn"), R("lo")), (R("ids"), R("one2")), (R("idp"), q[0]), (R("idp"), q[1])])
            x = R("ex0", 0, NW)
            mm(x, [(R("idp"), R("dv")), (R("idn"), q[2])])
            act(R("pen%d" % k), x, RELU, scale=PEN)
        if first:
            for c in C3N:
                act(R("g0", *c), R("d0", *c), SIGN, bias=127.5, scale=-1.0)
        zw = "za"
        mark = None
        for r in range(1, 4):
            zn = "zb" if r % 2 else "za"
            mark_anchors(zn, float(LT * 2 ** r))
            for c in OPT["share"]:
                by_scalar(zw, lists[r], [("idf", zw)], c, "zg", edge)
                act(R(zn, *c), R("pb", *c), ID)
            for j, c in enumerate(own):
                o = follow(o if j else None, tt(R(zn, *c), G(R(zw), off(lists[r], c)), R("zd", *c), ADD))
                dup(OPT["zdup"][r - 1][j], R("zd", *c), R(zn, *c))
            zw = zn
            o["mile"] = True
            if r == 1:
                mark = o
                if sends:
                    state["boost"] = OPT["mboost"]
                    x, mo, n = R("pb", 0, A), R("pb", A, 2 * A), OPT["zqv"]
                    mm(mo, [(R("idq"), mh), (R("idp"), R("qq")), (R("idq"), R("ones")), (R("idt"), R("ones"))])
                    act(R("zq", n, 1024), G(R(zw), R("lh", n // 16, 64)), ID, bias=-2.0 * LT)
                    ts(R("zq", 0, n), G(R(zw), R("lh", 0, n // 16)), -2.0 * LT, ADD)
                    for k in range(2):
                        mm(x, [(R("idh"), R("zq", A * i, A * i + A)) for i in range(4 * k, 4 * k + 4)], k == 0, k == 1)
                    tt(R("yi"), x, mh, MUL)
                    ts(R("yi"), R("yi"), 255, AND)
                    tt(R("msg", MS * e, MS * e + A), R("yi"), mo, ADD)
                    s = MS * (5 * e + rank)
                    mark = send(later, R("lsg", s, s + MS), R("msg", MS * e, MS * e + MS), "am%d_%d" % (e, rank), tail)
                    mark["mile"] = True
                    state["boost"] = 0.0
        if gets:
            for f in range(rank):
                s = MS * (5 * e + f)
                arrive(f, R("lsg", s, s + MS), "am%d_%d" % (e, f), [mark], OPT["arrive"] + (0.0 if sends else 2.8))
            shifts = [R("pb", 1536 + A * f, 1536 + A * f + A) for f in range(rank)]
            for f in range(rank):
                s = MS * (5 * e + f)
                act(R("ms", A * f, A * f + A), R("lsg", s, s + A), SIGN, bias=-895.5)
                dup("g", R("lp", 8 * f, 8 * f + 8), R("lsg", s + A, s + A + 8))
                mm(shifts[f], [(R("idh"), R("lsg", s, s + A))])
            yw = R("y0", A * e, A * e + A)
            for f in range(rank):
                u, y = R("uu", A * f, A * f + A), R("zz", A * f, A * f + A) if f < rank - 1 else R("za", 0, A)
                tt(u, G(yw, R("lp", 8 * f, 8 * f + 8)), R("ms", A * f, A * f + A), MUL)
                tt(y, u, shifts[f], ADD)
                yw = y
        else:
            act(R("za", 0, A), R("y0", A * e, A * e + A), ID)
        if first:
            for c, how in OPT["final"]:
                if how == "v":
                    dup(OPT["zer"], R("ze", *c), R("hm", *c))
                    c = (max(c[0], A), c[1])
                    dmas("g", [(R("ze", *c), R("zb", *c))], 1024 * (c[1] - c[0]), adding=True)
            mark_anchors("ze", 8.0 * LT + 2.0 * KK)
        for c, how in OPT["upper"]:
            if how == "v":
                o = tt(R("zc", *c), G(R("za"), off("l16", c)), R("zd", *c), ADD)
            else:
                o = by_scalar("za", "l16", [("idf", "zb")], c, "zd", 0)
                act(R("zc", *c), R("pb", *c), ID)
            tail.setdefault("op", o)
        o["mile"] = True
        for j, (c, how) in enumerate(OPT["final"]):
            if how == "v":
                x = R("za", *c)
                o = tt(x, G(R("zc"), off("l16", c)), R("ze" if first else "zd", *c), ADD)
            else:
                x = R("pb", c[0] - OPT["shift"], c[1] - OPT["shift"])
                by_scalar("zc", "l16", [("idf", "zb")] + ([("idp", "hm")] if first else []), c, "zd", 0, OPT["shift"])
            act(R("ui", *c), x, ABS, bias=-16.0 * LT - (KK if first else 0.0))["boost"] = OPT["uboost"]
            ts(R("xi", *c), R("ui", *c), 255, AND).update(boost=OPT["aboost"], mile=j == len(OPT["final"]) - 1)
            dup(OPT["xcv"][j], R("xd", *c), R("xi", *c))
        if first:
            for name in ("gs", "vd"):
                dmas("s", [(R(name, A, V, rows=w), R("g0", A, V, rows=w)) for w in REST], 565000, after=[o])
            dmas("s", [(R("ce"), hbm(T.dr, ALL, PTR)), (R("ch"), hbm(T.dr, ALL, HOST))], 196608, after=[tail["op"]])
            ts(R("ce"), R("ce"), 128.0, ALU.is_ge, 1.0, ADD)
            act(R("ch"), R("ch"), SIGN, bias=127.5, scale=-1.0)
            hosts(["gs", "vd"])
            for c in C3:
                act(R("hs", *c), R("ui", *c), SIGN, bias=-float(LL))
            if sends:
                tt(R("qq"), G(R("hs"), R("lh", 0, 8)), R("ann", A, 2 * A), MUL)
        else:
            for c in C3:
                dma("s", T.yx[:, c[0]:c[1]], R("xd", *c), 262144)
        sums = [[], [], []]
        for k, (name, l, pos) in enumerate((("da", "l1", "n0"), ("db", "lc0", "n1"), ("dc", "lc1", "j2"))):
            for c, how in OPT["votes"][k]:
                sums[k].append((c, [("msum", name)]))
                if how == "a":
                    act(R(name, *c), G(R("xi"), off(l, c)), ID)
                    total(c, [("idp", name), ("idn", "xd")])
                    act(R(name, *c), R("pb", *c), ABS)
                    continue
                tt(R(name, *c), G(R("xi"), off(l, c)), R("xd", *c), SUB)
                if how == "m":
                    act(R(name, *c), R(name, *c), ABS)
                else:
                    ts(R(pos, *c), R(name, *c), 0.0, ALU.max)
                    sums[k][-1] = (c, [("mneg", name), ("mtwo", pos)])
        for k, bank in enumerate(("pb", "ex0", "ex1")):
            for j, (c, parts) in enumerate(sums[k]):
                x = R(bank, 0, NW)
                pen = [(x, R("idp"), R("pen%d" % (k - 1)))] if k and j == 0 else []
                mms(x, pen + [t for m, src in parts for t in blocks(bank, m, src, c)], j == 0, j == len(sums[k]) - 1)
            if k == 0:
                act(R("dp"), R("pb", 0, NW), ID)
        s0, s1 = (R("ex%d" % k, 256, 256 + NW) for k in range(2))
        cc, w1 = (R("pb", 512 * k, 512 * k + NW) for k in (1, 2))
        d0, d1 = R("ex0", 0, NW), R("ex1", 0, NW)
        tt(R("w1c"), d0, R("dp"), ALU.is_lt)
        tt(R("cc"), s0, R("w1c"), MUL)
        tt(R("mn"), d0, R("dp"), ALU.min)
        tt(cc, R("blk"), R("cc"), ADD)
        tt(R("e1"), s1, R("cc"), SUB)
        tt(w1, d1, R("mn"), ALU.is_lt)
        tt(R("e0"), w1, R("e1"), MUL)
        tt(R("blk"), cc, R("e0"), ADD)["mile"] = True
        if first:
            state["boost"] = 10.0
            tt(R("hi"), cc, R("e0"), ADD)
            rows_from(R("blk"), "gs")
            wrap(R("blk"), OPT["wrap"])
            state["boost"] = 0.0
        else:
            dma("s", T.yp[:], R("blk"), 98304)
    ops[0]["seed"] = OPT["seed"][rank]
    return ops


def clash(a, b):
    if a["rows"] and b["rows"] and not set(range(a["rows"][0], 16, a["rows"][1])) & set(range(b["rows"][0], 16, b["rows"][1])):
        return False
    if psum(a):
        return a["c0"] // 512 <= (b["c1"] - 1) // 512 and b["c0"] // 512 <= (a["c1"] - 1) // 512
    return a["c0"] < b["c1"] and b["c0"] < a["c1"]


def deps(ops):
    seen = {}
    for o in ops:
        pre = set(p["id"] for p in o["after"])
        acc = [(r, False) for r in o["rd"]] + [(r, True) for r in o["wr"]]
        for r, w in acc:
            for r2, w2, o2 in seen.get(r["n"], []):
                if (w or w2 or (psum(r) and o2["eng"] != o["eng"])) and clash(r, r2):
                    pre.add(o2["id"])
        pre.discard(o["id"])
        o["all"] = pre
        o["pre"] = pre | set(q for p in o["behind"] for q in p["all"]) | set(o["queue"])
        for r, w in acc:
            seen.setdefault(r["n"], []).append((r, w, o))
    below = []
    for o in ops:
        far = 0
        for p in o["pre"]:
            far |= below[p]
        o["pre"] = set(p for p in o["pre"] if not far >> p & 1)
        for p in o["pre"]:
            far |= 1 << p
        below.append(far)


def lag_of(ops, p, o, hop):
    same = ops[p]["eng"] == o["eng"]
    if p not in o["all"]:
        return -9.0 if same else 0.0
    return 0.0 if same and o["eng"] == "t" else hop


def schedule(ops):
    deps(ops)
    n = len(ops)
    writes = [o for o in ops if o["kind"] == "s"]
    eng = [o["eng"] for o in ops]
    isd = [o["kind"] == "d" for o in ops]
    dur = [o["dur"] for o in ops]
    lat = [o["lat"] for o in ops]
    dl = OPT["dl"]
    forth = [[] for _ in ops]
    count = [len(o["pre"]) for o in ops]
    for k, o in enumerate(ops):
        for p in o["pre"]:
            forth[p].append((k, lag_of(ops, p, o, OPT["hop"])))
    for o in writes:
        forth[o["id"]].append((o["tail"]["op"]["id"], o["tail"]["lag"] - o["dur"]))
        count[o["tail"]["op"]["id"]] += 1
    rank = [0.0] * n
    for k in reversed(range(n)):
        rank[k] = max([0.0] + [lag + rank[m] for m, lag in forth[k]]) + dur[k] + lat[k] + ops[k]["bonus"]
    rank = [rank[k] + ops[k]["boost"] for k in range(n)]

    def dispatch(rank):
        left, can, who = list(count), [0.0] * n, [-1] * n
        ready = {q: [] for q in "vatgsx"}
        free, last = dict.fromkeys(ready, 0.0), dict.fromkeys(ready, -1)
        start, end, why, order, line = [0.0] * n, [0.0] * n, [-1] * n, [], 0.0
        for k in range(n):
            if not left[k]:
                ready[eng[k]].append(k)
        while len(order) < n:
            soon, q = min((min(max(can[k], free[q]) + OPT["look"] * dur[k] for k in r), q) for q, r in ready.items() if r)
            k = max((k for k in ready[q] if can[k] <= soon), key=lambda k: rank[k])
            ready[q].remove(k)
            order.append(k)
            if can[k] >= free[q] or q == "x":
                t, why[k] = can[k], who[k]
            else:
                t, why[k] = free[q], last[q]
            start[k], last[q] = t, k
            free[q] = t = t + dur[k]
            if isd[k]:
                line = max(t + 0.6 * dl, line) + ops[k]["xfer"]
                end[k] = t = line + 0.4 * dl
            else:
                end[k] = t = t + lat[k]
            for m, lag in forth[k]:
                if t + lag > can[m]:
                    can[m], who[m] = t + lag, k
                left[m] -= 1
                if not left[m]:
                    ready[eng[m]].append(m)
        k = max(range(n), key=lambda k: end[k])
        return end[k], start, why, k, order

    now = best = dispatch(rank)
    seed = ops[0]["seed"]
    for step in range(OPT["steps"]):
        held, k = [], now[3]
        while now[2][k] >= 0:
            p = now[2][k]
            if eng[p] == eng[k] and p not in ops[k]["pre"]:
                held.append((p, k))
            k = p
        new = list(rank)
        for trial in range(1 + step % 3):
            seed = (seed * 1103515245 + 12345) % 2147483648
            p, k = held[seed // 7 % len(held)]
            by = 0.2 + seed // 1031 % 100 * OPT["by"]
            if seed // 3 % 2:
                new[k] = max(new[k], new[p]) + by
                todo = [k]
                while todo:
                    m = todo.pop()
                    for x in ops[m]["pre"]:
                        if new[x] < new[m]:
                            new[x] = new[m] + 0.01
                            todo.append(x)
            else:
                new[p] = min(new[k], new[p]) - by
        r = dispatch(new)
        if r[0] < now[0] + OPT["warm"] * (1.0 - step / OPT["steps"]):
            now, rank = r, new
            if r[0] < best[0]:
                best = r
    place = {k: i for i, k in enumerate(best[4])}
    return polish(ops, writes, sorted(range(n), key=lambda k: (best[1][k], place[k])))


def polish(ops, writes, order):
    n = len(ops)
    eng = [o["eng"] for o in ops]
    isd = [o["kind"] == "d" for o in ops]
    sets = []
    for gc, hop, dl, bw, late in OPT["sets"]:
        dur = [o["dur"] + o["ng"] * (gc - OPT["gc"]) * OPT["cyc"] for o in ops]
        lat = [o["xfer"] * OPT["bw"] / bw if isd[k] else o["lat"] + (late if o["kind"] == "r" and o["pre"] else 0.0) for k, o in enumerate(ops)]
        pre = [[(p, lag_of(ops, p, o, hop)) for p in o["pre"]] for o in ops]
        for o in writes:
            pre[o["tail"]["op"]["id"]].append((o["id"], o["tail"]["lag"] + late - o["dur"]))
        post = [[] for _ in ops]
        for k in range(n):
            for p, lag in pre[k]:
                post[p].append((k, lag))
        sets.append((dur, lat, pre, post, dl))
    before = [[p for p, lag in x] for x in sets[0][2]]
    after = [[p for p, lag in x] for x in sets[0][3]]

    def heads(order, dur, lat, pre, post, dl):
        free, last = dict.fromkeys("vatgsx", 0.0), dict.fromkeys("vatgsx", -1)
        can, start, end, why, line, ahead, prev = [0.0] * n, [0.0] * n, [0.0] * n, [-1] * n, 0.0, {}, -1
        for k in order:
            q, t, w = eng[k], 0.0, -1
            for p, lag in pre[k]:
                if end[p] + lag > t:
                    t, w = end[p] + lag, p
            can[k] = t
            if free[q] > t and q != "x":
                t, w = free[q], last[q]
            start[k], why[k], last[q] = t, w, k
            free[q] = t = t + dur[k]
            if isd[k]:
                if line > t + 0.6 * dl:
                    ahead[k] = prev
                line, prev = max(t + 0.6 * dl, line) + lat[k], k
                end[k] = line + 0.4 * dl
            else:
                end[k] = t + lat[k]
        return max(end), can, start, end, why, ahead

    def tails(order, goal, dur, lat, pre, post, dl):
        far = -1e6 if goal >= 0 else 0.0
        nxt, need, rest, line = dict.fromkeys("vatgsx", far), [far] * n, [far] * n, far
        for k in reversed(order):
            t = 0.0 if k == goal else far
            for m, lag in post[k]:
                if lag + rest[m] > t:
                    t = lag + rest[m]
            if isd[k]:
                line = max(t, line) + lat[k]
                need[k] = t = line + dl
            else:
                need[k] = t = t + lat[k]
            if nxt[eng[k]] > t and eng[k] != "x":
                t = nxt[eng[k]]
            rest[k] = nxt[eng[k]] = t + dur[k]
        return need, rest

    def held_up(k, why, ahead):
        out, landed = [], True
        while True:
            p = ahead[k] if landed and k in ahead else why[k]
            if p < 0:
                return out
            landed = p in before[k] or p == ahead.get(k)
            if eng[p] == eng[k] and p not in before[k]:
                out.append((p, k))
            k = p

    def shifted(order, i, j, up):
        take = {order[j if up else i]}
        for x in (range(j - 1, i - 1, -1) if up else range(i + 1, j + 1)):
            if any(s in take for s in (after if up else before)[order[x]]):
                take.add(order[x])
        moved, stay = [x for x in order[i:j + 1] if x in take], [x for x in order[i:j + 1] if x not in take]
        return order[:i] + (moved + stay if up else stay + moved) + order[j + 1:]

    def by_start(order, start):
        place = {k: i for i, k in enumerate(order)}
        return sorted(order, key=lambda k: (start[k], place[k]))

    norm = [heads(order, *s)[0] for s in sets]
    best, kept = 1e9, order
    miles = [k for k, o in enumerate(ops) if o["mile"]]
    seed, tabu = ops[0]["seed"], {}
    for step in range(OPT["tries"]):
        hs = [heads(order, *s) for s in sets]
        total = sum((h[0] + OPT["pull"] * sum(h[3][m] for m in miles) / len(miles)) / w for h, w in zip(hs, norm))
        if total < best:
            best, kept = total, order
        use = step // OPT["turn"] % len(sets)
        span, can, start, end, why, ahead = hs[use]
        dur = sets[use][0]
        order = by_start(order, start)
        turn = step // (OPT["turn"] * len(sets)) % (len(miles) + OPT["ends"])
        goal = miles[turn] if turn < len(miles) else -1
        need, rest = tails(order, goal, *sets[use])
        lines = {q: [k for k in order if eng[k] == q] for q in "vatgs"}
        at = {k: i for q in lines for i, k in enumerate(lines[q])}
        held = held_up(goal if goal >= 0 else max(range(n), key=lambda k: end[k]), why, ahead)
        choice = None
        for trial in range(OPT["peek"] if held else 0):
            seed = (seed * 1103515245 + 12345) % 2147483648
            b = held[seed // 7 % len(held)][1]
            line, up, far = lines[eng[b]], seed // 3 % 2, seed // 4099 % OPT["far"]
            i, j = (max(at[b] - 1 - far, 0), at[b]) if up else (at[b] - 1, min(at[b] + far, len(line) - 1))
            u, v = line[i], line[j]
            if up and any(end[p] > start[u] + dur[u] for p in before[v]) or not up and any(start[m] < start[v] + dur[v] for m in after[u]):
                continue
            if up and any(x in before[v] for x in line[i:j]) or not up and any(x in after[u] for x in line[i + 1:j + 1]):
                continue
            seq = [v] + line[i:j] if up else line[i + 1:j + 1] + [u]
            t, begins = start[line[i - 1]] + dur[line[i - 1]] if i else 0.0, []
            for x in seq:
                t = max(t, can[x])
                begins.append(t)
                t += dur[x]
            t, guess = rest[line[j + 1]] if j + 1 < len(line) else -1e6, 0.0
            for x, t0 in zip(reversed(seq), reversed(begins)):
                t = dur[x] + max(t, need[x])
                guess = max(guess, t0 + t)
            pairs = [(v, x) for x in line[i:j]] if up else [(x, u) for x in line[i + 1:j + 1]]
            if any(tabu.get(p, -1) > step for p in pairs):
                continue
            if choice is None or guess < choice[0]:
                choice = (guess, up, u, v, pairs)
        if choice is None:
            continue
        guess, up, u, v, pairs = choice
        for x, y in pairs:
            tabu[y, x] = step + OPT["keep"] + seed % 7
        order = shifted(order, order.index(u), order.index(v), up)
    order, left = kept, OPT["last"]
    rs = [heads(order, *s) for s in sets]
    best = sum(h[0] / w for h, w in zip(rs, norm))
    while left > 0:
        left -= 1
        moves = set((p, k, up, far) for h in rs for p, k in held_up(max(range(n), key=lambda k: h[3][k]), h[4], h[5]) for up in (0, 1) for far in (0, 1, 3))
        seed = (seed * 1103515245 + 12345) % 2147483648
        moves = sorted(moves, key=lambda m: (m[0] * 7919 + m[1] * 31 + m[2] * 3 + m[3] + seed) * 2654435761 % 4294967296)
        for u, v, up, far in moves[:OPT["wide"]]:
            i, j = order.index(u), order.index(v)
            for step in range(far):
                if up:
                    i = ([x for x in range(i - 1, -1, -1) if eng[order[x]] == eng[u]] + [i])[0]
                else:
                    j = ([x for x in range(j + 1, n) if eng[order[x]] == eng[u]] + [j])[0]
            new = shifted(order, i, j, up)
            left -= 1
            hs = [heads(new, *s) for s in sets]
            total = sum(h[0] / w for h, w in zip(hs, norm))
            if total < best - 1e-6:
                best, rs, order = total, hs, by_start(new, hs[0][2])
                break
    for i, k in enumerate(order):
        ops[k]["est"] = i
    return [ops[k] for k in order]


def rank_program(g, core, T, topo):
    rank = T.rank_of(core)
    if rank is None:
        return
    ops = build(rank, T, topo)
    order = schedule(ops)
    queue = {"v": g.vector, "a": g.scalar, "t": g.tensor, "g": g, "s": g.sync}
    count = {"v": 0, "a": 0, "t": 0, "g": 0}
    total = {}
    for o in order:
        if o["kind"] == "c":
            count[o["eng"]] += 1
            o["sig"] = ("q" + o["eng"], count[o["eng"]])
        elif o["kind"] == "d":
            o["sig"] = (o["sem"], 16 * o["n"])
        elif o["kind"] == "r":
            o["sig"] = (o["sem"], o["n"])
        else:
            total["sent"] = total.get("sent", 0) + o["n"]
            continue
        total[o["sig"][0]] = o["sig"][1]
    waited = {}
    known = {q: {} for q in "vatgs"}
    for o in order:
        if o["kind"] == "r":
            o["knows"] = {}
            continue
        q, mine = queue[o["eng"]], known[o["eng"]]
        for p in sorted((ops[p] for p in o["all"]), key=lambda p: -p["est"]):
            if p["eng"] == "t" and o["eng"] == "t":
                continue
            s, n = p["sig"]
            if mine.get(s, 0) < n:
                q.wait_ge(T.sem[s], n)
                waited[(o["eng"], s)] = mine[s] = n
                for s, n in p["knows"].items():
                    mine[s] = max(mine.get(s, 0), n)
        o["knows"] = dict(mine)
        ins = o["fn"](q)
        if o["kind"] == "c":
            ins.then_inc(T.sem[o["sig"][0]], 1)
        elif o["kind"] == "d":
            for i in ins:
                i.then_inc(T.sem[o["sem"]], 16)
    for s in sorted(total):
        if not any(waited.get((q, s), 0) >= total[s] for q in "vatgs"):
            g.wait_ge(T.sem[s], total[s])
